import numpy as np
import ml_dtypes


def mxq(x, axis, fmt="e4m3"):
    dtype, down = {"e4m3": (ml_dtypes.float8_e4m3fn, 7), "e5m2": (ml_dtypes.float8_e5m2, 14)}[fmt]
    v = np.moveaxis(np.asarray(x, np.float32).astype(ml_dtypes.bfloat16).astype(np.float64), axis, -1)
    blocks = v.reshape(v.shape[:-1] + (-1, 32))
    amax = np.abs(blocks).max(-1, keepdims=True)
    byte = np.maximum(np.where(amax > 0, np.frexp(amax)[1] - 1 + 127, 0) - down, 1)
    scale = np.exp2(byte - 127.0)
    codes = (blocks / scale).astype(np.float32).astype(dtype).astype(np.float64)
    return np.moveaxis((codes * scale).reshape(v.shape), -1, axis)


WIDE = False


def mx_kscale(k):
    if not WIDE:
        return np.ones(k)
    levels = np.array([10, -10, 5, -5, 0])
    if k % 512:
        return np.exp2(np.random.permutation(np.resize(levels, k // 32))).repeat(32)
    a = np.empty((k // 512, 16))
    for p in range(k // 512):
        a[p, :8] = np.random.permutation(np.resize(levels, 8))
        for g in range(8):
            far = levels[np.abs(levels - a[p, g]) >= 10]
            a[p, g + 8] = far[np.random.randint(len(far))]
    return np.exp2(a.ravel()).repeat(32)


def f64(x):
    return np.asarray(x).astype(np.float64)


def striped(idx):
    return np.tile(idx.reshape(-1, 16).T, (8, 1)).astype(np.uint16)


def unstriped(offs):
    return offs[:16].T.reshape(-1).astype(np.int64)


E2M1 = np.array([0.0, 0.5, 1.0, 1.5, 2.0, 3.0, 4.0, 6.0, -0.0, -0.5, -1.0, -1.5, -2.0, -3.0, -4.0, -6.0])


def pack_weight(w, fmt):
    k, n = w.shape
    w = f64(np.asarray(w, np.float32).astype(ml_dtypes.bfloat16)).reshape(k // 32, 32, n)
    amax = np.abs(w).max(1)
    if fmt == "e4m3":
        byte = np.frexp(amax)[1] - 1 + 127 - 7
    else:
        mant, ex = np.frexp(amax / 6.0)
        byte = np.where(mant > 0.5, ex, ex - 1) + 127
    byte = np.clip(np.where(amax > 0, byte, 1), 1, 254)
    scaled = (w * np.exp2(127.0 - byte)[:, None, :]).reshape(k, n).astype(np.float32)
    by_word = np.ascontiguousarray(scaled.reshape(k // 512, 128, 4, n).transpose(0, 1, 3, 2))
    if fmt == "e4m3":
        words = by_word.astype(ml_dtypes.float8_e4m3fn).view(np.uint8)
    else:
        c = by_word.astype(ml_dtypes.float4_e2m1fn).view(np.uint8) & 0xF
        words = (c[..., 0::2] | (c[..., 1::2] << 4)).reshape(k // 512, 128, 2 * n)
    return np.ascontiguousarray(words), np.ascontiguousarray(byte.astype(np.uint8).reshape(k // 512, 16, n))


def unpack_weight(words, scales, fmt):
    g, _, n = scales.shape
    words = np.ascontiguousarray(words).reshape(g, 128, n, -1)
    if fmt == "e4m3":
        vals = words.view(ml_dtypes.float8_e4m3fn).astype(np.float64)
    else:
        nib = np.empty((g, 128, n, 4), np.uint8)
        nib[..., 0::2] = words & 0xF
        nib[..., 1::2] = words >> 4
        vals = E2M1[nib]
    vals = vals * np.repeat(np.exp2(scales.astype(np.float64) - 127.0), 8, axis=1)[..., None]
    return vals.transpose(0, 1, 3, 2).reshape(g * 512, n)


def d_relu(v):
    return (v > 0).astype(np.float64)


K, T, E, C, H, N = 256, 1024, 8, 256, 512, 512


def by_expert(wq, xq):
    return np.concatenate([wq[e].T @ xq[:, e * C:(e + 1) * C] for e in range(E)], axis=1)


def setup_inputs():
    n = np.random.standard_normal
    s = mx_kscale(N)[:, None]
    u = mx_kscale(H)
    first = np.random.permutation(np.repeat(np.arange(E), T // E))
    second = (first + 1 + np.random.permutation(np.repeat(np.arange(E - 1), -(-T // (E - 1)))[:T])) % E
    while np.bincount(second, minlength=E).max() != T // E:
        load = np.bincount(second, minlength=E); hi, lo = int(load.argmax()), int(load.argmin())
        t = np.flatnonzero((second == hi) & (first != lo))[0]; second[t] = lo
    slot_token = np.empty(E * C, np.int64); pos = np.empty((2, T), np.int64); fill = np.zeros(E, np.int64)
    place = np.stack([np.random.permutation(C) for _ in range(E)])
    for r, deal in enumerate((first, second)):
        for t in np.random.permutation(T):
            e = deal[t]; j = e * C + place[e, fill[e]]; fill[e] += 1; slot_token[j] = t; pos[r, t] = j
    g = np.random.uniform(0.2, 0.8, T)
    w_slot = np.empty(E * C); w_slot[pos[0]] = g; w_slot[pos[1]] = 1.0 - g
    w2 = [pack_weight(m, "e2m1") for m in n((E, N, H)) / np.sqrt(N) / s[None] * u[None, None, :]]
    w1 = [pack_weight(m, "e2m1") for m in n((E, H, K)) / np.sqrt(H) / u[None, :, None]]
    return {
        "dyT": (n((N, T)) * s).astype(np.float32),
        "a": n((H, E * C)).astype(np.float32),
        "w2_words": np.stack([m[0] for m in w2]),
        "w2_scales": np.stack([m[1] for m in w2]),
        "w1_words": np.stack([m[0] for m in w1]),
        "w1_scales": np.stack([m[1] for m in w1]),
        "gate": np.tile(w_slot, (N, 1)).astype(np.float32),
        "offs": striped(slot_token),
        "pos1": striped(pos[0]),
        "pos2": striped(pos[1]),
    }


def reference(dyT, a, w2_words, w2_scales, w1_words, w1_scales, gate, offs, pos1, pos2):
    idx = unstriped(offs)
    w2 = np.stack([unpack_weight(w2_words[e], w2_scales[e], "e2m1") for e in range(E)])
    w1 = np.stack([unpack_weight(w1_words[e], w1_scales[e], "e2m1") for e in range(E)])
    gq = mxq(f64(gate) * f64(dyT)[:, idx], 0, "e4m3")
    dh = by_expert(w2, gq)
    da = dh * d_relu(f64(a))
    dx = by_expert(w1, mxq(da, 0, "e4m3"))
    return dx[:, unstriped(pos1)] + dx[:, unstriped(pos2)]

@@ -1,0 +1,300 @@
+from contextlib import ExitStack
+
+import concourse.mybir as mybir
+
+K, T, E, C, H, N = 256, 1024, 8, 256, 512, 512
+S = E * C
+P = 128
+PACK = 4
+
+F32 = mybir.dt.float32
+BF16 = mybir.dt.bfloat16
+I32 = mybir.dt.int32
+U32 = mybir.dt.uint32
+U16 = mybir.dt.uint16
+U8 = mybir.dt.uint8
+FP8X4 = mybir.dt.float8_e4m3fn_x4
+FP4X4 = mybir.dt.float4_e2m1fn_x4
+MULT = mybir.AluOpType.mult
+ADD = mybir.AluOpType.add
+MAX = mybir.AluOpType.max
+SIGN = mybir.ActivationFunctionType.Sign
+RELU = mybir.ActivationFunctionType.Relu
+
+FLOPS = 2 * S * (N * H + H * K)
+BYTES = 4 * N * T + 4 * H * S + E * (N * H + H * K) * 17 // 32 + 4 * S + 2 * S + 2 * 2 * T + 4 * K * T
+
+PIECE = 512
+PIECES = S // PIECE
+CHUNK = 128
+SHARES = (((0, 1024, "gpsimd"),), ((0, 512, "gpsimd"), (512, 256, "vector"), (768, 256, "vector")))
+
+
+def tile_moe_bdx_mlp_relu_kernel(
+    tc, dyT, a, w2_words, w2_scales, w1_words, w1_scales, gate, offs, pos1, pos2, out
+):
+    nc = tc.nc
+    with ExitStack() as ctx:
+        lists = ctx.enter_context(tc.tile_pool(name="lists", bufs=1))
+        keep = ctx.enter_context(tc.tile_pool(name="keep", bufs=1))
+        work = ctx.enter_context(tc.tile_pool(name="work", bufs=3))
+        psum1 = ctx.enter_context(tc.psum_pool(name="psum1", bufs=4))
+        psum2 = ctx.enter_context(tc.psum_pool(name="psum2", bufs=2))
+
+        offs_t = lists.tile([P, S // 16], U16, name="offs_t")
+        pos1_t = lists.tile([P, T // 16], U16, name="pos1_t")
+        pos2_t = lists.tile([P, T // 16], U16, name="pos2_t")
+
+        dy = [keep.tile([P, T], F32, name=f"dy{t}") for t in range(PACK)]
+        gates = [keep.tile([P, PIECE], F32, name=f"gates{q}") for q in range(PIECES)]
+        pre = [keep.tile([P, PACK, PIECE], F32, name=f"pre{q}") for q in range(PIECES)]
+        w2_raw = [keep.tile([P, 2, 2 * H], U8, name=f"w2_raw{q}") for q in range(PIECES)]
+        w2_t = [keep.tile([P, 2, 2 * H], U8, name=f"w2_t{q}", align_bytes=64) for q in range(PIECES)]
+        s2_raw = keep.tile([P, E // 2, H], U8, name="s2_raw")
+        s2_mid = keep.tile([P, E // 2, H], U8, name="s2_mid")
+        s2_t = keep.tile([P, E, H], U8, name="s2_t", align_bytes=64)
+        w1_t = keep.tile([P, E, 2 * K], U8, name="w1_t", align_bytes=64)
+        s1_t = keep.tile([P, E, K], U8, name="s1_t", align_bytes=64)
+        dx = [keep.tile([P, S], F32, name=f"dx{k}") for k in range(2)]
+
+        for rows in (slice(32, 64), slice(64, P)):
+            nc.gpsimd.memset(s2_raw[rows].rearrange("p e i -> p (e i)").bitcast(I32), 0)
+        nc.gpsimd.memset(s2_t[:].rearrange("p e i -> p (e i)").bitcast(I32), 0)
+        nc.gpsimd.memset(s1_t[:].rearrange("p e i -> p (e i)").bitcast(I32), 0)
+
+        dyT_rows = dyT.rearrange("(p t) n -> p t n", t=PACK)
+        a_rows = a.rearrange("(p t) s -> p t s", t=PACK)
+
+        def load_gate(q):
+            nc.sync.dma_start(gates[q][:], gate[0:P, q * PIECE : (q + 1) * PIECE])
+
+        def load_pre(q):
+            nc.sync.dma_start(pre[q][:], a_rows[:, :, q * PIECE : (q + 1) * PIECE])
+
+        def load_w2(q):
+            nc.sync.dma_start(
+                w2_raw[q][:].rearrange("p e b -> p (e b)").bitcast(I32).rearrange("p (e b) -> p e b", e=2),
+                w2_words[2 * q : 2 * q + 2].rearrange("e g p b -> p (e g) b").bitcast(I32),
+            )
+
+        def as_i32(view):
+            e = view.shape[1]
+            return view.rearrange("p e i -> p (e i)").bitcast(I32).rearrange("p (e i) -> p e i", e=e)
+
+        def move_scales(j):
+            for quad in range(4):
+                nc.sync.dma_start(
+                    as_i32(s2_t[32 * quad : 32 * quad + 4, 4 * j : 4 * j + 4, :]),
+                    as_i32(s2_mid[16 * j + 4 * quad : 16 * j + 4 * quad + 4]),
+                )
+
+        for j in range(2):
+            nc.sync.dma_start(
+                as_i32(s2_raw[16 * j : 16 * j + 16]),
+                w2_scales[4 * j : 4 * j + 4].rearrange("e g f i -> (g f) e i").bitcast(I32),
+            )
+        load_w2(0)
+        nc.vector.tensor_copy(
+            s2_mid[:].rearrange("p e (t m) -> p e t m", t=PACK), s2_raw[:].rearrange("p e (m t) -> p e t m", t=PACK)
+        )
+        nc.sync.dma_start(offs_t[:], offs)
+        load_gate(0)
+        for t in range(PACK):
+            nc.sync.dma_start(dy[t][:], dyT_rows[:, t, :])
+        load_gate(1)
+        load_pre(0)
+        move_scales(0)
+        load_gate(2)
+        load_pre(1)
+        load_w2(1)
+        nc.sync.dma_start(as_i32(w1_t[:]), w1_words.rearrange("e g p b -> p (e g) b").bitcast(I32))
+        for quad in range(4):
+            nc.sync.dma_start(
+                as_i32(s1_t[32 * quad : 32 * quad + 4]),
+                w1_scales[:, :, 4 * quad : 4 * quad + 4, :].rearrange("e g f k -> f (e g) k").bitcast(I32),
+            )
+        load_gate(3)
+        load_pre(2)
+        load_w2(2)
+        move_scales(1)
+        load_w2(3)
+        load_pre(3)
+        nc.sync.dma_start(pos1_t[:], pos1)
+        nc.sync.dma_start(pos2_t[:], pos2)
+
+        g4, grouped, signs, ones, codes, raws, das = {}, {}, {}, {}, {}, {}, {}
+
+        def gather(q, t):
+            if t == 0:
+                g4[q] = work.tile([P, PACK, PIECE], F32, name="g4")
+            nc.vector.tensor_tensor(
+                g4[q][:, t, :],
+                dy[t][:].indirect(offs_t[:, q * (PIECE // 16) : (q + 1) * (PIECE // 16)]),
+                gates[q][:],
+                MULT,
+            )
+
+        def permute_words(q):
+            nc.vector.tensor_copy(
+                w2_t[q][:].rearrange("p e b -> p (e b)").bitcast(U16).rearrange("p (e t m) -> p e t m", e=2, t=PACK),
+                w2_raw[q][:].rearrange("p e b -> p (e b)").bitcast(U16).rearrange("p (e m t) -> p e t m", e=2, t=PACK),
+            )
+
+        def interleave(q):
+            grouped[q] = work.tile([P, PIECE, PACK], BF16, name="gb", align_bytes=64)
+            step = C if q == PIECES - 1 else PIECE
+            for first in range(0, PIECE, step):
+                cols = slice(first, first + step)
+                nc.scalar.copy(
+                    grouped[q][:, cols, :].rearrange("p (c i) t -> p c t i", i=4),
+                    g4[q][:, :, cols].rearrange("p t (c i) -> p c t i", i=4),
+                )
+
+        def sign(q):
+            signs[q] = work.tile([P, PIECE, PACK], BF16, name="sg")
+            nc.scalar.activation(
+                signs[q][:].rearrange("p (c i) t -> p c t i", i=4),
+                pre[q][:].rearrange("p t (c i) -> p c t i", i=4),
+                SIGN,
+            )
+
+        def mask(q):
+            ones[q] = work.tile([P, PIECE, PACK], BF16, name="mk")
+            if q == 0:
+                nc.scalar.activation(ones[q][:], signs[q][:], RELU)
+            else:
+                nc.vector.tensor_scalar(ones[q][:], signs[q][:], 0.0, None, MAX)
+
+        def quantise_g(q, first, width):
+            if first == 0:
+                codes[q] = (
+                    work.tile([P, PIECE], U32, name="g_words", align_bytes=64),
+                    work.tile([P, PIECE], U8, name="g_scales", align_bytes=64),
+                )
+                das[q] = work.tile([P, PIECE, PACK], BF16, name="da", align_bytes=64)
+            cols = slice(first, first + width)
+            nc.vector.quantize_mx(
+                out=codes[q][0][:, cols].bitcast(FP8X4),
+                scales=codes[q][1][:, cols],
+                in_=grouped[q][:, cols, :].rearrange("p s t -> p (s t)"),
+            )
+
+        def first_product(q, c):
+            h = c * CHUNK // C
+            cols = slice(c * CHUNK, (c + 1) * CHUNK)
+            bank = psum1.tile([P, PACK, CHUNK], F32, name="bank")
+            for t in range(PACK):
+                nc.tensor.matmul_mx(
+                    out=bank[:, t, :],
+                    lhsT=w2_t[q][:, h, t * 2 * P : (t + 1) * 2 * P].bitcast(FP4X4),
+                    lhsT_scale=s2_t[:, 2 * q + h, t * P : (t + 1) * P],
+                    rhs=codes[q][0][:, cols].bitcast(FP8X4),
+                    rhs_scale=codes[q][1][:, cols],
+                    start=True,
+                    stop=True,
+                )
+            return cols, bank[:].rearrange("p t s -> p s t")
+
+        def product_by_mask(q, c):
+            if c == 0:
+                raws[q] = work.tile([P, PIECE, PACK], BF16, name="raw")
+            cols, bank = first_product(q, c)
+            nc.scalar.copy(raws[q][:, cols, :], bank)
+            if c == PIECE // CHUNK - 1:
+                nc.vector.tensor_tensor(das[q][:], raws[q][:], ones[q][:], MULT)
+
+        def product_by_sign(q, c):
+            cols, bank = first_product(q, c)
+            nc.vector.scalar_tensor_tensor(das[q][:, cols, :], signs[q][:, cols, :], 0.0, bank, MAX, MULT)
+
+        def second_product(q, first, width):
+            words = work.tile([P, PIECE], U32, name="da_words", align_bytes=64)
+            scales = work.tile([P, PIECE], U8, name="da_scales", align_bytes=64)
+            nc.vector.quantize_mx(
+                out=words[:, 0:width].bitcast(FP8X4),
+                scales=scales[:, 0:width],
+                in_=das[q][:, first : first + width, :].rearrange("p s t -> p (s t)"),
+            )
+            for k in range(2):
+                acc = psum2.tile([P, PIECE], F32, name=f"acc{k}")
+                for start in range(0, width, min(width, C)):
+                    span = slice(start, start + min(width, C))
+                    h = (first + start) // C
+                    nc.tensor.matmul_mx(
+                        out=acc[:, span],
+                        lhsT=w1_t[:, 2 * q + h, k * 2 * P : (k + 1) * 2 * P].bitcast(FP4X4),
+                        lhsT_scale=s1_t[:, 2 * q + h, k * P : (k + 1) * P],
+                        rhs=words[:, span].bitcast(FP8X4),
+                        rhs_scale=scales[:, span],
+                        start=True,
+                        stop=True,
+                    )
+                slots = slice(q * PIECE + first, q * PIECE + first + width)
+                if k == 0 and first + width == PIECE and q == PIECES - 1:
+                    nc.vector.tensor_copy(dx[k][:, slots], acc[:, 0:width])
+                else:
+                    nc.scalar.copy(dx[k][:, slots], acc[:, 0:width])
+
+        permute_words(0)
+        for q in range(2):
+            for t in range(PACK):
+                gather(q, t)
+            interleave(q)
+            if q == 0:
+                sign(0)
+        quantise_g(0, 0, PIECE)
+        mask(0)
+        gather(2, 0)
+        gather(2, 1)
+        product_by_mask(0, 0)
+        product_by_mask(0, 1)
+        gather(2, 2)
+        product_by_mask(0, 2)
+        product_by_mask(0, 3)
+        quantise_g(1, 0, PIECE)
+        sign(1)
+        gather(2, 3)
+        interleave(2)
+        permute_words(1)
+        second_product(0, 0, PIECE)
+        mask(1)
+        gather(3, 0)
+        product_by_mask(1, 0)
+        product_by_mask(1, 1)
+        gather(3, 1)
+        permute_words(2)
+        product_by_mask(1, 2)
+        product_by_mask(1, 3)
+        gather(3, 2)
+        sign(2)
+        quantise_g(2, 0, PIECE)
+        gather(3, 3)
+        interleave(3)
+        second_product(1, 0, PIECE)
+        sign(3)
+        product_by_sign(2, 0)
+        product_by_sign(2, 1)
+        quantise_g(3, 0, C)
+        product_by_sign(2, 2)
+        product_by_sign(2, 3)
+        quantise_g(3, C, C)
+        permute_words(3)
+        product_by_sign(3, 0)
+        second_product(2, 0, PIECE)
+        product_by_sign(3, 1)
+        product_by_sign(3, 2)
+        second_product(3, 0, C)
+        product_by_sign(3, 3)
+        second_product(3, C, CHUNK)
+        second_product(3, C + CHUNK, CHUNK)
+
+        for k in range(2):
+            part1 = keep.tile([P, T], F32, name=f"part1_{k}")
+            nc.vector.tensor_copy(part1[:], dx[k][:].indirect(pos1_t[:]))
+            for first, width, adder in SHARES[k]:
+                part2 = keep.tile([P, width], F32, name=f"part2_{k}_{first}")
+                total = keep.tile([P, width], F32, name=f"total_{k}_{first}")
+                nc.vector.tensor_copy(part2[:], dx[k][:].indirect(pos2_t[:, first // 16 : (first + width) // 16]))
+                engine = nc.vector if adder == "vector" else nc.gpsimd
+                engine.tensor_tensor(total[:], part1[:, first : first + width], part2[:], ADD)
+                nc.sync.dma_start(out[k * P : (k + 1) * P, first : first + width], total[:])

@@ -1,6 +1,7 @@
 from contextlib import ExitStack
 
 import concourse.mybir as mybir
+from concourse.masks import make_identity
 
 K, T, E, C, H, N = 256, 1024, 8, 256, 512, 512
 S = E * C
@@ -18,6 +19,7 @@ FP4X4 = mybir.dt.float4_e2m1fn_x4
 MULT = mybir.AluOpType.mult
 ADD = mybir.AluOpType.add
 MAX = mybir.AluOpType.max
+IS_GT = mybir.AluOpType.is_gt
 SIGN = mybir.ActivationFunctionType.Sign
 RELU = mybir.ActivationFunctionType.Relu
 
@@ -27,7 +29,6 @@ BYTES = 4 * N * T + 4 * H * S + E * (N * H + H * K) * 17 // 32 + 4 * S + 2 * S +
 PIECE = 512
 PIECES = S // PIECE
 CHUNK = 128
-SHARES = (((0, 1024, "gpsimd"),), ((0, 512, "gpsimd"), (512, 256, "vector"), (768, 256, "vector")))
 
 
 def tile_moe_bdx_mlp_relu_kernel(
@@ -37,9 +38,8 @@ def tile_moe_bdx_mlp_relu_kernel(
     with ExitStack() as ctx:
         lists = ctx.enter_context(tc.tile_pool(name="lists", bufs=1))
         keep = ctx.enter_context(tc.tile_pool(name="keep", bufs=1))
-        work = ctx.enter_context(tc.tile_pool(name="work", bufs=3))
-        psum1 = ctx.enter_context(tc.psum_pool(name="psum1", bufs=4))
-        psum2 = ctx.enter_context(tc.psum_pool(name="psum2", bufs=2))
+        work = ctx.enter_context(tc.tile_pool(name="work", bufs=4))
+        psum = ctx.enter_context(tc.psum_pool(name="psum", bufs=1))
 
         offs_t = lists.tile([P, S // 16], U16, name="offs_t")
         pos1_t = lists.tile([P, T // 16], U16, name="pos1_t")
@@ -47,254 +47,244 @@ def tile_moe_bdx_mlp_relu_kernel(
 
         dy = [keep.tile([P, T], F32, name=f"dy{t}") for t in range(PACK)]
         gates = [keep.tile([P, PIECE], F32, name=f"gates{q}") for q in range(PIECES)]
-        pre = [keep.tile([P, PACK, PIECE], F32, name=f"pre{q}") for q in range(PIECES)]
-        w2_raw = [keep.tile([P, 2, 2 * H], U8, name=f"w2_raw{q}") for q in range(PIECES)]
+        pre = [keep.tile([P, PACK, C], F32, name=f"pre{e}", align_bytes=64) for e in range(E)]
         w2_t = [keep.tile([P, 2, 2 * H], U8, name=f"w2_t{q}", align_bytes=64) for q in range(PIECES)]
-        s2_raw = keep.tile([P, E // 2, H], U8, name="s2_raw")
-        s2_mid = keep.tile([P, E // 2, H], U8, name="s2_mid")
         s2_t = keep.tile([P, E, H], U8, name="s2_t", align_bytes=64)
         w1_t = keep.tile([P, E, 2 * K], U8, name="w1_t", align_bytes=64)
         s1_t = keep.tile([P, E, K], U8, name="s1_t", align_bytes=64)
-        dx = [keep.tile([P, S], F32, name=f"dx{k}") for k in range(2)]
+        dx = [keep.tile([P, S], F32, name="dx0")]
+        da_words = [keep.tile([P, PIECE], U32, name=f"da_words{q}", align_bytes=64) for q in range(PIECES)]
+        da_scales = [keep.tile([P, PIECE], U8, name=f"da_scales{q}", align_bytes=64) for q in range(PIECES)]
+        ident = keep.tile([P, P], F32, name="ident")
 
-        for rows in (slice(32, 64), slice(64, P)):
-            nc.gpsimd.memset(s2_raw[rows].rearrange("p e i -> p (e i)").bitcast(I32), 0)
         nc.gpsimd.memset(s2_t[:].rearrange("p e i -> p (e i)").bitcast(I32), 0)
         nc.gpsimd.memset(s1_t[:].rearrange("p e i -> p (e i)").bitcast(I32), 0)
+        make_identity(nc, ident[:])
 
         dyT_rows = dyT.rearrange("(p t) n -> p t n", t=PACK)
         a_rows = a.rearrange("(p t) s -> p t s", t=PACK)
-
-        def load_gate(q):
-            nc.sync.dma_start(gates[q][:], gate[0:P, q * PIECE : (q + 1) * PIECE])
-
-        def load_pre(q):
-            nc.sync.dma_start(pre[q][:], a_rows[:, :, q * PIECE : (q + 1) * PIECE])
-
-        def load_w2(q):
-            nc.sync.dma_start(
-                w2_raw[q][:].rearrange("p e b -> p (e b)").bitcast(I32).rearrange("p (e b) -> p e b", e=2),
-                w2_words[2 * q : 2 * q + 2].rearrange("e g p b -> p (e g) b").bitcast(I32),
-            )
 
         def as_i32(view):
             e = view.shape[1]
             return view.rearrange("p e i -> p (e i)").bitcast(I32).rearrange("p (e i) -> p e i", e=e)
 
-        def move_scales(j):
-            for quad in range(4):
+        def load_gate(q):
+            nc.sync.dma_start(gates[q][:], gate[0:P, q * PIECE : (q + 1) * PIECE])
+
+        def load_pre(e):
+            nc.sync.dma_start(pre[e][:], a_rows[:, :, e * C : (e + 1) * C])
+
+        def load_w2(q):
+            nc.sync.dma_start(
+                as_i32(w2_t[q][:]), w2_words[2 * q : 2 * q + 2].rearrange("e g p b -> p (e g) b").bitcast(I32)
+            )
+
+        def load_scales(plane, scales):
+            for r in range(4):
                 nc.sync.dma_start(
-                    as_i32(s2_t[32 * quad : 32 * quad + 4, 4 * j : 4 * j + 4, :]),
-                    as_i32(s2_mid[16 * j + 4 * quad : 16 * j + 4 * quad + 4]),
+                    as_i32(plane[r:P:32]),
+                    scales[:, :, r:16:4, :].rearrange("e g f k -> f (e g) k").bitcast(I32),
                 )
 
-        for j in range(2):
-            nc.sync.dma_start(
-                as_i32(s2_raw[16 * j : 16 * j + 16]),
-                w2_scales[4 * j : 4 * j + 4].rearrange("e g f i -> (g f) e i").bitcast(I32),
-            )
-        load_w2(0)
-        nc.vector.tensor_copy(
-            s2_mid[:].rearrange("p e (t m) -> p e t m", t=PACK), s2_raw[:].rearrange("p e (m t) -> p e t m", t=PACK)
-        )
         nc.sync.dma_start(offs_t[:], offs)
         load_gate(0)
         for t in range(PACK):
             nc.sync.dma_start(dy[t][:], dyT_rows[:, t, :])
         load_gate(1)
         load_pre(0)
-        move_scales(0)
-        load_gate(2)
         load_pre(1)
-        load_w2(1)
-        nc.sync.dma_start(as_i32(w1_t[:]), w1_words.rearrange("e g p b -> p (e g) b").bitcast(I32))
-        for quad in range(4):
-            nc.sync.dma_start(
-                as_i32(s1_t[32 * quad : 32 * quad + 4]),
-                w1_scales[:, :, 4 * quad : 4 * quad + 4, :].rearrange("e g f k -> f (e g) k").bitcast(I32),
-            )
-        load_gate(3)
+        load_gate(2)
+        load_w2(0)
+        load_scales(s2_t, w2_scales)
         load_pre(2)
-        load_w2(2)
-        move_scales(1)
-        load_w2(3)
         load_pre(3)
+        load_gate(3)
+        load_pre(4)
+        load_w2(1)
+        load_pre(5)
+        load_w2(2)
+        nc.sync.dma_start(as_i32(w1_t[:]), w1_words.rearrange("e g p b -> p (e g) b").bitcast(I32))
+        load_scales(s1_t, w1_scales)
+        load_pre(6)
+        load_w2(3)
+        load_pre(7)
         nc.sync.dma_start(pos1_t[:], pos1)
         nc.sync.dma_start(pos2_t[:], pos2)
 
-        g4, grouped, signs, ones, codes, raws, das = {}, {}, {}, {}, {}, {}, {}
+        g4 = [keep.tile([P, PACK, PIECE], F32, name=f"g4_{j}") for j in range(2)] * 2
+        grouped, signs, ones, codes, turned, das = {}, {}, {}, {}, {}, {}
 
-        def gather(q, t):
-            if t == 0:
-                g4[q] = work.tile([P, PACK, PIECE], F32, name="g4")
+        def gather(q, t, first, width):
             nc.vector.tensor_tensor(
-                g4[q][:, t, :],
-                dy[t][:].indirect(offs_t[:, q * (PIECE // 16) : (q + 1) * (PIECE // 16)]),
-                gates[q][:],
+                g4[q][:, t, first : first + width],
+                dy[t][:].indirect(offs_t[:, (q * PIECE + first) // 16 : (q * PIECE + first + width) // 16]),
+                gates[q][:, first : first + width],
                 MULT,
             )
 
-        def permute_words(q):
-            nc.vector.tensor_copy(
-                w2_t[q][:].rearrange("p e b -> p (e b)").bitcast(U16).rearrange("p (e t m) -> p e t m", e=2, t=PACK),
-                w2_raw[q][:].rearrange("p e b -> p (e b)").bitcast(U16).rearrange("p (e m t) -> p e t m", e=2, t=PACK),
+        def interleave(q, first, width, copy):
+            if q > 0:
+                spent = pre[2 * (q - 1) + first // C][:].rearrange("p t s -> p (t s)")[:, 0 : 2 * C].bitcast(BF16)
+                grouped[q, first] = spent.rearrange("p (s t) -> p s t", t=PACK)
+            else:
+                grouped[q, first] = keep.tile([P, width, PACK], BF16, name=f"gb_{first}", align_bytes=64)
+            cols = slice(first, first + width)
+            copy(
+                grouped[q, first][:].rearrange("p (c i) t -> p c t i", i=4),
+                g4[q][:, :, cols].rearrange("p t (c i) -> p c t i", i=4),
             )
 
-        def interleave(q):
-            grouped[q] = work.tile([P, PIECE, PACK], BF16, name="gb", align_bytes=64)
-            step = C if q == PIECES - 1 else PIECE
-            for first in range(0, PIECE, step):
-                cols = slice(first, first + step)
-                nc.scalar.copy(
-                    grouped[q][:, cols, :].rearrange("p (c i) t -> p c t i", i=4),
-                    g4[q][:, :, cols].rearrange("p t (c i) -> p c t i", i=4),
-                )
-
-        def sign(q):
-            signs[q] = work.tile([P, PIECE, PACK], BF16, name="sg")
+        def sign(e):
+            signs[e] = work.tile([P, C, PACK], BF16, name="sg")
             nc.scalar.activation(
-                signs[q][:].rearrange("p (c i) t -> p c t i", i=4),
-                pre[q][:].rearrange("p t (c i) -> p c t i", i=4),
+                signs[e][:].rearrange("p (c i) t -> p c t i", i=4),
+                pre[e][:].rearrange("p t (c i) -> p c t i", i=4),
                 SIGN,
             )
 
-        def mask(q):
-            ones[q] = work.tile([P, PIECE, PACK], BF16, name="mk")
-            if q == 0:
-                nc.scalar.activation(ones[q][:], signs[q][:], RELU)
-            else:
-                nc.vector.tensor_scalar(ones[q][:], signs[q][:], 0.0, None, MAX)
+        def mask(e):
+            ones[e] = work.tile([P, C, PACK], BF16, name="mk")
+            nc.vector.tensor_scalar(ones[e][:], signs[e][:], 0.0, None, MAX)
+
+        def compare(e):
+            ones[e] = grouped[e // 2, e % 2 * C]
+            nc.vector.tensor_scalar(
+                ones[e][:].rearrange("p (c i) t -> p c t i", i=4),
+                pre[e][:].rearrange("p t (c i) -> p c t i", i=4),
+                0.0,
+                None,
+                IS_GT,
+            )
 
         def quantise_g(q, first, width):
             if first == 0:
-                codes[q] = (
-                    work.tile([P, PIECE], U32, name="g_words", align_bytes=64),
-                    work.tile([P, PIECE], U8, name="g_scales", align_bytes=64),
-                )
-                das[q] = work.tile([P, PIECE, PACK], BF16, name="da", align_bytes=64)
-            cols = slice(first, first + width)
+                das[q] = keep.tile([P, PIECE, PACK], BF16, name=f"da{q}", align_bytes=64)
+            codes[q, first // C] = (
+                work.tile([P, width], U32, name="g_words", align_bytes=64, bufs=8),
+                work.tile([P, width], U8, name="g_scales", align_bytes=64, bufs=8),
+            )
             nc.vector.quantize_mx(
-                out=codes[q][0][:, cols].bitcast(FP8X4),
-                scales=codes[q][1][:, cols],
-                in_=grouped[q][:, cols, :].rearrange("p s t -> p (s t)"),
+                out=codes[q, first // C][0][:].bitcast(FP8X4),
+                scales=codes[q, first // C][1][:],
+                in_=grouped[q, first][:].rearrange("p s t -> p (s t)"),
             )
 
         def first_product(q, c):
             h = c * CHUNK // C
-            cols = slice(c * CHUNK, (c + 1) * CHUNK)
-            bank = psum1.tile([P, PACK, CHUNK], F32, name="bank")
-            for t in range(PACK):
+            cols = slice((c % 2) * CHUNK, (c % 2 + 1) * CHUNK)
+            bank = psum.tile([P, H], F32, name=f"bank{c}")
+            nc.tensor.matmul_mx(
+                out=bank[:],
+                lhsT=codes[q, h][0][:, cols].bitcast(FP8X4),
+                lhsT_scale=codes[q, h][1][:, cols],
+                rhs=w2_t[q][:, h, :].bitcast(FP4X4),
+                rhs_scale=s2_t[:, 2 * q + h, :],
+                start=True,
+                stop=True,
+            )
+            spent = C if q == PIECES - 1 else 0
+            raw = g4[(q + 1) % 2][:, c, spent : spent + C].bitcast(BF16)
+            nc.scalar.copy(
+                raw[:].rearrange("s (u p e) -> s u p e", u=2, e=2),
+                bank[:].rearrange("s (p u e) -> s u p e", u=2, e=2),
+            )
+            if c % 2 == 0:
+                turned[q, h] = psum.tile([P, 2, C], F32, name=f"turned{(2 * q + h) % 3}")
+            for u in range(2):
+                nc.tensor.transpose(
+                    turned[q, h][:, u, (c % 2) * CHUNK : (c % 2 + 1) * CHUNK],
+                    raw[:].bitcast(F32)[:, u * P : (u + 1) * P],
+                    ident[:],
+                )
+
+        def mask_product(q, h):
+            cols = slice(h * C, (h + 1) * C)
+            nc.vector.tensor_tensor(
+                das[q][:, cols, :].rearrange("p s (u e) -> p s u e", u=2),
+                turned[q, h][:].rearrange("p u s -> p (u s)").bitcast(BF16).rearrange("p (u s e) -> p s u e", u=2, e=2),
+                ones[2 * q + h][:].rearrange("p s (u e) -> p s u e", u=2),
+                MULT,
+            )
+
+        def quantise_da(q, first, width):
+            nc.vector.quantize_mx(
+                out=da_words[q][:, first : first + width].bitcast(FP8X4),
+                scales=da_scales[q][:, first : first + width],
+                in_=das[q][:, first : first + width, :].rearrange("p s t -> p (s t)"),
+            )
+
+        def second_product(k, q, first, width):
+            acc = psum.tile([P, PIECE], F32, name="acc" if k == 0 else f"bank{q}")
+            for start in reversed(range(first, first + width, C)):
+                span = slice(start, start + C)
+                h = start // C
                 nc.tensor.matmul_mx(
-                    out=bank[:, t, :],
-                    lhsT=w2_t[q][:, h, t * 2 * P : (t + 1) * 2 * P].bitcast(FP4X4),
-                    lhsT_scale=s2_t[:, 2 * q + h, t * P : (t + 1) * P],
-                    rhs=codes[q][0][:, cols].bitcast(FP8X4),
-                    rhs_scale=codes[q][1][:, cols],
+                    out=acc[:, span],
+                    lhsT=w1_t[:, 2 * q + h, k * 2 * P : (k + 1) * 2 * P].bitcast(FP4X4),
+                    lhsT_scale=s1_t[:, 2 * q + h, k * P : (k + 1) * P],
+                    rhs=da_words[q][:, span].bitcast(FP8X4),
+                    rhs_scale=da_scales[q][:, span],
                     start=True,
                     stop=True,
                 )
-            return cols, bank[:].rearrange("p t s -> p s t")
+            nc.scalar.copy(dx[k][:, q * PIECE + first : q * PIECE + first + width], acc[:, first : first + width])
 
-        def product_by_mask(q, c):
-            if c == 0:
-                raws[q] = work.tile([P, PIECE, PACK], BF16, name="raw")
-            cols, bank = first_product(q, c)
-            nc.scalar.copy(raws[q][:, cols, :], bank)
-            if c == PIECE // CHUNK - 1:
-                nc.vector.tensor_tensor(das[q][:], raws[q][:], ones[q][:], MULT)
-
-        def product_by_sign(q, c):
-            cols, bank = first_product(q, c)
-            nc.vector.scalar_tensor_tensor(das[q][:, cols, :], signs[q][:, cols, :], 0.0, bank, MAX, MULT)
-
-        def second_product(q, first, width):
-            words = work.tile([P, PIECE], U32, name="da_words", align_bytes=64)
-            scales = work.tile([P, PIECE], U8, name="da_scales", align_bytes=64)
-            nc.vector.quantize_mx(
-                out=words[:, 0:width].bitcast(FP8X4),
-                scales=scales[:, 0:width],
-                in_=das[q][:, first : first + width, :].rearrange("p s t -> p (s t)"),
-            )
-            for k in range(2):
-                acc = psum2.tile([P, PIECE], F32, name=f"acc{k}")
-                for start in range(0, width, min(width, C)):
-                    span = slice(start, start + min(width, C))
-                    h = (first + start) // C
-                    nc.tensor.matmul_mx(
-                        out=acc[:, span],
-                        lhsT=w1_t[:, 2 * q + h, k * 2 * P : (k + 1) * 2 * P].bitcast(FP4X4),
-                        lhsT_scale=s1_t[:, 2 * q + h, k * P : (k + 1) * P],
-                        rhs=words[:, span].bitcast(FP8X4),
-                        rhs_scale=scales[:, span],
-                        start=True,
-                        stop=True,
-                    )
-                slots = slice(q * PIECE + first, q * PIECE + first + width)
-                if k == 0 and first + width == PIECE and q == PIECES - 1:
-                    nc.vector.tensor_copy(dx[k][:, slots], acc[:, 0:width])
-                else:
-                    nc.scalar.copy(dx[k][:, slots], acc[:, 0:width])
-
-        permute_words(0)
-        for q in range(2):
+        def gathers(q):
             for t in range(PACK):
-                gather(q, t)
-            interleave(q)
-            if q == 0:
-                sign(0)
-        quantise_g(0, 0, PIECE)
-        mask(0)
-        gather(2, 0)
-        gather(2, 1)
-        product_by_mask(0, 0)
-        product_by_mask(0, 1)
-        gather(2, 2)
-        product_by_mask(0, 2)
-        product_by_mask(0, 3)
-        quantise_g(1, 0, PIECE)
-        sign(1)
-        gather(2, 3)
-        interleave(2)
-        permute_words(1)
-        second_product(0, 0, PIECE)
-        mask(1)
-        gather(3, 0)
-        product_by_mask(1, 0)
-        product_by_mask(1, 1)
-        gather(3, 1)
-        permute_words(2)
-        product_by_mask(1, 2)
-        product_by_mask(1, 3)
-        gather(3, 2)
-        sign(2)
-        quantise_g(2, 0, PIECE)
-        gather(3, 3)
-        interleave(3)
-        second_product(1, 0, PIECE)
-        sign(3)
-        product_by_sign(2, 0)
-        product_by_sign(2, 1)
-        quantise_g(3, 0, C)
-        product_by_sign(2, 2)
-        product_by_sign(2, 3)
-        quantise_g(3, C, C)
-        permute_words(3)
-        product_by_sign(3, 0)
-        second_product(2, 0, PIECE)
-        product_by_sign(3, 1)
-        product_by_sign(3, 2)
-        second_product(3, 0, C)
-        product_by_sign(3, 3)
-        second_product(3, C, CHUNK)
-        second_product(3, C + CHUNK, CHUNK)
+                for first in (0, C) if (q, t) == (0, PACK - 1) else (0,):
+                    gather(q, t, first, C if (q, t) == (0, PACK - 1) else PIECE)
+
+        def round_g(q, copy_a, copy_b):
+            interleave(q, 0, C, copy_a)
+            interleave(q, C, C, copy_b)
+            for first in (0, C):
+                quantise_g(q, first, C)
+
+        def first_products(q):
+            for c in range(PIECE // CHUNK):
+                first_product(q, c)
+
+        def masked(q):
+            mask_product(q, 0)
+            mask_product(q, 1)
+            quantise_da(q, 0, PIECE)
+
+        for q in range(PIECES + 1):
+            if q < PIECES:
+                gathers(q)
+                round_g(q, nc.scalar.copy, nc.scalar.copy)
+            if q > 0:
+                first_products(q - 1)
+            if 0 < q < PIECES:
+                masked(q - 1)
+                second_product(0, q - 1, 0, PIECE)
+            for e in range(2 * q, min(2 * q + 2, E)):
+                if e < E - 2:
+                    sign(e)
+                    mask(e)
+                else:
+                    compare(e)
+        for h in range(2):
+            mask_product(3, h)
+            quantise_da(3, h * C, C)
+            second_product(0, 3, h * C, C)
 
         for k in range(2):
-            part1 = keep.tile([P, T], F32, name=f"part1_{k}")
-            nc.vector.tensor_copy(part1[:], dx[k][:].indirect(pos1_t[:]))
-            for first, width, adder in SHARES[k]:
-                part2 = keep.tile([P, width], F32, name=f"part2_{k}_{first}")
+            halves = []
+            for first in range(0, T, T // 2):
+                part1 = keep.tile([P, T // 2], F32, name=f"part1_{k}_{first}")
+                nc.vector.tensor_copy(part1[:], dx[k][:].indirect(pos1_t[:, first // 16 : (first + T // 2) // 16]))
+                halves.append(part1)
+            if k == 0:
+                dx.append(keep.tile([P, S], F32, name=f"da_words{PIECES - 1}", align_bytes=64))
+                for q in range(PIECES):
+                    second_product(1, q, 0, PIECE)
+            for first, width in ((0, 512), (512, 256), (768, 256)):
                 total = keep.tile([P, width], F32, name=f"total_{k}_{first}")
-                nc.vector.tensor_copy(part2[:], dx[k][:].indirect(pos2_t[:, first // 16 : (first + width) // 16]))
-                engine = nc.vector if adder == "vector" else nc.gpsimd
-                engine.tensor_tensor(total[:], part1[:, first : first + width], part2[:], ADD)
+                nc.vector.tensor_tensor(
+                    total[:],
+                    dx[k][:].indirect(pos2_t[:, first // 16 : (first + width) // 16]),
+                    halves[first // 512][:, first % 512 : first % 512 + width],
+                    ADD,
+                )
                 nc.sync.dma_start(out[k * P : (k + 1) * P, first : first + width], total[:])

@@ -53,7 +53,7 @@ def tile_moe_bdx_mlp_relu_kernel(
         w1_t = keep.tile([P, E, 2 * K], U8, name="w1_t", align_bytes=64)
         s1_t = keep.tile([P, E, K], U8, name="s1_t", align_bytes=64)
         dx = [keep.tile([P, S], F32, name="dx0")]
-        da_words = [keep.tile([P, PIECE], U32, name=f"da_words{q}", align_bytes=64) for q in range(PIECES)]
+        da_words = {}
         da_scales = [keep.tile([P, PIECE], U8, name=f"da_scales{q}", align_bytes=64) for q in range(PIECES)]
         ident = keep.tile([P, P], F32, name="ident")
 
@@ -87,31 +87,32 @@ def tile_moe_bdx_mlp_relu_kernel(
                 )
 
         nc.sync.dma_start(offs_t[:], offs)
-        load_gate(0)
         for t in range(PACK):
+            if t < 2:
+                nc.sync.dma_start(gates[0][:, t * C : (t + 1) * C], gate[0:P, t * C : (t + 1) * C])
             nc.sync.dma_start(dy[t][:], dyT_rows[:, t, :])
         load_gate(1)
+        load_gate(2)
+        load_gate(3)
         load_pre(0)
         load_pre(1)
-        load_gate(2)
+        load_pre(2)
         load_w2(0)
         load_scales(s2_t, w2_scales)
-        load_pre(2)
         load_pre(3)
-        load_gate(3)
-        load_pre(4)
         load_w2(1)
-        load_pre(5)
+        load_pre(4)
         load_w2(2)
         nc.sync.dma_start(as_i32(w1_t[:]), w1_words.rearrange("e g p b -> p (e g) b").bitcast(I32))
         load_scales(s1_t, w1_scales)
-        load_pre(6)
+        load_pre(5)
         load_w2(3)
+        load_pre(6)
         load_pre(7)
         nc.sync.dma_start(pos1_t[:], pos1)
         nc.sync.dma_start(pos2_t[:], pos2)
 
-        g4 = [keep.tile([P, PACK, PIECE], F32, name=f"g4_{j}") for j in range(2)] * 2
+        g4 = [keep.tile([P, PACK, PIECE], F32, name=f"g4_{j}", align_bytes=64) for j in range(2)] * 2
         grouped, signs, ones, codes, turned, das = {}, {}, {}, {}, {}, {}
 
         def gather(q, t, first, width):
@@ -123,8 +124,10 @@ def tile_moe_bdx_mlp_relu_kernel(
             )
 
         def interleave(q, first, width, copy):
-            if q > 0:
-                spent = pre[2 * (q - 1) + first // C][:].rearrange("p t s -> p (t s)")[:, 0 : 2 * C].bitcast(BF16)
+            if q == PIECES - 1:
+                grouped[q, first] = g4[0][:, first // C, :].bitcast(BF16).rearrange("p (s t) -> p s t", t=PACK)
+            elif q > 0:
+                spent = pre[2 * q - 1][:].rearrange("p t s -> p (t s)")[:, 2 * first : 2 * (first + C)].bitcast(BF16)
                 grouped[q, first] = spent.rearrange("p (s t) -> p s t", t=PACK)
             else:
                 grouped[q, first] = keep.tile([P, width, PACK], BF16, name=f"gb_{first}", align_bytes=64)
@@ -135,7 +138,7 @@ def tile_moe_bdx_mlp_relu_kernel(
             )
 
         def sign(e):
-            signs[e] = work.tile([P, C, PACK], BF16, name="sg")
+            signs[e] = work.tile([P, C, PACK], BF16, name="sg", bufs=E)
             nc.scalar.activation(
                 signs[e][:].rearrange("p (c i) t -> p c t i", i=4),
                 pre[e][:].rearrange("p t (c i) -> p c t i", i=4),
@@ -143,7 +146,7 @@ def tile_moe_bdx_mlp_relu_kernel(
             )
 
         def mask(e):
-            ones[e] = work.tile([P, C, PACK], BF16, name="mk")
+            ones[e] = work.tile([P, C, PACK], BF16, name="mk", bufs=E)
             nc.vector.tensor_scalar(ones[e][:], signs[e][:], 0.0, None, MAX)
 
         def compare(e):
@@ -160,7 +163,7 @@ def tile_moe_bdx_mlp_relu_kernel(
             if first == 0:
                 das[q] = keep.tile([P, PIECE, PACK], BF16, name=f"da{q}", align_bytes=64)
             codes[q, first // C] = (
-                work.tile([P, width], U32, name="g_words", align_bytes=64, bufs=8),
+                keep.tile([P, width], U32, name=f"g_words{q}_{first // C}", align_bytes=64),
                 work.tile([P, width], U8, name="g_scales", align_bytes=64, bufs=8),
             )
             nc.vector.quantize_mx(
@@ -172,9 +175,9 @@ def tile_moe_bdx_mlp_relu_kernel(
         def first_product(q, c):
             h = c * CHUNK // C
             cols = slice((c % 2) * CHUNK, (c % 2 + 1) * CHUNK)
-            bank = psum.tile([P, H], F32, name=f"bank{c}")
+            bank = psum.tile([P, H], F32, name=f"bank{c}")[:]
             nc.tensor.matmul_mx(
-                out=bank[:],
+                out=bank,
                 lhsT=codes[q, h][0][:, cols].bitcast(FP8X4),
                 lhsT_scale=codes[q, h][1][:, cols],
                 rhs=w2_t[q][:, h, :].bitcast(FP4X4),
@@ -182,14 +185,18 @@ def tile_moe_bdx_mlp_relu_kernel(
                 start=True,
                 stop=True,
             )
-            spent = C if q == PIECES - 1 else 0
-            raw = g4[(q + 1) % 2][:, c, spent : spent + C].bitcast(BF16)
+            if q == 0:
+                raw = keep.tile([P, H], BF16, name=f"raw{c}")
+            elif q == PIECES - 1:
+                raw = keep.tile([P, H], BF16, name=f"late{c}", align_bytes=64)
+            else:
+                raw = g4[(q + 1) % 2][:, 2 + c % 2, c // 2 * C : (c // 2 + 1) * C].bitcast(BF16)
             nc.scalar.copy(
                 raw[:].rearrange("s (u p e) -> s u p e", u=2, e=2),
-                bank[:].rearrange("s (p u e) -> s u p e", u=2, e=2),
+                bank.rearrange("s (p u e) -> s u p e", u=2, e=2),
             )
             if c % 2 == 0:
-                turned[q, h] = psum.tile([P, 2, C], F32, name=f"turned{(2 * q + h) % 3}")
+                turned[q, h] = psum.tile([P, 2, C], F32, name=f"ring{(2 * q + h) % 4}")
             for u in range(2):
                 nc.tensor.transpose(
                     turned[q, h][:, u, (c % 2) * CHUNK : (c % 2 + 1) * CHUNK],
@@ -207,14 +214,22 @@ def tile_moe_bdx_mlp_relu_kernel(
             )
 
         def quantise_da(q, first, width):
+            name = {(0, 0): "pre3", (2, 0): "late1", (3, 0): "late3"}.get((q, first), f"da_words{q}")
+            words = keep.tile([P, width], U32, name=name, align_bytes=64)
+            for start in range(0, width, C):
+                da_words[2 * q + (first + start) // C] = words[:, start : start + C]
             nc.vector.quantize_mx(
-                out=da_words[q][:, first : first + width].bitcast(FP8X4),
+                out=words[:].bitcast(FP8X4),
                 scales=da_scales[q][:, first : first + width],
                 in_=das[q][:, first : first + width, :].rearrange("p s t -> p (s t)"),
             )
 
         def second_product(k, q, first, width):
-            acc = psum.tile([P, PIECE], F32, name="acc" if k == 0 else f"bank{q}")
+            if k == 0:
+                name = "ring0" if first else f"bank{(q + 2) % 4}"
+            else:
+                name = ("bank1", "ring0")[q % 2]
+            acc = psum.tile([P, PIECE], F32, name=name)
             for start in reversed(range(first, first + width, C)):
                 span = slice(start, start + C)
                 h = start // C
@@ -222,7 +237,7 @@ def tile_moe_bdx_mlp_relu_kernel(
                     out=acc[:, span],
                     lhsT=w1_t[:, 2 * q + h, k * 2 * P : (k + 1) * 2 * P].bitcast(FP4X4),
                     lhsT_scale=s1_t[:, 2 * q + h, k * P : (k + 1) * P],
-                    rhs=da_words[q][:, span].bitcast(FP8X4),
+                    rhs=da_words[2 * q + h].bitcast(FP8X4),
                     rhs_scale=da_scales[q][:, span],
                     start=True,
                     stop=True,
@@ -231,8 +246,9 @@ def tile_moe_bdx_mlp_relu_kernel(
 
         def gathers(q):
             for t in range(PACK):
-                for first in (0, C) if (q, t) == (0, PACK - 1) else (0,):
-                    gather(q, t, first, C if (q, t) == (0, PACK - 1) else PIECE)
+                width = C if q == 0 and t in (0, PACK - 1) else PIECE
+                for first in range(0, PIECE, width):
+                    gather(q, t, first, width)
 
         def round_g(q, copy_a, copy_b):
             interleave(q, 0, C, copy_a)
@@ -247,7 +263,6 @@ def tile_moe_bdx_mlp_relu_kernel(
         def masked(q):
             mask_product(q, 0)
             mask_product(q, 1)
-            quantise_da(q, 0, PIECE)
 
         for q in range(PIECES + 1):
             if q < PIECES:
@@ -257,17 +272,25 @@ def tile_moe_bdx_mlp_relu_kernel(
                 first_products(q - 1)
             if 0 < q < PIECES:
                 masked(q - 1)
-                second_product(0, q - 1, 0, PIECE)
+            if q == 2:
+                quantise_da(0, 0, PIECE)
+                quantise_da(1, 0, PIECE)
             for e in range(2 * q, min(2 * q + 2, E)):
                 if e < E - 2:
                     sign(e)
                     mask(e)
                 else:
                     compare(e)
-        for h in range(2):
-            mask_product(3, h)
-            quantise_da(3, h * C, C)
-            second_product(0, 3, h * C, C)
+        for q in range(2):
+            second_product(0, q, 0, PIECE)
+        mask_product(3, 0)
+        quantise_da(2, 0, PIECE)
+        second_product(0, 2, 0, PIECE)
+        mask_product(3, 1)
+        quantise_da(3, 0, C)
+        quantise_da(3, C, C)
+        second_product(0, 3, 0, C)
+        second_product(0, 3, C, C)
 
         for k in range(2):
             halves = []
@@ -276,10 +299,10 @@ def tile_moe_bdx_mlp_relu_kernel(
                 nc.vector.tensor_copy(part1[:], dx[k][:].indirect(pos1_t[:, first // 16 : (first + T // 2) // 16]))
                 halves.append(part1)
             if k == 0:
-                dx.append(keep.tile([P, S], F32, name=f"da_words{PIECES - 1}", align_bytes=64))
+                dx.append(keep.tile([P, S], F32, name="dx1"))
                 for q in range(PIECES):
                     second_product(1, q, 0, PIECE)
-            for first, width in ((0, 512), (512, 256), (768, 256)):
+            for first, width in ((0, 512), (512, 384), (896, 128)):
                 total = keep.tile([P, width], F32, name=f"total_{k}_{first}")
                 nc.vector.tensor_tensor(
                     total[:],

@@ -29,6 +29,7 @@ BYTES = 4 * N * T + 4 * H * S + E * (N * H + H * K) * 17 // 32 + 4 * S + 2 * S +
 PIECE = 512
 PIECES = S // PIECE
 CHUNK = 128
+BANKS = ((0, 1, 2, 3), (3, 2, 4, 5), (0, 1, 3, 2), (4, 5, 0, 1))
 
 
 def tile_moe_bdx_mlp_relu_kernel(
@@ -126,6 +127,8 @@ def tile_moe_bdx_mlp_relu_kernel(
         def interleave(q, first, width, copy):
             if q == PIECES - 1:
                 grouped[q, first] = g4[0][:, first // C, :].bitcast(BF16).rearrange("p (s t) -> p s t", t=PACK)
+            elif q == 2:
+                grouped[q, first] = g4[1][:, 1 + first // C, :].bitcast(BF16).rearrange("p (s t) -> p s t", t=PACK)
             elif q > 0:
                 spent = pre[2 * q - 1][:].rearrange("p t s -> p (t s)")[:, 2 * first : 2 * (first + C)].bitcast(BF16)
                 grouped[q, first] = spent.rearrange("p (s t) -> p s t", t=PACK)
@@ -138,7 +141,10 @@ def tile_moe_bdx_mlp_relu_kernel(
             )
 
         def sign(e):
-            signs[e] = work.tile([P, C, PACK], BF16, name="sg", bufs=E)
+            if e == 6:
+                signs[e] = g4[1][:, 0, :].bitcast(BF16).rearrange("p (s t) -> p s t", t=PACK)
+            else:
+                signs[e] = work.tile([P, C, PACK], BF16, name="sg", bufs=E)
             nc.scalar.activation(
                 signs[e][:].rearrange("p (c i) t -> p c t i", i=4),
                 pre[e][:].rearrange("p t (c i) -> p c t i", i=4),
@@ -146,11 +152,11 @@ def tile_moe_bdx_mlp_relu_kernel(
             )
 
         def mask(e):
-            ones[e] = work.tile([P, C, PACK], BF16, name="mk", bufs=E)
+            ones[e] = keep.tile([P, C, PACK], BF16, name=f"mk{e}", align_bytes=64)
             nc.vector.tensor_scalar(ones[e][:], signs[e][:], 0.0, None, MAX)
 
         def compare(e):
-            ones[e] = grouped[e // 2, e % 2 * C]
+            ones[e] = keep.tile([P, C, PACK], BF16, name=f"mk{e - 2}", align_bytes=64)
             nc.vector.tensor_scalar(
                 ones[e][:].rearrange("p (c i) t -> p c t i", i=4),
                 pre[e][:].rearrange("p t (c i) -> p c t i", i=4),
@@ -160,10 +166,12 @@ def tile_moe_bdx_mlp_relu_kernel(
             )
 
         def quantise_g(q, first, width):
-            if first == 0:
+            if first == 0 and q == 2:
+                das[q] = g4[0][:, 0:2, :].rearrange("p t s -> p (t s)").bitcast(BF16).rearrange("p (s t) -> p s t", t=PACK)
+            elif first == 0:
                 das[q] = keep.tile([P, PIECE, PACK], BF16, name=f"da{q}", align_bytes=64)
             codes[q, first // C] = (
-                keep.tile([P, width], U32, name=f"g_words{q}_{first // C}", align_bytes=64),
+                keep.tile([P, width], U32, name="mk0" if first and q == 1 else f"g_words{q}_{first // C}", align_bytes=64),
                 work.tile([P, width], U8, name="g_scales", align_bytes=64, bufs=8),
             )
             nc.vector.quantize_mx(
@@ -175,7 +183,7 @@ def tile_moe_bdx_mlp_relu_kernel(
         def first_product(q, c):
             h = c * CHUNK // C
             cols = slice((c % 2) * CHUNK, (c % 2 + 1) * CHUNK)
-            bank = psum.tile([P, H], F32, name=f"bank{c}")[:]
+            bank = psum.tile([P, H], F32, name=f"bank{BANKS[q][c]}")[:]
             nc.tensor.matmul_mx(
                 out=bank,
                 lhsT=codes[q, h][0][:, cols].bitcast(FP8X4),
@@ -185,22 +193,28 @@ def tile_moe_bdx_mlp_relu_kernel(
                 start=True,
                 stop=True,
             )
-            if q == 0:
-                raw = keep.tile([P, H], BF16, name=f"raw{c}")
-            elif q == PIECES - 1:
-                raw = keep.tile([P, H], BF16, name=f"late{c}", align_bytes=64)
+            if (q, c) == (0, 3):
+                raw = g4[1][:, 1:3, 0:P]
+            elif (q, c) in ((0, 1), (0, 2)):
+                raw = g4[1][:, 3 * (c - 1), 0:C].rearrange("s (u p) -> s u p", u=2)
+            elif (q, c) == (2, 0):
+                raw = g4[0][:, 0:2, 0:P]
+            elif q == 1:
+                raw = g4[0][:, 2 + c % 2, c // 2 * C : (c // 2 + 1) * C].rearrange("s (u p) -> s u p", u=2)
+            elif q == PIECES - 1 and c == 2:
+                raw = dx[0][:, 0 : 2 * PIECE].rearrange("s (u p) -> s u p", u=2)[:, :, 0:P]
             else:
-                raw = g4[(q + 1) % 2][:, 2 + c % 2, c // 2 * C : (c // 2 + 1) * C].bitcast(BF16)
+                raw = keep.tile([P, 2, P], F32, name=f"raw{q}_{c}", align_bytes=64)[:]
             nc.scalar.copy(
-                raw[:].rearrange("s (u p e) -> s u p e", u=2, e=2),
+                raw.bitcast(BF16).rearrange("s u (p e) -> s u p e", e=2),
                 bank.rearrange("s (p u e) -> s u p e", u=2, e=2),
             )
             if c % 2 == 0:
-                turned[q, h] = psum.tile([P, 2, C], F32, name=f"ring{(2 * q + h) % 4}")
+                turned[q, h] = psum.tile([P, 2, C], F32, name=f"ring{h}")
             for u in range(2):
                 nc.tensor.transpose(
                     turned[q, h][:, u, (c % 2) * CHUNK : (c % 2 + 1) * CHUNK],
-                    raw[:].bitcast(F32)[:, u * P : (u + 1) * P],
+                    raw[:, u, :],
                     ident[:],
                 )
 
@@ -214,7 +228,7 @@ def tile_moe_bdx_mlp_relu_kernel(
             )
 
         def quantise_da(q, first, width):
-            name = {(0, 0): "pre3", (2, 0): "late1", (3, 0): "late3"}.get((q, first), f"da_words{q}")
+            name = {(0, 0): "g_words2_1", (3, 0): "raw3_3"}.get((q, first), f"da_words{q}")
             words = keep.tile([P, width], U32, name=name, align_bytes=64)
             for start in range(0, width, C):
                 da_words[2 * q + (first + start) // C] = words[:, start : start + C]
@@ -226,9 +240,9 @@ def tile_moe_bdx_mlp_relu_kernel(
 
         def second_product(k, q, first, width):
             if k == 0:
-                name = "ring0" if first else f"bank{(q + 2) % 4}"
+                name = "bank5" if first else ("bank3", "bank2", "bank1", "bank4")[q]
             else:
-                name = ("bank1", "ring0")[q % 2]
+                name = ("bank4", "bank5")[q % 2]
             acc = psum.tile([P, PIECE], F32, name=name)
             for start in reversed(range(first, first + width, C)):
                 span = slice(start, start + C)
@@ -242,7 +256,8 @@ def tile_moe_bdx_mlp_relu_kernel(
                     start=True,
                     stop=True,
                 )
-            nc.scalar.copy(dx[k][:, q * PIECE + first : q * PIECE + first + width], acc[:, first : first + width])
+            copy = nc.vector.tensor_copy if k == 0 and q == 3 else nc.scalar.copy
+            copy(dx[k][:, q * PIECE + first : q * PIECE + first + width], acc[:, first : first + width])
 
         def gathers(q):
             for t in range(PACK):
@@ -253,8 +268,9 @@ def tile_moe_bdx_mlp_relu_kernel(
         def round_g(q, copy_a, copy_b):
             interleave(q, 0, C, copy_a)
             interleave(q, C, C, copy_b)
-            for first in (0, C):
-                quantise_g(q, first, C)
+            quantise_g(q, 0, C)
+            if q != 1:
+                quantise_g(q, C, C)
 
         def first_products(q):
             for c in range(PIECE // CHUNK):
@@ -264,27 +280,32 @@ def tile_moe_bdx_mlp_relu_kernel(
             mask_product(q, 0)
             mask_product(q, 1)
 
-        for q in range(PIECES + 1):
-            if q < PIECES:
-                gathers(q)
-                round_g(q, nc.scalar.copy, nc.scalar.copy)
-            if q > 0:
-                first_products(q - 1)
-            if 0 < q < PIECES:
-                masked(q - 1)
+        for q in range(PIECES - 1):
+            gathers(q)
             if q == 2:
-                quantise_da(0, 0, PIECE)
-                quantise_da(1, 0, PIECE)
-            for e in range(2 * q, min(2 * q + 2, E)):
-                if e < E - 2:
-                    sign(e)
-                    mask(e)
-                else:
-                    compare(e)
+                first_products(0)
+                mask_product(0, 0)
+                quantise_g(1, C, C)
+                mask_product(0, 1)
+            round_g(q, nc.scalar.copy, nc.scalar.copy)
+            for e in (2 * q, 2 * q + 1):
+                sign(e)
+                mask(e)
+        first_products(1)
+        masked(1)
+        quantise_da(1, 0, PIECE)
+        first_products(2)
+        quantise_da(0, 0, PIECE)
+        gathers(3)
+        round_g(3, nc.scalar.copy, nc.scalar.copy)
+        masked(2)
+        compare(6)
+        compare(7)
+        quantise_da(2, 0, PIECE)
+        first_products(3)
         for q in range(2):
             second_product(0, q, 0, PIECE)
         mask_product(3, 0)
-        quantise_da(2, 0, PIECE)
         second_product(0, 2, 0, PIECE)
         mask_product(3, 1)
         quantise_da(3, 0, C)

@@ -30,6 +30,7 @@ PIECE = 512
 PIECES = S // PIECE
 CHUNK = 128
 BANKS = ((0, 1, 2, 3), (3, 2, 4, 5), (0, 1, 3, 2), (4, 5, 0, 1))
+SHARES = (((0, 512), (512, 512)), ((0, 512), (512, 384), (896, 128)))
 
 
 def tile_moe_bdx_mlp_relu_kernel(
@@ -39,7 +40,6 @@ def tile_moe_bdx_mlp_relu_kernel(
     with ExitStack() as ctx:
         lists = ctx.enter_context(tc.tile_pool(name="lists", bufs=1))
         keep = ctx.enter_context(tc.tile_pool(name="keep", bufs=1))
-        work = ctx.enter_context(tc.tile_pool(name="work", bufs=4))
         psum = ctx.enter_context(tc.psum_pool(name="psum", bufs=1))
 
         offs_t = lists.tile([P, S // 16], U16, name="offs_t")
@@ -53,9 +53,8 @@ def tile_moe_bdx_mlp_relu_kernel(
         s2_t = keep.tile([P, E, H], U8, name="s2_t", align_bytes=64)
         w1_t = keep.tile([P, E, 2 * K], U8, name="w1_t", align_bytes=64)
         s1_t = keep.tile([P, E, K], U8, name="s1_t", align_bytes=64)
-        dx = [keep.tile([P, S], F32, name="dx0")]
-        da_words = {}
-        da_scales = [keep.tile([P, PIECE], U8, name=f"da_scales{q}", align_bytes=64) for q in range(PIECES)]
+        dx = [keep.tile([P, S], F32, name=f"dx{k}") for k in range(2)]
+        planes = [keep.tile([P, PACK, PIECE], F32, name=f"planes{j}", align_bytes=64) for j in range(2)]
         ident = keep.tile([P, P], F32, name="ident")
 
         nc.gpsimd.memset(s2_t[:].rearrange("p e i -> p (e i)").bitcast(I32), 0)
@@ -68,6 +67,9 @@ def tile_moe_bdx_mlp_relu_kernel(
         def as_i32(view):
             e = view.shape[1]
             return view.rearrange("p e i -> p (e i)").bitcast(I32).rearrange("p (e i) -> p e i", e=e)
+
+        def as_words(view):
+            return view.rearrange("p t s -> p (t s)").bitcast(BF16).rearrange("p (s t) -> p s t", t=PACK)
 
         def load_gate(q):
             nc.sync.dma_start(gates[q][:], gate[0:P, q * PIECE : (q + 1) * PIECE])
@@ -113,205 +115,180 @@ def tile_moe_bdx_mlp_relu_kernel(
         nc.sync.dma_start(pos1_t[:], pos1)
         nc.sync.dma_start(pos2_t[:], pos2)
 
-        g4 = [keep.tile([P, PACK, PIECE], F32, name=f"g4_{j}", align_bytes=64) for j in range(2)] * 2
-        grouped, signs, ones, codes, turned, das = {}, {}, {}, {}, {}, {}
-
-        def gather(q, t, first, width):
-            nc.vector.tensor_tensor(
-                g4[q][:, t, first : first + width],
-                dy[t][:].indirect(offs_t[:, (q * PIECE + first) // 16 : (q * PIECE + first + width) // 16]),
-                gates[q][:, first : first + width],
-                MULT,
-            )
-
-        def interleave(q, first, width, copy):
-            if q == PIECES - 1:
-                grouped[q, first] = g4[0][:, first // C, :].bitcast(BF16).rearrange("p (s t) -> p s t", t=PACK)
-            elif q == 2:
-                grouped[q, first] = g4[1][:, 1 + first // C, :].bitcast(BF16).rearrange("p (s t) -> p s t", t=PACK)
-            elif q > 0:
-                spent = pre[2 * q - 1][:].rearrange("p t s -> p (t s)")[:, 2 * first : 2 * (first + C)].bitcast(BF16)
-                grouped[q, first] = spent.rearrange("p (s t) -> p s t", t=PACK)
-            else:
-                grouped[q, first] = keep.tile([P, width, PACK], BF16, name=f"gb_{first}", align_bytes=64)
-            cols = slice(first, first + width)
-            copy(
-                grouped[q, first][:].rearrange("p (c i) t -> p c t i", i=4),
-                g4[q][:, :, cols].rearrange("p t (c i) -> p c t i", i=4),
-            )
-
-        def sign(e):
-            if e == 6:
-                signs[e] = g4[1][:, 0, :].bitcast(BF16).rearrange("p (s t) -> p s t", t=PACK)
-            else:
-                signs[e] = work.tile([P, C, PACK], BF16, name="sg", bufs=E)
-            nc.scalar.activation(
-                signs[e][:].rearrange("p (c i) t -> p c t i", i=4),
-                pre[e][:].rearrange("p t (c i) -> p c t i", i=4),
-                SIGN,
-            )
-
-        def mask(e):
-            ones[e] = keep.tile([P, C, PACK], BF16, name=f"mk{e}", align_bytes=64)
-            nc.vector.tensor_scalar(ones[e][:], signs[e][:], 0.0, None, MAX)
-
-        def compare(e):
-            ones[e] = keep.tile([P, C, PACK], BF16, name=f"mk{e - 2}", align_bytes=64)
-            nc.vector.tensor_scalar(
-                ones[e][:].rearrange("p (c i) t -> p c t i", i=4),
-                pre[e][:].rearrange("p t (c i) -> p c t i", i=4),
-                0.0,
-                None,
-                IS_GT,
-            )
-
-        def quantise_g(q, first, width):
-            if first == 0 and q == 2:
-                das[q] = g4[0][:, 0:2, :].rearrange("p t s -> p (t s)").bitcast(BF16).rearrange("p (s t) -> p s t", t=PACK)
-            elif first == 0:
-                das[q] = keep.tile([P, PIECE, PACK], BF16, name=f"da{q}", align_bytes=64)
-            codes[q, first // C] = (
-                keep.tile([P, width], U32, name="mk0" if first and q == 1 else f"g_words{q}_{first // C}", align_bytes=64),
-                work.tile([P, width], U8, name="g_scales", align_bytes=64, bufs=8),
-            )
-            nc.vector.quantize_mx(
-                out=codes[q, first // C][0][:].bitcast(FP8X4),
-                scales=codes[q, first // C][1][:],
-                in_=grouped[q, first][:].rearrange("p s t -> p (s t)"),
-            )
-
-        def first_product(q, c):
-            h = c * CHUNK // C
-            cols = slice((c % 2) * CHUNK, (c % 2 + 1) * CHUNK)
-            bank = psum.tile([P, H], F32, name=f"bank{BANKS[q][c]}")[:]
-            nc.tensor.matmul_mx(
-                out=bank,
-                lhsT=codes[q, h][0][:, cols].bitcast(FP8X4),
-                lhsT_scale=codes[q, h][1][:, cols],
-                rhs=w2_t[q][:, h, :].bitcast(FP4X4),
-                rhs_scale=s2_t[:, 2 * q + h, :],
-                start=True,
-                stop=True,
-            )
-            if (q, c) == (0, 3):
-                raw = g4[1][:, 1:3, 0:P]
-            elif (q, c) in ((0, 1), (0, 2)):
-                raw = g4[1][:, 3 * (c - 1), 0:C].rearrange("s (u p) -> s u p", u=2)
-            elif (q, c) == (2, 0):
-                raw = g4[0][:, 0:2, 0:P]
-            elif q == 1:
-                raw = g4[0][:, 2 + c % 2, c // 2 * C : (c // 2 + 1) * C].rearrange("s (u p) -> s u p", u=2)
-            elif q == PIECES - 1 and c == 2:
-                raw = dx[0][:, 0 : 2 * PIECE].rearrange("s (u p) -> s u p", u=2)[:, :, 0:P]
-            else:
-                raw = keep.tile([P, 2, P], F32, name=f"raw{q}_{c}", align_bytes=64)[:]
-            nc.scalar.copy(
-                raw.bitcast(BF16).rearrange("s u (p e) -> s u p e", e=2),
-                bank.rearrange("s (p u e) -> s u p e", u=2, e=2),
-            )
-            if c % 2 == 0:
-                turned[q, h] = psum.tile([P, 2, C], F32, name=f"ring{h}")
-            for u in range(2):
-                nc.tensor.transpose(
-                    turned[q, h][:, u, (c % 2) * CHUNK : (c % 2 + 1) * CHUNK],
-                    raw[:, u, :],
-                    ident[:],
-                )
-
-        def mask_product(q, h):
-            cols = slice(h * C, (h + 1) * C)
-            nc.vector.tensor_tensor(
-                das[q][:, cols, :].rearrange("p s (u e) -> p s u e", u=2),
-                turned[q, h][:].rearrange("p u s -> p (u s)").bitcast(BF16).rearrange("p (u s e) -> p s u e", u=2, e=2),
-                ones[2 * q + h][:].rearrange("p s (u e) -> p s u e", u=2),
-                MULT,
-            )
-
-        def quantise_da(q, first, width):
-            name = {(0, 0): "g_words2_1", (3, 0): "raw3_3"}.get((q, first), f"da_words{q}")
-            words = keep.tile([P, width], U32, name=name, align_bytes=64)
-            for start in range(0, width, C):
-                da_words[2 * q + (first + start) // C] = words[:, start : start + C]
-            nc.vector.quantize_mx(
-                out=words[:].bitcast(FP8X4),
-                scales=da_scales[q][:, first : first + width],
-                in_=das[q][:, first : first + width, :].rearrange("p s t -> p (s t)"),
-            )
-
-        def second_product(k, q, first, width):
-            if k == 0:
-                name = "bank5" if first else ("bank3", "bank2", "bank1", "bank4")[q]
-            else:
-                name = ("bank4", "bank5")[q % 2]
-            acc = psum.tile([P, PIECE], F32, name=name)
-            for start in reversed(range(first, first + width, C)):
-                span = slice(start, start + C)
-                h = start // C
-                nc.tensor.matmul_mx(
-                    out=acc[:, span],
-                    lhsT=w1_t[:, 2 * q + h, k * 2 * P : (k + 1) * 2 * P].bitcast(FP4X4),
-                    lhsT_scale=s1_t[:, 2 * q + h, k * P : (k + 1) * P],
-                    rhs=da_words[2 * q + h].bitcast(FP8X4),
-                    rhs_scale=da_scales[q][:, span],
-                    start=True,
-                    stop=True,
-                )
-            copy = nc.vector.tensor_copy if k == 0 and q == 3 else nc.scalar.copy
-            copy(dx[k][:, q * PIECE + first : q * PIECE + first + width], acc[:, first : first + width])
+        g_codes, ones, turned, das, da_codes = {}, {}, {}, {}, {}
 
         def gathers(q):
             for t in range(PACK):
-                width = C if q == 0 and t in (0, PACK - 1) else PIECE
+                width = C if (q, t) == (0, 0) else PIECE
                 for first in range(0, PIECE, width):
-                    gather(q, t, first, width)
+                    nc.vector.tensor_tensor(
+                        planes[q % 2][:, t, first : first + width],
+                        dy[t][:].indirect(offs_t[:, (q * PIECE + first) // 16 : (q * PIECE + first + width) // 16]),
+                        gates[q][:, first : first + width],
+                        MULT,
+                    )
 
-        def round_g(q, copy_a, copy_b):
-            interleave(q, 0, C, copy_a)
-            interleave(q, C, C, copy_b)
-            quantise_g(q, 0, C)
-            if q != 1:
-                quantise_g(q, C, C)
+        def round_g(q, grouped):
+            for first in (0, C):
+                nc.scalar.copy(
+                    grouped[:, first : first + C, :].rearrange("p (c i) t -> p c t i", i=4),
+                    planes[q % 2][:, :, first : first + C].rearrange("p t (c i) -> p c t i", i=4),
+                )
+
+        def quantise_g(q, grouped, first, width, name):
+            words = keep.tile([P, width], U32, name=name, align_bytes=64)
+            scales = keep.tile([P, width], U8, name=f"g_scales{q}_{first}", align_bytes=64)
+            for start in range(0, width, CHUNK):
+                g_codes[q, (first + start) // CHUNK] = (words[:, start : start + CHUNK], scales[:, start : start + CHUNK])
+            nc.vector.quantize_mx(
+                out=words[:].bitcast(FP8X4),
+                scales=scales[:],
+                in_=grouped[:, first : first + width, :].rearrange("p s t -> p (s t)"),
+            )
+
+        def sign(e, signs):
+            nc.scalar.activation(signs, pre[e][:].rearrange("p (u e) s -> p u s e", u=2), SIGN)
+
+        def pair_mask(q):
+            signs = keep.tile([P, 2, 2, C, 2], BF16, name=f"signs{q}")
+            both = keep.tile([P, 2, 2, C, 2], BF16, name=f"ones{q}", align_bytes=64)
+            for h in range(2):
+                sign(2 * q + h, signs[:, h])
+                ones[2 * q + h] = both[:, h]
+            nc.vector.tensor_scalar(
+                both[:].rearrange("p h u s e -> p (h u s e)"),
+                signs[:].rearrange("p h u s e -> p (h u s e)"),
+                0.0,
+                None,
+                MAX,
+            )
+
+        def compare_mask(e, name):
+            ones[e] = keep.tile([P, 2, C, 2], BF16, name=name, align_bytes=64)[:]
+            nc.vector.tensor_scalar(ones[e], pre[e][:].rearrange("p (u e) s -> p u s e", u=2), 0.0, None, IS_GT)
 
         def first_products(q):
             for c in range(PIECE // CHUNK):
-                first_product(q, c)
+                h = c * CHUNK // C
+                bank = psum.tile([P, H], F32, name=f"bank{BANKS[q][c]}")
+                nc.tensor.matmul_mx(
+                    out=bank[:],
+                    lhsT=g_codes[q, c][0].bitcast(FP8X4),
+                    lhsT_scale=g_codes[q, c][1],
+                    rhs=w2_t[q][:, h, :].bitcast(FP4X4),
+                    rhs_scale=s2_t[:, 2 * q + h, :],
+                    start=True,
+                    stop=True,
+                )
+                if (q, c) == (0, 3):
+                    raw = planes[1][:, 1:3, 0:P]
+                elif q == 1:
+                    raw = planes[0][:, 2 + c % 2, h * C : (h + 1) * C].rearrange("s (u p) -> s u p", u=2)
+                elif (q, c) == (2, 0):
+                    raw = planes[0][:, 0:2, 0:P]
+                elif (q, c) == (3, 2):
+                    raw = dx[0][:, 0 : 2 * PIECE].rearrange("s (u p) -> s u p", u=2)[:, :, 0:P]
+                else:
+                    raw = keep.tile([P, 2, P], F32, name=f"raw{q}_{c}", align_bytes=64)[:]
+                nc.scalar.copy(
+                    raw.bitcast(BF16).rearrange("s u (p e) -> s u p e", e=2),
+                    bank[:].rearrange("s (p u e) -> s u p e", u=2, e=2),
+                )
+                if c % 2 == 0:
+                    turned[2 * q + h] = psum.tile([P, 2, C], F32, name=f"ring{h}")
+                for u in range(2):
+                    nc.tensor.transpose(
+                        turned[2 * q + h][:, u, (c % 2) * CHUNK : (c % 2 + 1) * CHUNK], raw[:, u, :], ident[:]
+                    )
 
-        def masked(q):
-            mask_product(q, 0)
-            mask_product(q, 1)
+        def mask_product(e):
+            cols = slice(e % 2 * C, (e % 2 + 1) * C)
+            nc.vector.tensor_tensor(
+                das[e // 2][:, cols, :].rearrange("p s (u e) -> p s u e", u=2),
+                turned[e][:].rearrange("p u s -> p (u s)").bitcast(BF16).rearrange("p (u s e) -> p s u e", u=2, e=2),
+                ones[e].rearrange("p u s e -> p s u e"),
+                MULT,
+            )
 
-        for q in range(PIECES - 1):
-            gathers(q)
-            if q == 2:
-                first_products(0)
-                mask_product(0, 0)
-                quantise_g(1, C, C)
-                mask_product(0, 1)
-            round_g(q, nc.scalar.copy, nc.scalar.copy)
-            for e in (2 * q, 2 * q + 1):
-                sign(e)
-                mask(e)
+        def quantise_da(q, first, width, name):
+            words = keep.tile([P, width], U32, name=name, align_bytes=64)
+            scales = keep.tile([P, width], U8, name=f"da_scales{q}_{first}", align_bytes=64)
+            for start in range(0, width, C):
+                da_codes[2 * q + (first + start) // C] = (words[:, start : start + C], scales[:, start : start + C])
+            nc.vector.quantize_mx(
+                out=words[:].bitcast(FP8X4),
+                scales=scales[:],
+                in_=das[q][:, first : first + width, :].rearrange("p s t -> p (s t)"),
+            )
+
+        def second_product(k, q, first, width, name, copy):
+            acc = psum.tile([P, PIECE], F32, name=name)
+            for start in range(first, first + width, C):
+                e = 2 * q + start // C
+                nc.tensor.matmul_mx(
+                    out=acc[:, start : start + C],
+                    lhsT=w1_t[:, e, k * 2 * P : (k + 1) * 2 * P].bitcast(FP4X4),
+                    lhsT_scale=s1_t[:, e, k * P : (k + 1) * P],
+                    rhs=da_codes[e][0].bitcast(FP8X4),
+                    rhs_scale=da_codes[e][1],
+                    start=True,
+                    stop=True,
+                )
+            copy(dx[k][:, q * PIECE + first : q * PIECE + first + width], acc[:, first : first + width])
+
+        for q in (0, 1, 3):
+            das[q] = keep.tile([P, PIECE, PACK], BF16, name=f"da{q}", align_bytes=64)[:]
+        das[2] = as_words(planes[0][:, 0:2, :])
+        grouped = [
+            keep.tile([P, PIECE, PACK], BF16, name="grouped0", align_bytes=64)[:],
+            as_words(pre[1][:]),
+            as_words(planes[1][:, 1:3, :]),
+            as_words(planes[0][:, 0:2, :]),
+        ]
+
+        gathers(0)
+        round_g(0, grouped[0])
+        quantise_g(0, grouped[0], 0, PIECE, "g_words0")
+        gathers(1)
+        pair_mask(0)
+        round_g(1, grouped[1])
+        quantise_g(1, grouped[1], 0, C, "g_words1")
+        gathers(2)
+        first_products(0)
+        mask_product(0)
+        quantise_g(1, grouped[1], C, C, "raw0_1")
+        mask_product(1)
+        pair_mask(1)
+        round_g(2, grouped[2])
+        quantise_g(2, grouped[2], 0, PIECE, "g_words2")
         first_products(1)
-        masked(1)
-        quantise_da(1, 0, PIECE)
+        mask_product(2)
+        mask_product(3)
+        pair_mask(2)
         first_products(2)
-        quantise_da(0, 0, PIECE)
+        quantise_da(0, 0, PIECE, "g_words2")
+        quantise_da(1, 0, PIECE, "da_words1")
         gathers(3)
-        round_g(3, nc.scalar.copy, nc.scalar.copy)
-        masked(2)
-        compare(6)
-        compare(7)
-        quantise_da(2, 0, PIECE)
+        round_g(3, grouped[3])
+        quantise_g(3, grouped[3], 0, C, "g_words3")
+        quantise_g(3, grouped[3], C, C, "g_words4")
+        mask_product(4)
+        mask_product(5)
+        compare_mask(6, "raw2_1")
+        quantise_da(2, 0, PIECE, "da_words2")
         first_products(3)
-        for q in range(2):
-            second_product(0, q, 0, PIECE)
-        mask_product(3, 0)
-        second_product(0, 2, 0, PIECE)
-        mask_product(3, 1)
-        quantise_da(3, 0, C)
-        quantise_da(3, C, C)
-        second_product(0, 3, 0, C)
-        second_product(0, 3, C, C)
+        compare_mask(7, "g_words3")
+        second_product(0, 0, 0, PIECE, "bank3", nc.scalar.copy)
+        second_product(0, 1, 0, PIECE, "bank2", nc.scalar.copy)
+        mask_product(6)
+        second_product(0, 2, 0, PIECE, "bank1", nc.scalar.copy)
+        mask_product(7)
+        quantise_da(3, 0, C, "raw3_3")
+        quantise_da(3, C, C, "da_words3")
+        second_product(0, 3, 0, C, "bank4", nc.vector.tensor_copy)
+        second_product(0, 3, C, C, "bank5", nc.vector.tensor_copy)
+        for q in range(PIECES):
+            second_product(1, q, 0, PIECE, f"bank{4 + q % 2}", nc.scalar.copy)
 
         for k in range(2):
             halves = []
@@ -319,11 +296,7 @@ def tile_moe_bdx_mlp_relu_kernel(
                 part1 = keep.tile([P, T // 2], F32, name=f"part1_{k}_{first}")
                 nc.vector.tensor_copy(part1[:], dx[k][:].indirect(pos1_t[:, first // 16 : (first + T // 2) // 16]))
                 halves.append(part1)
-            if k == 0:
-                dx.append(keep.tile([P, S], F32, name="dx1"))
-                for q in range(PIECES):
-                    second_product(1, q, 0, PIECE)
-            for first, width in ((0, 512), (512, 384), (896, 128)):
+            for first, width in SHARES[k]:
                 total = keep.tile([P, width], F32, name=f"total_{k}_{first}")
                 nc.vector.tensor_tensor(
                     total[:],

@@ -21,7 +21,6 @@ ADD = mybir.AluOpType.add
 MAX = mybir.AluOpType.max
 IS_GT = mybir.AluOpType.is_gt
 SIGN = mybir.ActivationFunctionType.Sign
-RELU = mybir.ActivationFunctionType.Relu
 
 FLOPS = 2 * S * (N * H + H * K)
 BYTES = 4 * N * T + 4 * H * S + E * (N * H + H * K) * 17 // 32 + 4 * S + 2 * S + 2 * 2 * T + 4 * K * T
@@ -29,8 +28,8 @@ BYTES = 4 * N * T + 4 * H * S + E * (N * H + H * K) * 17 // 32 + 4 * S + 2 * S +
 PIECE = 512
 PIECES = S // PIECE
 CHUNK = 128
-BANKS = ((0, 1, 2, 3), (3, 2, 4, 5), (0, 1, 3, 2), (4, 5, 0, 1))
-SHARES = (((0, 512), (512, 512)), ((0, 512), (512, 384), (896, 128)))
+SIGNED = 5
+SHARES = (((0, 512), (512, 512)), ((0, 640), (640, 256), (896, 128)))
 
 
 def tile_moe_bdx_mlp_relu_kernel(
@@ -55,6 +54,8 @@ def tile_moe_bdx_mlp_relu_kernel(
         s1_t = keep.tile([P, E, K], U8, name="s1_t", align_bytes=64)
         dx = [keep.tile([P, S], F32, name=f"dx{k}") for k in range(2)]
         planes = [keep.tile([P, PACK, PIECE], F32, name=f"planes{j}", align_bytes=64) for j in range(2)]
+        da = keep.tile([P, E, C * PACK], BF16, name="da", align_bytes=64)
+        signs = keep.tile([P, SIGNED, 2, C, 2], BF16, name="signs")
         ident = keep.tile([P, P], F32, name="ident")
 
         nc.gpsimd.memset(s2_t[:].rearrange("p e i -> p (e i)").bitcast(I32), 0)
@@ -95,31 +96,31 @@ def tile_moe_bdx_mlp_relu_kernel(
                 nc.sync.dma_start(gates[0][:, t * C : (t + 1) * C], gate[0:P, t * C : (t + 1) * C])
             nc.sync.dma_start(dy[t][:], dyT_rows[:, t, :])
         load_gate(1)
-        load_gate(2)
-        load_gate(3)
         load_pre(0)
         load_pre(1)
         load_pre(2)
+        load_gate(2)
         load_w2(0)
         load_scales(s2_t, w2_scales)
+        load_gate(3)
         load_pre(3)
         load_w2(1)
         load_pre(4)
-        load_w2(2)
-        nc.sync.dma_start(as_i32(w1_t[:]), w1_words.rearrange("e g p b -> p (e g) b").bitcast(I32))
-        load_scales(s1_t, w1_scales)
         load_pre(5)
+        load_w2(2)
         load_w2(3)
         load_pre(6)
         load_pre(7)
+        nc.sync.dma_start(as_i32(w1_t[:]), w1_words.rearrange("e g p b -> p (e g) b").bitcast(I32))
+        load_scales(s1_t, w1_scales)
         nc.sync.dma_start(pos1_t[:], pos1)
         nc.sync.dma_start(pos2_t[:], pos2)
 
         g_codes, ones, turned, das, da_codes = {}, {}, {}, {}, {}
 
-        def gathers(q):
-            for t in range(PACK):
-                width = C if (q, t) == (0, 0) else PIECE
+        def gathers(q, rows=range(PACK)):
+            for t in rows:
+                width = C if (q, t) in ((0, 0), (0, PACK - 1)) else PIECE
                 for first in range(0, PIECE, width):
                     nc.vector.tensor_tensor(
                         planes[q % 2][:, t, first : first + width],
@@ -128,12 +129,11 @@ def tile_moe_bdx_mlp_relu_kernel(
                         MULT,
                     )
 
-        def round_g(q, grouped):
-            for first in (0, C):
-                nc.scalar.copy(
-                    grouped[:, first : first + C, :].rearrange("p (c i) t -> p c t i", i=4),
-                    planes[q % 2][:, :, first : first + C].rearrange("p t (c i) -> p c t i", i=4),
-                )
+        def round_g(q, grouped, first):
+            nc.scalar.copy(
+                grouped[:, first : first + C, :].rearrange("p (c i) t -> p c t i", i=4),
+                planes[q % 2][:, :, first : first + C].rearrange("p t (c i) -> p c t i", i=4),
+            )
 
         def quantise_g(q, grouped, first, width, name):
             words = keep.tile([P, width], U32, name=name, align_bytes=64)
@@ -146,18 +146,20 @@ def tile_moe_bdx_mlp_relu_kernel(
                 in_=grouped[:, first : first + width, :].rearrange("p s t -> p (s t)"),
             )
 
-        def sign(e, signs):
-            nc.scalar.activation(signs, pre[e][:].rearrange("p (u e) s -> p u s e", u=2), SIGN)
+        def sign(e, halves=False):
+            rows = pre[e][:].rearrange("p (u e) s -> p u s e", u=2)
+            if halves:
+                for u in range(2):
+                    nc.scalar.activation(signs[:, e, u], rows[:, u], SIGN)
+            else:
+                nc.scalar.activation(signs[:, e], rows, SIGN)
 
-        def pair_mask(q):
-            signs = keep.tile([P, 2, 2, C, 2], BF16, name=f"signs{q}")
-            both = keep.tile([P, 2, 2, C, 2], BF16, name=f"ones{q}", align_bytes=64)
-            for h in range(2):
-                sign(2 * q + h, signs[:, h])
-                ones[2 * q + h] = both[:, h]
+        def clip_signs(first, count, into):
+            for h in range(count):
+                ones[first + h] = into[:, h, :].rearrange("p (u s e) -> p u s e", u=2, e=2)
             nc.vector.tensor_scalar(
-                both[:].rearrange("p h u s e -> p (h u s e)"),
-                signs[:].rearrange("p h u s e -> p (h u s e)"),
+                into.rearrange("p h x -> p (h x)"),
+                signs[:, first : first + count].rearrange("p h u s e -> p (h u s e)"),
                 0.0,
                 None,
                 MAX,
@@ -167,39 +169,34 @@ def tile_moe_bdx_mlp_relu_kernel(
             ones[e] = keep.tile([P, 2, C, 2], BF16, name=name, align_bytes=64)[:]
             nc.vector.tensor_scalar(ones[e], pre[e][:].rearrange("p (u e) s -> p u s e", u=2), 0.0, None, IS_GT)
 
-        def first_products(q):
-            for c in range(PIECE // CHUNK):
-                h = c * CHUNK // C
-                bank = psum.tile([P, H], F32, name=f"bank{BANKS[q][c]}")
+        def first_products(e):
+            q, h = divmod(e, 2)
+            turned[e] = psum.tile([P, 2, C], F32, name=f"bank{4 + e % 4}")
+            for half in range(2):
+                c = 2 * h + half
+                bank = psum.tile([P, H], F32, name=f"bank{c}")
                 nc.tensor.matmul_mx(
                     out=bank[:],
                     lhsT=g_codes[q, c][0].bitcast(FP8X4),
                     lhsT_scale=g_codes[q, c][1],
                     rhs=w2_t[q][:, h, :].bitcast(FP4X4),
-                    rhs_scale=s2_t[:, 2 * q + h, :],
+                    rhs_scale=s2_t[:, e, :],
                     start=True,
                     stop=True,
                 )
                 if (q, c) == (0, 3):
-                    raw = planes[1][:, 1:3, 0:P]
-                elif q == 1:
-                    raw = planes[0][:, 2 + c % 2, h * C : (h + 1) * C].rearrange("s (u p) -> s u p", u=2)
-                elif (q, c) == (2, 0):
-                    raw = planes[0][:, 0:2, 0:P]
-                elif (q, c) == (3, 2):
-                    raw = dx[0][:, 0 : 2 * PIECE].rearrange("s (u p) -> s u p", u=2)[:, :, 0:P]
+                    seams = planes[1][:].rearrange("p t s -> p (t s)")[:, 2 * PIECE - P // 2 : 4 * PIECE - P // 2]
+                    raw = seams.rearrange("p (u s) -> p u s", u=2)[:, :, 0:P]
+                elif (q, c) == (1, 3):
+                    raw = da[:, 1:7:5, 0 : 2 * P].bitcast(F32)
                 else:
                     raw = keep.tile([P, 2, P], F32, name=f"raw{q}_{c}", align_bytes=64)[:]
                 nc.scalar.copy(
                     raw.bitcast(BF16).rearrange("s u (p e) -> s u p e", e=2),
                     bank[:].rearrange("s (p u e) -> s u p e", u=2, e=2),
                 )
-                if c % 2 == 0:
-                    turned[2 * q + h] = psum.tile([P, 2, C], F32, name=f"ring{h}")
                 for u in range(2):
-                    nc.tensor.transpose(
-                        turned[2 * q + h][:, u, (c % 2) * CHUNK : (c % 2 + 1) * CHUNK], raw[:, u, :], ident[:]
-                    )
+                    nc.tensor.transpose(turned[e][:, u, half * CHUNK : (half + 1) * CHUNK], raw[:, u, :], ident[:])
 
         def mask_product(e):
             cols = slice(e % 2 * C, (e % 2 + 1) * C)
@@ -221,8 +218,8 @@ def tile_moe_bdx_mlp_relu_kernel(
                 in_=das[q][:, first : first + width, :].rearrange("p s t -> p (s t)"),
             )
 
-        def second_product(k, q, first, width, name, copy):
-            acc = psum.tile([P, PIECE], F32, name=name)
+        def second_product(k, q, first, width, bank, copy):
+            acc = psum.tile([P, PIECE], F32, name=f"bank{bank}")
             for start in range(first, first + width, C):
                 e = 2 * q + start // C
                 nc.tensor.matmul_mx(
@@ -236,72 +233,81 @@ def tile_moe_bdx_mlp_relu_kernel(
                 )
             copy(dx[k][:, q * PIECE + first : q * PIECE + first + width], acc[:, first : first + width])
 
-        for q in (0, 1, 3):
-            das[q] = keep.tile([P, PIECE, PACK], BF16, name=f"da{q}", align_bytes=64)[:]
-        das[2] = as_words(planes[0][:, 0:2, :])
-        grouped = [
-            keep.tile([P, PIECE, PACK], BF16, name="grouped0", align_bytes=64)[:],
-            as_words(pre[1][:]),
-            as_words(planes[1][:, 1:3, :]),
-            as_words(planes[0][:, 0:2, :]),
-        ]
+        for q in range(PIECES):
+            das[q] = da[:, 2 * q : 2 * q + 2, :].rearrange("p h (s t) -> p (h s) t", t=PACK)
 
         gathers(0)
-        round_g(0, grouped[0])
-        quantise_g(0, grouped[0], 0, PIECE, "g_words0")
+        grouped = keep.tile([P, PIECE, PACK], BF16, name="grouped0", align_bytes=64)[:]
+        round_g(0, grouped, 0)
+        round_g(0, grouped, C)
         gathers(1)
-        pair_mask(0)
-        round_g(1, grouped[1])
-        quantise_g(1, grouped[1], 0, C, "g_words1")
+        quantise_g(0, grouped, 0, PIECE, "g_words0")
+        sign(0)
+        sign(1)
+        sign(2, halves=True)
         gathers(2)
+        clip_signs(0, 2, keep.tile([P, 2, C * PACK], BF16, name="ones0")[:])
+        grouped = as_words(pre[2][:])
+        round_g(1, grouped, 0)
+        round_g(1, grouped, C)
         first_products(0)
-        mask_product(0)
-        quantise_g(1, grouped[1], C, C, "raw0_1")
-        mask_product(1)
-        pair_mask(1)
-        round_g(2, grouped[2])
-        quantise_g(2, grouped[2], 0, PIECE, "g_words2")
         first_products(1)
-        mask_product(2)
-        mask_product(3)
-        pair_mask(2)
+        gathers(3, (0,))
+        mask_product(0)
+        quantise_g(1, grouped, 0, PIECE, "raw0_2")
+        gathers(3, (1, 2, 3))
+        sign(3)
+        grouped = keep.tile([P, PIECE, PACK], BF16, name="raw0_1", align_bytes=64)[:]
+        round_g(2, grouped, 0)
+        round_g(2, grouped, C)
         first_products(2)
-        quantise_da(0, 0, PIECE, "g_words2")
-        quantise_da(1, 0, PIECE, "da_words1")
-        gathers(3)
-        round_g(3, grouped[3])
-        quantise_g(3, grouped[3], 0, C, "g_words3")
-        quantise_g(3, grouped[3], C, C, "g_words4")
-        mask_product(4)
-        mask_product(5)
-        compare_mask(6, "raw2_1")
-        quantise_da(2, 0, PIECE, "da_words2")
         first_products(3)
-        compare_mask(7, "g_words3")
-        second_product(0, 0, 0, PIECE, "bank3", nc.scalar.copy)
-        second_product(0, 1, 0, PIECE, "bank2", nc.scalar.copy)
+        quantise_g(2, grouped, 0, PIECE, "raw1_2")
+        sign(4, halves=True)
+        grouped = as_words(pre[4][:])
+        round_g(3, grouped, 0)
+        mask_product(1)
+        clip_signs(2, 2, da[:, 6:8, :])
+        quantise_da(0, 0, PIECE, "da_words0")
+        mask_product(2)
+        quantise_g(3, grouped, 0, C, "g_words3")
+        mask_product(3)
+        clip_signs(4, 1, keep.tile([P, 1, C * PACK], BF16, name="ones4")[:])
+        quantise_da(1, 0, PIECE, "da_words1")
+        first_products(4)
+        round_g(3, grouped, C)
+        quantise_g(3, grouped, C, C, "g_words4")
+        compare_mask(5, "raw2_0")
+        mask_product(4)
+        compare_mask(6, "raw2_1")
+        first_products(5)
+        mask_product(5)
+        compare_mask(7, "raw2_3")
+        first_products(6)
         mask_product(6)
-        second_product(0, 2, 0, PIECE, "bank1", nc.scalar.copy)
+        quantise_da(2, 0, PIECE, "raw3_1")
+        first_products(7)
         mask_product(7)
         quantise_da(3, 0, C, "raw3_3")
         quantise_da(3, C, C, "da_words3")
-        second_product(0, 3, 0, C, "bank4", nc.vector.tensor_copy)
-        second_product(0, 3, C, C, "bank5", nc.vector.tensor_copy)
+        for q, bank in enumerate((3, 6, 0)):
+            second_product(0, q, 0, PIECE, bank, nc.scalar.copy)
+        second_product(0, 3, 0, C, 1, nc.vector.tensor_copy)
+        second_product(0, 3, C, C, 2, nc.vector.tensor_copy)
         for q in range(PIECES):
-            second_product(1, q, 0, PIECE, f"bank{4 + q % 2}", nc.scalar.copy)
+            second_product(1, q, 0, PIECE, 1 + q % 2, nc.scalar.copy)
 
         for k in range(2):
-            halves = []
-            for first in range(0, T, T // 2):
-                part1 = keep.tile([P, T // 2], F32, name=f"part1_{k}_{first}")
-                nc.vector.tensor_copy(part1[:], dx[k][:].indirect(pos1_t[:, first // 16 : (first + T // 2) // 16]))
-                halves.append(part1)
+            part = keep.tile([P, T], F32, name=f"part{k}")
+            cut = SHARES[k][0][1]
+            for first, last in ((0, cut), (cut, T)):
+                nc.vector.tensor_copy(part[:, first:last], dx[k][:].indirect(pos1_t[:, first // 16 : last // 16]))
             for first, width in SHARES[k]:
                 total = keep.tile([P, width], F32, name=f"total_{k}_{first}")
                 nc.vector.tensor_tensor(
                     total[:],
                     dx[k][:].indirect(pos2_t[:, first // 16 : (first + width) // 16]),
-                    halves[first // 512][:, first % 512 : first % 512 + width],
+                    part[:, first : first + width],
                     ADD,
                 )
                 nc.sync.dma_start(out[k * P : (k + 1) * P, first : first + width], total[:])

@@ -28,7 +28,7 @@ BYTES = 4 * N * T + 4 * H * S + E * (N * H + H * K) * 17 // 32 + 4 * S + 2 * S +
 PIECE = 512
 PIECES = S // PIECE
 CHUNK = 128
-SIGNED = 5
+SIGNED = 7
 SHARES = (((0, 512), (512, 512)), ((0, 640), (640, 256), (896, 128)))
 
 
@@ -104,12 +104,12 @@ def tile_moe_bdx_mlp_relu_kernel(
         load_scales(s2_t, w2_scales)
         load_gate(3)
         load_pre(3)
-        load_w2(1)
         load_pre(4)
         load_pre(5)
+        load_w2(1)
+        load_pre(6)
         load_w2(2)
         load_w2(3)
-        load_pre(6)
         load_pre(7)
         nc.sync.dma_start(as_i32(w1_t[:]), w1_words.rearrange("e g p b -> p (e g) b").bitcast(I32))
         load_scales(s1_t, w1_scales)
@@ -257,14 +257,16 @@ def tile_moe_bdx_mlp_relu_kernel(
         quantise_g(1, grouped, 0, PIECE, "raw0_2")
         gathers(3, (1, 2, 3))
         sign(3)
-        grouped = keep.tile([P, PIECE, PACK], BF16, name="raw0_1", align_bytes=64)[:]
+        sign(4, halves=True)
+        grouped = as_words(pre[4][:])
         round_g(2, grouped, 0)
         round_g(2, grouped, C)
+        sign(5)
         first_products(2)
         first_products(3)
         quantise_g(2, grouped, 0, PIECE, "raw1_2")
-        sign(4, halves=True)
-        grouped = as_words(pre[4][:])
+        sign(6, halves=True)
+        grouped = as_words(pre[6][:])
         round_g(3, grouped, 0)
         mask_product(1)
         clip_signs(2, 2, da[:, 6:8, :])
@@ -272,14 +274,13 @@ def tile_moe_bdx_mlp_relu_kernel(
         mask_product(2)
         quantise_g(3, grouped, 0, C, "g_words3")
         mask_product(3)
-        clip_signs(4, 1, keep.tile([P, 1, C * PACK], BF16, name="ones4")[:])
+        clip_signs(4, 2, keep.tile([P, 2, C * PACK], BF16, name="ones4")[:])
         quantise_da(1, 0, PIECE, "da_words1")
         first_products(4)
         round_g(3, grouped, C)
         quantise_g(3, grouped, C, C, "g_words4")
-        compare_mask(5, "raw2_0")
         mask_product(4)
-        compare_mask(6, "raw2_1")
+        clip_signs(6, 1, keep.tile([P, 1, C * PACK], BF16, name="raw2_1", align_bytes=64)[:])
         first_products(5)
         mask_product(5)
         compare_mask(7, "raw2_3")

@@ -58,9 +58,9 @@ def tile_moe_bdx_mlp_relu_kernel(
         signs = keep.tile([P, SIGNED, 2, C, 2], BF16, name="signs")
         ident = keep.tile([P, P], F32, name="ident")
 
+        make_identity(nc, ident[:])
         nc.gpsimd.memset(s2_t[:].rearrange("p e i -> p (e i)").bitcast(I32), 0)
         nc.gpsimd.memset(s1_t[:].rearrange("p e i -> p (e i)").bitcast(I32), 0)
-        make_identity(nc, ident[:])
 
         dyT_rows = dyT.rearrange("(p t) n -> p t n", t=PACK)
         a_rows = a.rearrange("(p t) s -> p t s", t=PACK)
@@ -131,8 +131,8 @@ def tile_moe_bdx_mlp_relu_kernel(
 
         def round_g(q, grouped, first):
             nc.scalar.copy(
-                grouped[:, first : first + C, :].rearrange("p (c i) t -> p c t i", i=4),
-                planes[q % 2][:, :, first : first + C].rearrange("p t (c i) -> p c t i", i=4),
+                grouped[:, first : first + C, :].rearrange("p (c i) (u e) -> p c u i e", i=4, u=2),
+                planes[q % 2][:, :, first : first + C].rearrange("p (u e) (c i) -> p c u i e", i=4, u=2),
             )
 
         def quantise_g(q, grouped, first, width, name):

@@ -28,7 +28,7 @@ BYTES = 4 * N * T + 4 * H * S + E * (N * H + H * K) * 17 // 32 + 4 * S + 2 * S +
 PIECE = 512
 PIECES = S // PIECE
 CHUNK = 128
-SIGNED = 7
+SIGNED = 6
 SHARES = (((0, 512), (512, 512)), ((0, 640), (640, 256), (896, 128)))
 
 
@@ -105,11 +105,11 @@ def tile_moe_bdx_mlp_relu_kernel(
         load_gate(3)
         load_pre(3)
         load_pre(4)
-        load_pre(5)
         load_w2(1)
-        load_pre(6)
+        load_pre(5)
         load_w2(2)
         load_w2(3)
+        load_pre(6)
         load_pre(7)
         nc.sync.dma_start(as_i32(w1_t[:]), w1_words.rearrange("e g p b -> p (e g) b").bitcast(I32))
         load_scales(s1_t, w1_scales)
@@ -261,12 +261,11 @@ def tile_moe_bdx_mlp_relu_kernel(
         grouped = as_words(pre[4][:])
         round_g(2, grouped, 0)
         round_g(2, grouped, C)
-        sign(5)
         first_products(2)
         first_products(3)
         quantise_g(2, grouped, 0, PIECE, "raw1_2")
-        sign(6, halves=True)
-        grouped = as_words(pre[6][:])
+        sign(5, halves=True)
+        grouped = as_words(pre[5][:])
         round_g(3, grouped, 0)
         mask_product(1)
         clip_signs(2, 2, da[:, 6:8, :])
@@ -280,7 +279,7 @@ def tile_moe_bdx_mlp_relu_kernel(
         round_g(3, grouped, C)
         quantise_g(3, grouped, C, C, "g_words4")
         mask_product(4)
-        clip_signs(6, 1, keep.tile([P, 1, C * PACK], BF16, name="raw2_1", align_bytes=64)[:])
+        compare_mask(6, "raw2_1")
         first_products(5)
         mask_product(5)
         compare_mask(7, "raw2_3")

@@ -1,7 +1,6 @@
 from contextlib import ExitStack
 
 import concourse.mybir as mybir
-from concourse.masks import make_identity
 
 K, T, E, C, H, N = 256, 1024, 8, 256, 512, 512
 S = E * C
@@ -18,9 +17,8 @@ FP8X4 = mybir.dt.float8_e4m3fn_x4
 FP4X4 = mybir.dt.float4_e2m1fn_x4
 MULT = mybir.AluOpType.mult
 ADD = mybir.AluOpType.add
-MAX = mybir.AluOpType.max
 IS_GT = mybir.AluOpType.is_gt
-SIGN = mybir.ActivationFunctionType.Sign
+COPY = mybir.ActivationFunctionType.Copy
 
 FLOPS = 2 * S * (N * H + H * K)
 BYTES = 4 * N * T + 4 * H * S + E * (N * H + H * K) * 17 // 32 + 4 * S + 2 * S + 2 * 2 * T + 4 * K * T
@@ -28,8 +26,7 @@ BYTES = 4 * N * T + 4 * H * S + E * (N * H + H * K) * 17 // 32 + 4 * S + 2 * S +
 PIECE = 512
 PIECES = S // PIECE
 CHUNK = 128
-SIGNED = 6
-SHARES = (((0, 512), (512, 512)), ((0, 640), (640, 256), (896, 128)))
+SHARE = 256
 
 
 def tile_moe_bdx_mlp_relu_kernel(
@@ -48,17 +45,17 @@ def tile_moe_bdx_mlp_relu_kernel(
         dy = [keep.tile([P, T], F32, name=f"dy{t}") for t in range(PACK)]
         gates = [keep.tile([P, PIECE], F32, name=f"gates{q}") for q in range(PIECES)]
         pre = [keep.tile([P, PACK, C], F32, name=f"pre{e}", align_bytes=64) for e in range(E)]
-        w2_t = [keep.tile([P, 2, 2 * H], U8, name=f"w2_t{q}", align_bytes=64) for q in range(PIECES)]
+        w2_raw = [keep.tile([P, 2, 2 * H], U8, name=f"w2_raw{q}") for q in range(PIECES)]
+        w2_t = [keep.tile([P, 2 * H], U8, name=f"w2_t{e}", align_bytes=64) for e in range(E)]
+        s2_raw = keep.tile([P, H], U8, name="s2_raw")
+        s2_mid = keep.tile([P, H], U8, name="s2_mid")
         s2_t = keep.tile([P, E, H], U8, name="s2_t", align_bytes=64)
         w1_t = keep.tile([P, E, 2 * K], U8, name="w1_t", align_bytes=64)
         s1_t = keep.tile([P, E, K], U8, name="s1_t", align_bytes=64)
         dx = [keep.tile([P, S], F32, name=f"dx{k}") for k in range(2)]
         planes = [keep.tile([P, PACK, PIECE], F32, name=f"planes{j}", align_bytes=64) for j in range(2)]
-        da = keep.tile([P, E, C * PACK], BF16, name="da", align_bytes=64)
-        signs = keep.tile([P, SIGNED, 2, C, 2], BF16, name="signs")
-        ident = keep.tile([P, P], F32, name="ident")
+        da = [keep.tile([P, PIECE, PACK], BF16, name=f"da{q}", align_bytes=64) for q in range(PIECES)]
 
-        make_identity(nc, ident[:])
         nc.gpsimd.memset(s2_t[:].rearrange("p e i -> p (e i)").bitcast(I32), 0)
         nc.gpsimd.memset(s1_t[:].rearrange("p e i -> p (e i)").bitcast(I32), 0)
 
@@ -80,142 +77,117 @@ def tile_moe_bdx_mlp_relu_kernel(
 
         def load_w2(q):
             nc.sync.dma_start(
-                as_i32(w2_t[q][:]), w2_words[2 * q : 2 * q + 2].rearrange("e g p b -> p (e g) b").bitcast(I32)
+                as_i32(w2_raw[q][:]), w2_words[2 * q : 2 * q + 2].rearrange("e g p b -> p (e g) b").bitcast(I32)
             )
 
-        def load_scales(plane, scales):
-            for r in range(4):
-                nc.sync.dma_start(
-                    as_i32(plane[r:P:32]),
-                    scales[:, :, r:16:4, :].rearrange("e g f k -> f (e g) k").bitcast(I32),
-                )
-
         nc.sync.dma_start(offs_t[:], offs)
-        for t in range(PACK):
-            if t < 2:
-                nc.sync.dma_start(gates[0][:, t * C : (t + 1) * C], gate[0:P, t * C : (t + 1) * C])
-            nc.sync.dma_start(dy[t][:], dyT_rows[:, t, :])
+        nc.sync.dma_start(dy[0][:], dyT_rows[:, 0, :])
         load_gate(1)
+        nc.sync.dma_start(s2_raw[:].bitcast(I32), w2_scales.rearrange("e g f i -> f (e g) i").bitcast(I32))
+        for t in range(1, PACK):
+            nc.sync.dma_start(dy[t][:], dyT_rows[:, t, :])
+        load_gate(0)
+        load_w2(0)
+        load_w2(1)
         load_pre(0)
         load_pre(1)
         load_pre(2)
-        load_gate(2)
-        load_w2(0)
-        load_scales(s2_t, w2_scales)
-        load_gate(3)
         load_pre(3)
-        load_pre(4)
-        load_w2(1)
-        load_pre(5)
+        load_gate(2)
         load_w2(2)
+        nc.sync.dma_start(as_i32(w1_t[:]), w1_words.rearrange("e g p b -> p (e g) b").bitcast(I32))
+        for r in range(4):
+            nc.sync.dma_start(
+                as_i32(s1_t[r:P:32]), w1_scales[:, :, r:16:4, :].rearrange("e g f k -> f (e g) k").bitcast(I32)
+            )
+        load_pre(4)
+        load_gate(3)
+        load_pre(5)
         load_w2(3)
         load_pre(6)
         load_pre(7)
-        nc.sync.dma_start(as_i32(w1_t[:]), w1_words.rearrange("e g p b -> p (e g) b").bitcast(I32))
-        load_scales(s1_t, w1_scales)
         nc.sync.dma_start(pos1_t[:], pos1)
         nc.sync.dma_start(pos2_t[:], pos2)
 
-        g_codes, ones, turned, das, da_codes = {}, {}, {}, {}, {}
+        g_codes, da_codes, grouped = {}, {}, {}
 
-        def gathers(q, rows=range(PACK)):
-            for t in rows:
-                width = C if (q, t) in ((0, 0), (0, PACK - 1)) else PIECE
-                for first in range(0, PIECE, width):
-                    nc.vector.tensor_tensor(
-                        planes[q % 2][:, t, first : first + width],
-                        dy[t][:].indirect(offs_t[:, (q * PIECE + first) // 16 : (q * PIECE + first + width) // 16]),
-                        gates[q][:, first : first + width],
-                        MULT,
-                    )
+        def window(q, t):
+            return dy[t][:].indirect(offs_t[:, q * PIECE // 16 : (q + 1) * PIECE // 16])
 
-        def round_g(q, grouped, first):
+        def plain_gathers(q):
+            for t in range(PACK):
+                nc.scalar.activation(planes[q % 2][:, t, :], window(q, t), COPY)
+
+        def gated_gather(q, t):
+            nc.vector.tensor_tensor(planes[q % 2][:, t, :], window(q, t), gates[q][:], MULT)
+
+        def turn_scales():
+            nc.vector.tensor_copy(
+                s2_mid[:].rearrange("p (t m) -> p t m", t=PACK), s2_raw[:].rearrange("p (m t) -> p t m", t=PACK)
+            )
+            for quad in range(4):
+                nc.scalar.dma_start(as_i32(s2_t[32 * quad : 32 * quad + 4]), s2_mid[32 * quad : 32 * quad + 32].bitcast(I32))
+
+        def turn_words(e):
             nc.scalar.copy(
-                grouped[:, first : first + C, :].rearrange("p (c i) (u e) -> p c u i e", i=4, u=2),
+                w2_t[e][:].bitcast(U16).rearrange("p (t m) -> p t m", t=PACK),
+                w2_raw[e // 2][:, e % 2, :].bitcast(U16).rearrange("p (m t) -> p t m", t=PACK),
+            )
+
+        def round_g(e):
+            q, first = e // 2, e % 2 * C
+            nc.scalar.copy(
+                grouped[q][:, first : first + C, :].rearrange("p (c i) (u e) -> p c u i e", i=4, u=2),
                 planes[q % 2][:, :, first : first + C].rearrange("p (u e) (c i) -> p c u i e", i=4, u=2),
             )
 
-        def quantise_g(q, grouped, first, width, name):
-            words = keep.tile([P, width], U32, name=name, align_bytes=64)
-            scales = keep.tile([P, width], U8, name=f"g_scales{q}_{first}", align_bytes=64)
-            for start in range(0, width, CHUNK):
-                g_codes[q, (first + start) // CHUNK] = (words[:, start : start + CHUNK], scales[:, start : start + CHUNK])
-            nc.vector.quantize_mx(
-                out=words[:].bitcast(FP8X4),
-                scales=scales[:],
-                in_=grouped[:, first : first + width, :].rearrange("p s t -> p (s t)"),
-            )
-
-        def sign(e, halves=False):
-            rows = pre[e][:].rearrange("p (u e) s -> p u s e", u=2)
-            if halves:
-                for u in range(2):
-                    nc.scalar.activation(signs[:, e, u], rows[:, u], SIGN)
-            else:
-                nc.scalar.activation(signs[:, e], rows, SIGN)
-
-        def clip_signs(first, count, into):
-            for h in range(count):
-                ones[first + h] = into[:, h, :].rearrange("p (u s e) -> p u s e", u=2, e=2)
-            nc.vector.tensor_scalar(
-                into.rearrange("p h x -> p (h x)"),
-                signs[:, first : first + count].rearrange("p h u s e -> p (h u s e)"),
-                0.0,
-                None,
-                MAX,
-            )
-
-        def compare_mask(e, name):
-            ones[e] = keep.tile([P, 2, C, 2], BF16, name=name, align_bytes=64)[:]
-            nc.vector.tensor_scalar(ones[e], pre[e][:].rearrange("p (u e) s -> p u s e", u=2), 0.0, None, IS_GT)
-
-        def first_products(e):
-            q, h = divmod(e, 2)
-            turned[e] = psum.tile([P, 2, C], F32, name=f"bank{4 + e % 4}")
-            for half in range(2):
-                c = 2 * h + half
-                bank = psum.tile([P, H], F32, name=f"bank{c}")
-                nc.tensor.matmul_mx(
-                    out=bank[:],
-                    lhsT=g_codes[q, c][0].bitcast(FP8X4),
-                    lhsT_scale=g_codes[q, c][1],
-                    rhs=w2_t[q][:, h, :].bitcast(FP4X4),
-                    rhs_scale=s2_t[:, e, :],
-                    start=True,
-                    stop=True,
-                )
-                if (q, c) == (0, 3):
-                    seams = planes[1][:].rearrange("p t s -> p (t s)")[:, 2 * PIECE - P // 2 : 4 * PIECE - P // 2]
-                    raw = seams.rearrange("p (u s) -> p u s", u=2)[:, :, 0:P]
-                elif (q, c) == (1, 3):
-                    raw = da[:, 1:7:5, 0 : 2 * P].bitcast(F32)
-                else:
-                    raw = keep.tile([P, 2, P], F32, name=f"raw{q}_{c}", align_bytes=64)[:]
-                nc.scalar.copy(
-                    raw.bitcast(BF16).rearrange("s u (p e) -> s u p e", e=2),
-                    bank[:].rearrange("s (p u e) -> s u p e", u=2, e=2),
-                )
-                for u in range(2):
-                    nc.tensor.transpose(turned[e][:, u, half * CHUNK : (half + 1) * CHUNK], raw[:, u, :], ident[:])
-
-        def mask_product(e):
-            cols = slice(e % 2 * C, (e % 2 + 1) * C)
+        def gate_g(e):
+            q, first = e // 2, e % 2 * C
             nc.vector.tensor_tensor(
-                das[e // 2][:, cols, :].rearrange("p s (u e) -> p s u e", u=2),
-                turned[e][:].rearrange("p u s -> p (u s)").bitcast(BF16).rearrange("p (u s e) -> p s u e", u=2, e=2),
-                ones[e].rearrange("p u s e -> p s u e"),
+                grouped[q][:, first : first + C, :].rearrange("p (c i) t -> p c t i", i=2),
+                planes[q % 2][:, :, first : first + C].rearrange("p t (c i) -> p c t i", i=2),
+                gates[q][:, first : first + C].rearrange("p (c i) -> p c i", i=2).unsqueeze(2).to_broadcast([P, C // 2, PACK, 2]),
                 MULT,
             )
 
-        def quantise_da(q, first, width, name):
-            words = keep.tile([P, width], U32, name=name, align_bytes=64)
-            scales = keep.tile([P, width], U8, name=f"da_scales{q}_{first}", align_bytes=64)
+        def quantise(source, codes, label, q, first, width):
+            words = keep.tile([P, width], U32, name=f"{label}_words{q}_{first}", align_bytes=64)
+            scales = keep.tile([P, width], U8, name=f"{label}_scales{q}_{first}", align_bytes=64)
             for start in range(0, width, C):
-                da_codes[2 * q + (first + start) // C] = (words[:, start : start + C], scales[:, start : start + C])
+                codes[2 * q + (first + start) // C] = (words[:, start : start + C], scales[:, start : start + C])
             nc.vector.quantize_mx(
                 out=words[:].bitcast(FP8X4),
                 scales=scales[:],
-                in_=das[q][:, first : first + width, :].rearrange("p s t -> p (s t)"),
+                in_=source[q][:, first : first + width, :].rearrange("p s t -> p (s t)"),
+            )
+
+        def quantise_g(q, first=0, width=PIECE):
+            quantise(grouped, g_codes, "g", q, first, width)
+
+        def quantise_da(q, first=0, width=PIECE):
+            quantise(da, da_codes, "da", q, first, width)
+
+        def make_da(e, half):
+            bank = psum.tile([P, PACK, CHUNK], F32, name=f"bank{(2 * e + half) % 4}")
+            cols = slice(half * CHUNK, (half + 1) * CHUNK)
+            for t in range(PACK):
+                nc.tensor.matmul_mx(
+                    out=bank[:, t, :],
+                    lhsT=w2_t[e][:, t * 2 * P : (t + 1) * 2 * P].bitcast(FP4X4),
+                    lhsT_scale=s2_t[:, e, t * P : (t + 1) * P],
+                    rhs=g_codes[e][0][:, cols].bitcast(FP8X4),
+                    rhs_scale=g_codes[e][1][:, cols],
+                    start=True,
+                    stop=True,
+                )
+            first = e % 2 * C + half * CHUNK
+            nc.vector.scalar_tensor_tensor(
+                da[e // 2][:, first : first + CHUNK, :],
+                pre[e][:, :, cols].rearrange("p t s -> p s t"),
+                0.0,
+                bank[:].rearrange("p t s -> p s t"),
+                IS_GT,
+                MULT,
             )
 
         def second_product(k, q, first, width, bank, copy):
@@ -233,81 +205,77 @@ def tile_moe_bdx_mlp_relu_kernel(
                 )
             copy(dx[k][:, q * PIECE + first : q * PIECE + first + width], acc[:, first : first + width])
 
-        for q in range(PIECES):
-            das[q] = da[:, 2 * q : 2 * q + 2, :].rearrange("p h (s t) -> p (h s) t", t=PACK)
+        def second_products(q):
+            for k in range(2):
+                second_product(k, q, 0, PIECE, 4 + 2 * (q % 2) + k, nc.scalar.copy)
 
-        gathers(0)
-        grouped = keep.tile([P, PIECE, PACK], BF16, name="grouped0", align_bytes=64)[:]
-        round_g(0, grouped, 0)
-        round_g(0, grouped, C)
-        gathers(1)
-        quantise_g(0, grouped, 0, PIECE, "g_words0")
-        sign(0)
-        sign(1)
-        sign(2, halves=True)
-        gathers(2)
-        clip_signs(0, 2, keep.tile([P, 2, C * PACK], BF16, name="ones0")[:])
-        grouped = as_words(pre[2][:])
-        round_g(1, grouped, 0)
-        round_g(1, grouped, C)
-        first_products(0)
-        first_products(1)
-        gathers(3, (0,))
-        mask_product(0)
-        quantise_g(1, grouped, 0, PIECE, "raw0_2")
-        gathers(3, (1, 2, 3))
-        sign(3)
-        sign(4, halves=True)
-        grouped = as_words(pre[4][:])
-        round_g(2, grouped, 0)
-        round_g(2, grouped, C)
-        first_products(2)
-        first_products(3)
-        quantise_g(2, grouped, 0, PIECE, "raw1_2")
-        sign(5, halves=True)
-        grouped = as_words(pre[5][:])
-        round_g(3, grouped, 0)
-        mask_product(1)
-        clip_signs(2, 2, da[:, 6:8, :])
-        quantise_da(0, 0, PIECE, "da_words0")
-        mask_product(2)
-        quantise_g(3, grouped, 0, C, "g_words3")
-        mask_product(3)
-        clip_signs(4, 2, keep.tile([P, 2, C * PACK], BF16, name="ones4")[:])
-        quantise_da(1, 0, PIECE, "da_words1")
-        first_products(4)
-        round_g(3, grouped, C)
-        quantise_g(3, grouped, C, C, "g_words4")
-        mask_product(4)
-        compare_mask(6, "raw2_1")
-        first_products(5)
-        mask_product(5)
-        compare_mask(7, "raw2_3")
-        first_products(6)
-        mask_product(6)
-        quantise_da(2, 0, PIECE, "raw3_1")
-        first_products(7)
-        mask_product(7)
-        quantise_da(3, 0, C, "raw3_3")
-        quantise_da(3, C, C, "da_words3")
-        for q, bank in enumerate((3, 6, 0)):
-            second_product(0, q, 0, PIECE, bank, nc.scalar.copy)
-        second_product(0, 3, 0, C, 1, nc.vector.tensor_copy)
-        second_product(0, 3, C, C, 2, nc.vector.tensor_copy)
-        for q in range(PIECES):
-            second_product(1, q, 0, PIECE, 1 + q % 2, nc.scalar.copy)
+        for q in range(2):
+            grouped[q] = keep.tile([P, PIECE, PACK], BF16, name=f"grouped{q}", align_bytes=64)[:]
+        grouped[2] = as_words(pre[2][:])
+        grouped[3] = as_words(pre[3][:])
+
+        plain_gathers(0)
+        gated_gather(1, 0)
+        turn_scales()
+        for t in range(1, PACK):
+            gated_gather(1, t)
+        turn_words(0)
+        turn_words(1)
+        gate_g(0)
+        gate_g(1)
+        round_g(2)
+        round_g(3)
+        quantise_g(0, 0, C)
+        quantise_g(0, C, C)
+        turn_words(2)
+        turn_words(3)
+        plain_gathers(2)
+        make_da(0, 0)
+        quantise_g(1)
+        make_da(0, 1)
+        make_da(1, 0)
+        make_da(1, 1)
+        make_da(2, 0)
+        quantise_da(0)
+        make_da(2, 1)
+        make_da(3, 0)
+        make_da(3, 1)
+        turn_words(4)
+        turn_words(5)
+        plain_gathers(3)
+        gate_g(4)
+        gate_g(5)
+        quantise_da(1)
+        quantise_g(2)
+        second_products(0)
+        turn_words(6)
+        turn_words(7)
+        gate_g(6)
+        make_da(4, 0)
+        make_da(4, 1)
+        gate_g(7)
+        make_da(5, 0)
+        quantise_g(3)
+        make_da(5, 1)
+        second_products(1)
+        make_da(6, 0)
+        quantise_da(2)
+        make_da(6, 1)
+        make_da(7, 0)
+        quantise_da(3, 0, C)
+        make_da(7, 1)
+        second_products(2)
+        quantise_da(3, C, C)
+        second_product(0, 3, 0, C, 6, nc.scalar.copy)
+        second_product(1, 3, 0, C, 7, nc.scalar.copy)
+        second_product(0, 3, C, C, 0, nc.scalar.copy)
+        second_product(1, 3, C, C, 1, nc.vector.tensor_copy)
 
         for k in range(2):
-            part = keep.tile([P, T], F32, name=f"part{k}")
-            cut = SHARES[k][0][1]
-            for first, last in ((0, cut), (cut, T)):
-                nc.vector.tensor_copy(part[:, first:last], dx[k][:].indirect(pos1_t[:, first // 16 : last // 16]))
-            for first, width in SHARES[k]:
-                total = keep.tile([P, width], F32, name=f"total_{k}_{first}")
-                nc.vector.tensor_tensor(
-                    total[:],
-                    dx[k][:].indirect(pos2_t[:, first // 16 : (first + width) // 16]),
-                    part[:, first : first + width],
-                    ADD,
-                )
-                nc.sync.dma_start(out[k * P : (k + 1) * P, first : first + width], total[:])
+            for first in range(0, T, SHARE):
+                cols = slice(first // 16, (first + SHARE) // 16)
+                part = keep.tile([P, SHARE], F32, name=f"part_{k}_{first}")
+                total = keep.tile([P, SHARE], F32, name=f"total_{k}_{first}")
+                nc.scalar.activation(part[:], dx[k][:].indirect(pos1_t[:, cols]), COPY)
+                nc.vector.tensor_tensor(total[:], dx[k][:].indirect(pos2_t[:, cols]), part[:], ADD)
+                nc.sync.dma_start(out[k * P : (k + 1) * P, first : first + SHARE], total[:])

@@ -26,6 +26,7 @@ BYTES = 4 * N * T + 4 * H * S + E * (N * H + H * K) * 17 // 32 + 4 * S + 2 * S +
 PIECE = 512
 PIECES = S // PIECE
 CHUNK = 128
+PITCH = C + 9
 SHARE = 256
 
 
@@ -44,8 +45,9 @@ def tile_moe_bdx_mlp_relu_kernel(
 
         dy = [keep.tile([P, T], F32, name=f"dy{t}") for t in range(PACK)]
         gates = [keep.tile([P, PIECE], F32, name=f"gates{q}") for q in range(PIECES)]
-        pre = [keep.tile([P, PACK, C], F32, name=f"pre{e}", align_bytes=64) for e in range(E)]
-        w2_raw = [keep.tile([P, 2, 2 * H], U8, name=f"w2_raw{q}") for q in range(PIECES)]
+        pre_flat = [keep.tile([P, PACK * PITCH], F32, name=f"pre{e}", align_bytes=64) for e in range(E)]
+        pre = [flat[:].rearrange("p (t s) -> p t s", t=PACK)[:, :, 0:C] for flat in pre_flat]
+        w2_raw = [keep.tile([P, 2 * H], U8, name=f"w2_raw{e}") for e in range(E)]
         w2_t = [keep.tile([P, 2 * H], U8, name=f"w2_t{e}", align_bytes=64) for e in range(E)]
         s2_raw = keep.tile([P, H], U8, name="s2_raw")
         s2_mid = keep.tile([P, H], U8, name="s2_mid")
@@ -67,34 +69,34 @@ def tile_moe_bdx_mlp_relu_kernel(
             return view.rearrange("p e i -> p (e i)").bitcast(I32).rearrange("p (e i) -> p e i", e=e)
 
         def as_words(view):
-            return view.rearrange("p t s -> p (t s)").bitcast(BF16).rearrange("p (s t) -> p s t", t=PACK)
+            return view[:, 0 : PIECE * PACK // 2].bitcast(BF16).rearrange("p (s t) -> p s t", t=PACK)
 
         def load_gate(q):
             nc.sync.dma_start(gates[q][:], gate[0:P, q * PIECE : (q + 1) * PIECE])
 
         def load_pre(e):
-            nc.sync.dma_start(pre[e][:], a_rows[:, :, e * C : (e + 1) * C])
+            nc.sync.dma_start(pre[e], a_rows[:, :, e * C : (e + 1) * C])
 
-        def load_w2(q):
-            nc.sync.dma_start(
-                as_i32(w2_raw[q][:]), w2_words[2 * q : 2 * q + 2].rearrange("e g p b -> p (e g) b").bitcast(I32)
-            )
+        def load_w2(e):
+            nc.sync.dma_start(w2_raw[e][:].bitcast(I32), w2_words[e, 0].bitcast(I32))
 
-        nc.sync.dma_start(offs_t[:], offs)
-        nc.sync.dma_start(dy[0][:], dyT_rows[:, 0, :])
-        load_gate(1)
-        nc.sync.dma_start(s2_raw[:].bitcast(I32), w2_scales.rearrange("e g f i -> f (e g) i").bitcast(I32))
-        for t in range(1, PACK):
-            nc.sync.dma_start(dy[t][:], dyT_rows[:, t, :])
-        load_gate(0)
         load_w2(0)
-        load_w2(1)
+        nc.sync.dma_start(s2_raw[:].bitcast(I32), w2_scales.rearrange("e g f i -> f (e g) i").bitcast(I32))
+        nc.sync.dma_start(offs_t[:], offs)
+        for t in range(PACK):
+            nc.sync.dma_start(dy[t][:], dyT_rows[:, t, :])
+            if t == 0:
+                load_gate(1)
+        load_gate(0)
+        for e in range(1, 4):
+            load_w2(e)
         load_pre(0)
         load_pre(1)
         load_pre(2)
         load_pre(3)
         load_gate(2)
-        load_w2(2)
+        load_w2(4)
+        load_w2(5)
         nc.sync.dma_start(as_i32(w1_t[:]), w1_words.rearrange("e g p b -> p (e g) b").bitcast(I32))
         for r in range(4):
             nc.sync.dma_start(
@@ -103,7 +105,8 @@ def tile_moe_bdx_mlp_relu_kernel(
         load_pre(4)
         load_gate(3)
         load_pre(5)
-        load_w2(3)
+        load_w2(6)
+        load_w2(7)
         load_pre(6)
         load_pre(7)
         nc.sync.dma_start(pos1_t[:], pos1)
@@ -126,12 +129,12 @@ def tile_moe_bdx_mlp_relu_kernel(
                 s2_mid[:].rearrange("p (t m) -> p t m", t=PACK), s2_raw[:].rearrange("p (m t) -> p t m", t=PACK)
             )
             for quad in range(4):
-                nc.scalar.dma_start(as_i32(s2_t[32 * quad : 32 * quad + 4]), s2_mid[32 * quad : 32 * quad + 32].bitcast(I32))
+                (nc.scalar, nc.gpsimd)[quad % 2].dma_start(as_i32(s2_t[32 * quad : 32 * quad + 4]), s2_mid[32 * quad : 32 * quad + 32].bitcast(I32))
 
         def turn_words(e):
             nc.scalar.copy(
                 w2_t[e][:].bitcast(U16).rearrange("p (t m) -> p t m", t=PACK),
-                w2_raw[e // 2][:, e % 2, :].bitcast(U16).rearrange("p (m t) -> p t m", t=PACK),
+                w2_raw[e][:].bitcast(U16).rearrange("p (m t) -> p t m", t=PACK),
             )
 
         def round_g(e):
@@ -211,15 +214,14 @@ def tile_moe_bdx_mlp_relu_kernel(
 
         for q in range(2):
             grouped[q] = keep.tile([P, PIECE, PACK], BF16, name=f"grouped{q}", align_bytes=64)[:]
-        grouped[2] = as_words(pre[2][:])
-        grouped[3] = as_words(pre[3][:])
+        grouped[2] = as_words(pre_flat[2])
+        grouped[3] = as_words(pre_flat[3])
 
-        plain_gathers(0)
-        gated_gather(1, 0)
-        turn_scales()
-        for t in range(1, PACK):
-            gated_gather(1, t)
         turn_words(0)
+        turn_scales()
+        plain_gathers(0)
+        for t in range(PACK):
+            gated_gather(1, t)
         turn_words(1)
         gate_g(0)
         gate_g(1)

@@ -47,7 +47,7 @@ def tile_moe_bdx_mlp_relu_kernel(
         gates = [keep.tile([P, PIECE], F32, name=f"gates{q}") for q in range(PIECES)]
         pre_flat = [keep.tile([P, PACK * PITCH], F32, name=f"pre{e}", align_bytes=64) for e in range(E)]
         pre = [flat[:].rearrange("p (t s) -> p t s", t=PACK)[:, :, 0:C] for flat in pre_flat]
-        w2_raw = [keep.tile([P, 2 * H], U8, name=f"w2_raw{e}") for e in range(E)]
+        w2_raw = [keep.tile([P, 2 * H], U8, name=f"w2_raw{e}", align_bytes=64) for e in range(E)]
         w2_t = [keep.tile([P, 2 * H], U8, name=f"w2_t{e}", align_bytes=64) for e in range(E)]
         s2_raw = keep.tile([P, H], U8, name="s2_raw")
         s2_mid = keep.tile([P, H], U8, name="s2_mid")
@@ -112,17 +112,17 @@ def tile_moe_bdx_mlp_relu_kernel(
         nc.sync.dma_start(pos1_t[:], pos1)
         nc.sync.dma_start(pos2_t[:], pos2)
 
-        g_codes, da_codes, grouped = {}, {}, {}
+        g_codes, da_codes, grouped, pairs = {}, {}, {}, {}
 
         def window(q, t):
             return dy[t][:].indirect(offs_t[:, q * PIECE // 16 : (q + 1) * PIECE // 16])
 
         def plain_gathers(q):
             for t in range(PACK):
-                nc.scalar.activation(planes[q % 2][:, t, :], window(q, t), COPY)
+                nc.scalar.activation(planes[q][:, t, :], window(q, t), COPY)
 
         def gated_gather(q, t):
-            nc.vector.tensor_tensor(planes[q % 2][:, t, :], window(q, t), gates[q][:], MULT)
+            nc.vector.tensor_tensor(planes[q][:, t, :], window(q, t), gates[q][:], MULT)
 
         def turn_scales():
             nc.vector.tensor_copy(
@@ -141,14 +141,14 @@ def tile_moe_bdx_mlp_relu_kernel(
             q, first = e // 2, e % 2 * C
             nc.scalar.copy(
                 grouped[q][:, first : first + C, :].rearrange("p (c i) (u e) -> p c u i e", i=4, u=2),
-                planes[q % 2][:, :, first : first + C].rearrange("p (u e) (c i) -> p c u i e", i=4, u=2),
+                planes[q][:, :, first : first + C].rearrange("p (u e) (c i) -> p c u i e", i=4, u=2),
             )
 
         def gate_g(e):
             q, first = e // 2, e % 2 * C
             nc.vector.tensor_tensor(
                 grouped[q][:, first : first + C, :].rearrange("p (c i) t -> p c t i", i=2),
-                planes[q % 2][:, :, first : first + C].rearrange("p t (c i) -> p c t i", i=2),
+                planes[q][:, :, first : first + C].rearrange("p t (c i) -> p c t i", i=2),
                 gates[q][:, first : first + C].rearrange("p (c i) -> p c i", i=2).unsqueeze(2).to_broadcast([P, C // 2, PACK, 2]),
                 MULT,
             )
@@ -193,6 +193,37 @@ def tile_moe_bdx_mlp_relu_kernel(
                 MULT,
             )
 
+        def make_pairs(e, u):
+            bank = psum.tile([P, 2, C], F32, name=f"bank{(2 * e + u) % 4}")
+            for j in range(2):
+                t = 2 * u + j
+                nc.tensor.matmul_mx(
+                    out=bank[:, j, :],
+                    lhsT=w2_t[e][:, t * 2 * P : (t + 1) * 2 * P].bitcast(FP4X4),
+                    lhsT_scale=s2_t[:, e, t * P : (t + 1) * P],
+                    rhs=g_codes[e][0].bitcast(FP8X4),
+                    rhs_scale=g_codes[e][1],
+                    start=True,
+                    stop=True,
+                )
+            if u == 0:
+                pairs[e] = keep.tile([P, 2, C, 2], BF16, name=f"pairs{e}")
+            nc.vector.scalar_tensor_tensor(
+                pairs[e][:, u],
+                pre[e][:, 2 * u : 2 * u + 2, :].rearrange("p j s -> p s j"),
+                0.0,
+                bank[:].rearrange("p j s -> p s j"),
+                IS_GT,
+                MULT,
+            )
+
+        def weave(e):
+            first = e % 2 * C
+            nc.scalar.copy(
+                da[e // 2][:, first : first + C, :].rearrange("p s t -> p (s t)").bitcast(U32).rearrange("p (s u) -> p s u", u=2),
+                pairs[e][:].rearrange("p u s j -> p (u s j)").bitcast(U32).rearrange("p (u s) -> p s u", u=2),
+            )
+
         def second_product(k, q, first, width, bank, copy):
             acc = psum.tile([P, PIECE], F32, name=f"bank{bank}")
             for start in range(first, first + width, C):
@@ -215,7 +246,7 @@ def tile_moe_bdx_mlp_relu_kernel(
         for q in range(2):
             grouped[q] = keep.tile([P, PIECE, PACK], BF16, name=f"grouped{q}", align_bytes=64)[:]
         grouped[2] = as_words(pre_flat[2])
-        grouped[3] = as_words(pre_flat[3])
+        grouped[3] = as_words(pre_flat[4])
 
         turn_words(0)
         turn_scales()
@@ -231,6 +262,7 @@ def tile_moe_bdx_mlp_relu_kernel(
         quantise_g(0, C, C)
         turn_words(2)
         turn_words(3)
+        planes.append(planes[0])
         plain_gathers(2)
         make_da(0, 0)
         quantise_g(1)
@@ -244,25 +276,31 @@ def tile_moe_bdx_mlp_relu_kernel(
         make_da(3, 1)
         turn_words(4)
         turn_words(5)
+        planes.append(keep.tile([P, PACK, PIECE], F32, name="w2_raw5", align_bytes=64))
         plain_gathers(3)
         gate_g(4)
         gate_g(5)
+        quantise_g(2, 0, C)
         quantise_da(1)
-        quantise_g(2)
-        second_products(0)
+        quantise_g(2, C, C)
         turn_words(6)
         turn_words(7)
+        second_products(0)
+        make_pairs(4, 0)
+        make_pairs(4, 1)
+        weave(4)
+        make_pairs(5, 0)
+        make_pairs(5, 1)
+        weave(5)
         gate_g(6)
-        make_da(4, 0)
-        make_da(4, 1)
         gate_g(7)
-        make_da(5, 0)
-        quantise_g(3)
-        make_da(5, 1)
-        second_products(1)
-        make_da(6, 0)
+        quantise_g(3, 0, C)
         quantise_da(2)
-        make_da(6, 1)
+        quantise_g(3, C, C)
+        second_products(1)
+        make_pairs(6, 0)
+        make_pairs(6, 1)
+        weave(6)
         make_da(7, 0)
         quantise_da(3, 0, C)
         make_da(7, 1)

@@ -27,7 +27,10 @@ PIECE = 512
 PIECES = S // PIECE
 CHUNK = 128
 PITCH = C + 9
-SHARE = 256
+SHARES = (
+    ((0, 128), (128, 256), (384, 320), (704, 320)),
+    ((0, 320), (320, 320), (640, 256), (896, 128)),
+)
 
 
 def tile_moe_bdx_mlp_relu_kernel(
@@ -147,9 +150,9 @@ def tile_moe_bdx_mlp_relu_kernel(
         def gate_g(e):
             q, first = e // 2, e % 2 * C
             nc.vector.tensor_tensor(
-                grouped[q][:, first : first + C, :].rearrange("p (c i) t -> p c t i", i=2),
-                planes[q][:, :, first : first + C].rearrange("p t (c i) -> p c t i", i=2),
-                gates[q][:, first : first + C].rearrange("p (c i) -> p c i", i=2).unsqueeze(2).to_broadcast([P, C // 2, PACK, 2]),
+                grouped[q][:, first : first + C, :].rearrange("p (c i) t -> p c t i", i=4),
+                planes[q][:, :, first : first + C].rearrange("p t (c i) -> p c t i", i=4),
+                gates[q][:, first : first + C].rearrange("p (c i) -> p c i", i=4).unsqueeze(2).to_broadcast([P, C // 4, PACK, 4]),
                 MULT,
             )
 
@@ -312,10 +315,13 @@ def tile_moe_bdx_mlp_relu_kernel(
         second_product(1, 3, C, C, 1, nc.vector.tensor_copy)
 
         for k in range(2):
-            for first in range(0, T, SHARE):
-                cols = slice(first // 16, (first + SHARE) // 16)
-                part = keep.tile([P, SHARE], F32, name=f"part_{k}_{first}")
-                total = keep.tile([P, SHARE], F32, name=f"total_{k}_{first}")
-                nc.scalar.activation(part[:], dx[k][:].indirect(pos1_t[:, cols]), COPY)
+            for first, width in SHARES[k]:
+                cols = slice(first // 16, (first + width) // 16)
+                part = keep.tile([P, width], F32, name=f"part_{k}_{first}")
+                total = keep.tile([P, width], F32, name=f"total_{k}_{first}")
+                if (k, first) == (0, 0):
+                    nc.vector.tensor_copy(part[:], dx[k][:].indirect(pos1_t[:, cols]))
+                else:
+                    nc.scalar.activation(part[:], dx[k][:].indirect(pos1_t[:, cols]), COPY)
                 nc.vector.tensor_tensor(total[:], dx[k][:].indirect(pos2_t[:, cols]), part[:], ADD)
-                nc.sync.dma_start(out[k * P : (k + 1) * P, first : first + SHARE], total[:])
+                nc.sync.dma_start(out[k * P : (k + 1) * P, first : first + width], total[:])

@@ -26,7 +26,7 @@ BYTES = 4 * N * T + 4 * H * S + E * (N * H + H * K) * 17 // 32 + 4 * S + 2 * S +
 PIECE = 512
 PIECES = S // PIECE
 CHUNK = 128
-PITCH = C + 9
+GROUPS = ((0, 1), (1, 1), (2, 2), (4, 2), (6, 2))
 SHARES = (
     ((0, 128), (128, 256), (384, 320), (704, 320)),
     ((0, 320), (320, 320), (640, 256), (896, 128)),
@@ -46,12 +46,12 @@ def tile_moe_bdx_mlp_relu_kernel(
         pos1_t = lists.tile([P, T // 16], U16, name="pos1_t")
         pos2_t = lists.tile([P, T // 16], U16, name="pos2_t")
 
-        dy = [keep.tile([P, T], F32, name=f"dy{t}") for t in range(PACK)]
-        gates = [keep.tile([P, PIECE], F32, name=f"gates{q}") for q in range(PIECES)]
-        pre_flat = [keep.tile([P, PACK * PITCH], F32, name=f"pre{e}", align_bytes=64) for e in range(E)]
-        pre = [flat[:].rearrange("p (t s) -> p t s", t=PACK)[:, :, 0:C] for flat in pre_flat]
-        w2_raw = [keep.tile([P, 2 * H], U8, name=f"w2_raw{e}", align_bytes=64) for e in range(E)]
-        w2_t = [keep.tile([P, 2 * H], U8, name=f"w2_t{e}", align_bytes=64) for e in range(E)]
+        dy = [keep.tile([P, T], F32, name=f"dy{t}", align_bytes=64) for t in range(PACK)]
+        gates = [keep.tile([P, PIECE], F32, name=f"gates{q}", align_bytes=64) for q in range(PIECES)]
+        pre = [keep.tile([P, PACK, C], F32, name=f"pre{e}", align_bytes=64) for e in range(E)]
+        w2_raw = {e: keep.tile([P, n, 2 * H], U8, name=f"w2_raw{e}", align_bytes=64) for e, n in GROUPS}
+        w2_turned = {e: keep.tile([P, n, 2 * H], U8, name=f"w2_t{e}", align_bytes=64) for e, n in GROUPS}
+        w2_t = [w2_turned[e][:, j, :] for e, n in GROUPS for j in range(n)]
         s2_raw = keep.tile([P, H], U8, name="s2_raw")
         s2_mid = keep.tile([P, H], U8, name="s2_mid")
         s2_t = keep.tile([P, E, H], U8, name="s2_t", align_bytes=64)
@@ -59,7 +59,7 @@ def tile_moe_bdx_mlp_relu_kernel(
         s1_t = keep.tile([P, E, K], U8, name="s1_t", align_bytes=64)
         dx = [keep.tile([P, S], F32, name=f"dx{k}") for k in range(2)]
         planes = [keep.tile([P, PACK, PIECE], F32, name=f"planes{j}", align_bytes=64) for j in range(2)]
-        da = [keep.tile([P, PIECE, PACK], BF16, name=f"da{q}", align_bytes=64) for q in range(PIECES)]
+        da = {}
 
         nc.gpsimd.memset(s2_t[:].rearrange("p e i -> p (e i)").bitcast(I32), 0)
         nc.gpsimd.memset(s1_t[:].rearrange("p e i -> p (e i)").bitcast(I32), 0)
@@ -72,16 +72,17 @@ def tile_moe_bdx_mlp_relu_kernel(
             return view.rearrange("p e i -> p (e i)").bitcast(I32).rearrange("p (e i) -> p e i", e=e)
 
         def as_words(view):
-            return view[:, 0 : PIECE * PACK // 2].bitcast(BF16).rearrange("p (s t) -> p s t", t=PACK)
+            return view.rearrange("p t s -> p (t s)").bitcast(BF16).rearrange("p (s t) -> p s t", t=PACK)
 
         def load_gate(q):
             nc.sync.dma_start(gates[q][:], gate[0:P, q * PIECE : (q + 1) * PIECE])
 
         def load_pre(e):
-            nc.sync.dma_start(pre[e], a_rows[:, :, e * C : (e + 1) * C])
+            nc.sync.dma_start(pre[e][:], a_rows[:, :, e * C : (e + 1) * C])
 
         def load_w2(e):
-            nc.sync.dma_start(w2_raw[e][:].bitcast(I32), w2_words[e, 0].bitcast(I32))
+            n = w2_raw[e].shape[1]
+            nc.sync.dma_start(as_i32(w2_raw[e][:]), w2_words[e : e + n].bitcast(I32).rearrange("e g p b -> p (e g) b"))
 
         load_w2(0)
         nc.sync.dma_start(s2_raw[:].bitcast(I32), w2_scales.rearrange("e g f i -> f (e g) i").bitcast(I32))
@@ -91,15 +92,14 @@ def tile_moe_bdx_mlp_relu_kernel(
             if t == 0:
                 load_gate(1)
         load_gate(0)
-        for e in range(1, 4):
-            load_w2(e)
+        load_w2(1)
+        load_w2(2)
         load_pre(0)
         load_pre(1)
         load_pre(2)
         load_pre(3)
         load_gate(2)
         load_w2(4)
-        load_w2(5)
         nc.sync.dma_start(as_i32(w1_t[:]), w1_words.rearrange("e g p b -> p (e g) b").bitcast(I32))
         for r in range(4):
             nc.sync.dma_start(
@@ -109,7 +109,6 @@ def tile_moe_bdx_mlp_relu_kernel(
         load_gate(3)
         load_pre(5)
         load_w2(6)
-        load_w2(7)
         load_pre(6)
         load_pre(7)
         nc.sync.dma_start(pos1_t[:], pos1)
@@ -135,9 +134,10 @@ def tile_moe_bdx_mlp_relu_kernel(
                 (nc.scalar, nc.gpsimd)[quad % 2].dma_start(as_i32(s2_t[32 * quad : 32 * quad + 4]), s2_mid[32 * quad : 32 * quad + 32].bitcast(I32))
 
         def turn_words(e):
+            n = w2_raw[e].shape[1]
             nc.scalar.copy(
-                w2_t[e][:].bitcast(U16).rearrange("p (t m) -> p t m", t=PACK),
-                w2_raw[e][:].bitcast(U16).rearrange("p (m t) -> p t m", t=PACK),
+                w2_turned[e][:].rearrange("p e b -> p (e b)").bitcast(U16).rearrange("p (e t m) -> p e t m", e=n, t=PACK),
+                w2_raw[e][:].rearrange("p e b -> p (e b)").bitcast(U16).rearrange("p (e m t) -> p e t m", e=n, t=PACK),
             )
 
         def round_g(e):
@@ -156,8 +156,8 @@ def tile_moe_bdx_mlp_relu_kernel(
                 MULT,
             )
 
-        def quantise(source, codes, label, q, first, width):
-            words = keep.tile([P, width], U32, name=f"{label}_words{q}_{first}", align_bytes=64)
+        def quantise(source, codes, label, q, first, width, place):
+            words = keep.tile([P, width], U32, name=place or f"{label}_words{q}_{first}", align_bytes=64)
             scales = keep.tile([P, width], U8, name=f"{label}_scales{q}_{first}", align_bytes=64)
             for start in range(0, width, C):
                 codes[2 * q + (first + start) // C] = (words[:, start : start + C], scales[:, start : start + C])
@@ -168,10 +168,10 @@ def tile_moe_bdx_mlp_relu_kernel(
             )
 
         def quantise_g(q, first=0, width=PIECE):
-            quantise(grouped, g_codes, "g", q, first, width)
+            quantise(grouped, g_codes, "g", q, first, width, None)
 
-        def quantise_da(q, first=0, width=PIECE):
-            quantise(da, da_codes, "da", q, first, width)
+        def quantise_da(q, first=0, width=PIECE, place=None):
+            quantise(da, da_codes, "da", q, first, width, place)
 
         def make_da(e, half):
             bank = psum.tile([P, PACK, CHUNK], F32, name=f"bank{(2 * e + half) % 4}")
@@ -209,10 +209,10 @@ def tile_moe_bdx_mlp_relu_kernel(
                     start=True,
                     stop=True,
                 )
-            if u == 0:
-                pairs[e] = keep.tile([P, 2, C, 2], BF16, name=f"pairs{e}")
+            if e // 2 not in pairs:
+                pairs[e // 2] = keep.tile([P, 2, 2, C, 2], BF16, name=f"pairs{e // 2}")
             nc.vector.scalar_tensor_tensor(
-                pairs[e][:, u],
+                pairs[e // 2][:, e % 2, u],
                 pre[e][:, 2 * u : 2 * u + 2, :].rearrange("p j s -> p s j"),
                 0.0,
                 bank[:].rearrange("p j s -> p s j"),
@@ -220,12 +220,10 @@ def tile_moe_bdx_mlp_relu_kernel(
                 MULT,
             )
 
-        def weave(e):
-            first = e % 2 * C
-            nc.scalar.copy(
-                da[e // 2][:, first : first + C, :].rearrange("p s t -> p (s t)").bitcast(U32).rearrange("p (s u) -> p s u", u=2),
-                pairs[e][:].rearrange("p u s j -> p (u s j)").bitcast(U32).rearrange("p (u s) -> p s u", u=2),
-            )
+        def weave(q, count=2):
+            words = da[q][:].rearrange("p s t -> p (s t)").bitcast(U32).rearrange("p (e s u) -> p e s u", e=2, u=2)
+            halves = pairs[q][:].rearrange("p e u s j -> p (e u s j)").bitcast(U32).rearrange("p (e u s) -> p e s u", e=2, u=2)
+            nc.scalar.copy(words[:, 0:count], halves[:, 0:count])
 
         def second_product(k, q, first, width, bank, copy):
             acc = psum.tile([P, PIECE], F32, name=f"bank{bank}")
@@ -248,8 +246,8 @@ def tile_moe_bdx_mlp_relu_kernel(
 
         for q in range(2):
             grouped[q] = keep.tile([P, PIECE, PACK], BF16, name=f"grouped{q}", align_bytes=64)[:]
-        grouped[2] = as_words(pre_flat[2])
-        grouped[3] = as_words(pre_flat[4])
+        grouped[2] = as_words(pre[2][:])
+        grouped[3] = as_words(pre[4][:])
 
         turn_words(0)
         turn_scales()
@@ -264,46 +262,40 @@ def tile_moe_bdx_mlp_relu_kernel(
         quantise_g(0, 0, C)
         quantise_g(0, C, C)
         turn_words(2)
-        turn_words(3)
         planes.append(planes[0])
         plain_gathers(2)
-        make_da(0, 0)
         quantise_g(1)
-        make_da(0, 1)
-        make_da(1, 0)
-        make_da(1, 1)
-        make_da(2, 0)
-        quantise_da(0)
-        make_da(2, 1)
-        make_da(3, 0)
-        make_da(3, 1)
+        for e in range(4):
+            make_pairs(e, 0)
+            make_pairs(e, 1)
         turn_words(4)
-        turn_words(5)
-        planes.append(keep.tile([P, PACK, PIECE], F32, name="w2_raw5", align_bytes=64))
+        planes.append(keep.tile([P, PACK, PIECE], F32, name="w2_raw4", align_bytes=64))
         plain_gathers(3)
         gate_g(4)
         gate_g(5)
         quantise_g(2, 0, C)
-        quantise_da(1)
         quantise_g(2, C, C)
+        for q, place in enumerate(("dy2", "dy3", "da2", "da3")):
+            da[q] = keep.tile([P, PIECE, PACK], BF16, name=place, align_bytes=64)
+        weave(0)
+        weave(1)
         turn_words(6)
-        turn_words(7)
-        second_products(0)
-        make_pairs(4, 0)
-        make_pairs(4, 1)
-        weave(4)
-        make_pairs(5, 0)
-        make_pairs(5, 1)
-        weave(5)
+        for e in (4, 5):
+            make_pairs(e, 0)
+            make_pairs(e, 1)
+        weave(2)
         gate_g(6)
         gate_g(7)
         quantise_g(3, 0, C)
-        quantise_da(2)
+        quantise_da(0, place="w2_raw4")
         quantise_g(3, C, C)
-        second_products(1)
+        quantise_da(1, place="gates3")
+        second_products(0)
         make_pairs(6, 0)
+        quantise_da(2, place="pre4")
         make_pairs(6, 1)
-        weave(6)
+        weave(3, 1)
+        second_products(1)
         make_da(7, 0)
         quantise_da(3, 0, C)
         make_da(7, 1)
@@ -311,8 +303,8 @@ def tile_moe_bdx_mlp_relu_kernel(
         quantise_da(3, C, C)
         second_product(0, 3, 0, C, 6, nc.scalar.copy)
         second_product(1, 3, 0, C, 7, nc.scalar.copy)
-        second_product(0, 3, C, C, 0, nc.scalar.copy)
-        second_product(1, 3, C, C, 1, nc.vector.tensor_copy)
+        second_product(0, 3, C, C, 0, nc.vector.tensor_copy)
+        second_product(1, 3, C, C, 1, nc.scalar.copy)
 
         for k in range(2):
             for first, width in SHARES[k]:

@@ -50,8 +50,7 @@ def tile_moe_bdx_mlp_relu_kernel(
         gates = [keep.tile([P, PIECE], F32, name=f"gates{q}", align_bytes=64) for q in range(PIECES)]
         pre = [keep.tile([P, PACK, C], F32, name=f"pre{e}", align_bytes=64) for e in range(E)]
         w2_raw = {e: keep.tile([P, n, 2 * H], U8, name=f"w2_raw{e}", align_bytes=64) for e, n in GROUPS}
-        w2_turned = {e: keep.tile([P, n, 2 * H], U8, name=f"w2_t{e}", align_bytes=64) for e, n in GROUPS}
-        w2_t = [w2_turned[e][:, j, :] for e, n in GROUPS for j in range(n)]
+        w2_t = {}
         s2_raw = keep.tile([P, H], U8, name="s2_raw")
         s2_mid = keep.tile([P, H], U8, name="s2_mid")
         s2_t = keep.tile([P, E, H], U8, name="s2_t", align_bytes=64)
@@ -96,10 +95,10 @@ def tile_moe_bdx_mlp_relu_kernel(
         load_w2(2)
         load_pre(0)
         load_pre(1)
+        load_w2(4)
         load_pre(2)
         load_pre(3)
         load_gate(2)
-        load_w2(4)
         nc.sync.dma_start(as_i32(w1_t[:]), w1_words.rearrange("e g p b -> p (e g) b").bitcast(I32))
         for r in range(4):
             nc.sync.dma_start(
@@ -133,12 +132,27 @@ def tile_moe_bdx_mlp_relu_kernel(
             for quad in range(4):
                 (nc.scalar, nc.gpsimd)[quad % 2].dma_start(as_i32(s2_t[32 * quad : 32 * quad + 4]), s2_mid[32 * quad : 32 * quad + 32].bitcast(I32))
 
+        def turned_tile(e, place):
+            n = w2_raw[e].shape[1]
+            turned = keep.tile([P, n, 2 * H], U8, name=place, align_bytes=64)
+            for j in range(n):
+                w2_t[e + j] = turned[:, j, :]
+            return turned
+
         def turn_words(e):
             n = w2_raw[e].shape[1]
             nc.scalar.copy(
-                w2_turned[e][:].rearrange("p e b -> p (e b)").bitcast(U16).rearrange("p (e t m) -> p e t m", e=n, t=PACK),
+                turned_tile(e, f"w2_t{e}")[:].rearrange("p e b -> p (e b)").bitcast(U16).rearrange("p (e t m) -> p e t m", e=n, t=PACK),
                 w2_raw[e][:].rearrange("p e b -> p (e b)").bitcast(U16).rearrange("p (e m t) -> p e t m", e=n, t=PACK),
             )
+
+        def turn_bytes(e, place):
+            turned = turned_tile(e, place)
+            for j in range(2):
+                nc.gpsimd.tensor_copy(
+                    turned[:, j, :].rearrange("p (t m b) -> p t m b", t=PACK, b=2),
+                    w2_raw[e][:, j, :].rearrange("p (m t b) -> p t m b", t=PACK, b=2),
+                )
 
         def round_g(e):
             q, first = e // 2, e % 2 * C
@@ -265,11 +279,11 @@ def tile_moe_bdx_mlp_relu_kernel(
         planes.append(planes[0])
         plain_gathers(2)
         quantise_g(1)
+        turn_bytes(4, "grouped1")
         for e in range(4):
             make_pairs(e, 0)
             make_pairs(e, 1)
-        turn_words(4)
-        planes.append(keep.tile([P, PACK, PIECE], F32, name="w2_raw4", align_bytes=64))
+        planes.append(keep.tile([P, PACK, PIECE], F32, name="planes1", align_bytes=64))
         plain_gathers(3)
         gate_g(4)
         gate_g(5)
@@ -279,7 +293,7 @@ def tile_moe_bdx_mlp_relu_kernel(
             da[q] = keep.tile([P, PIECE, PACK], BF16, name=place, align_bytes=64)
         weave(0)
         weave(1)
-        turn_words(6)
+        turn_bytes(6, "pre2")
         for e in (4, 5):
             make_pairs(e, 0)
             make_pairs(e, 1)
@@ -287,7 +301,7 @@ def tile_moe_bdx_mlp_relu_kernel(
         gate_g(6)
         gate_g(7)
         quantise_g(3, 0, C)
-        quantise_da(0, place="w2_raw4")
+        quantise_da(0, place="planes1")
         quantise_g(3, C, C)
         quantise_da(1, place="gates3")
         second_products(0)

@@ -1,6 +1,7 @@
 from contextlib import ExitStack
 
 import concourse.mybir as mybir
+from concourse.masks import make_identity
 
 K, T, E, C, H, N = 256, 1024, 8, 256, 512, 512
 S = E * C
@@ -27,8 +28,9 @@ PIECE = 512
 PIECES = S // PIECE
 CHUNK = 128
 GROUPS = ((0, 1), (1, 1), (2, 2), (4, 2), (6, 2))
+WALK = 4
 SHARES = (
-    ((0, 128), (128, 256), (384, 320), (704, 320)),
+    ((0, 192), (192, 256), (448, 320), (768, 256)),
     ((0, 320), (320, 320), (640, 256), (896, 128)),
 )
 
@@ -47,7 +49,10 @@ def tile_moe_bdx_mlp_relu_kernel(
         pos2_t = lists.tile([P, T // 16], U16, name="pos2_t")
 
         dy = [keep.tile([P, T], F32, name=f"dy{t}", align_bytes=64) for t in range(PACK)]
-        gates = [keep.tile([P, PIECE], F32, name=f"gates{q}", align_bytes=64) for q in range(PIECES)]
+        gates = keep.tile([P, PIECE], F32, name="gates", align_bytes=64)
+        gate_cols = [keep.tile([P, 2, 2], F32, name=f"gate_cols{j}") for j in range(2)]
+        gate_rows = {e: keep.tile([P, C], F32, name=f"gate_rows{e}") for e in (4, 6)}
+        ident = keep.tile([P, P], F32, name="ident")
         pre = [keep.tile([P, PACK, C], F32, name=f"pre{e}", align_bytes=64) for e in range(E)]
         w2_raw = {e: keep.tile([P, n, 2 * H], U8, name=f"w2_raw{e}", align_bytes=64) for e, n in GROUPS}
         w2_t = {}
@@ -56,10 +61,11 @@ def tile_moe_bdx_mlp_relu_kernel(
         s2_t = keep.tile([P, E, H], U8, name="s2_t", align_bytes=64)
         w1_t = keep.tile([P, E, 2 * K], U8, name="w1_t", align_bytes=64)
         s1_t = keep.tile([P, E, K], U8, name="s1_t", align_bytes=64)
-        dx = [keep.tile([P, S], F32, name=f"dx{k}") for k in range(2)]
-        planes = [keep.tile([P, PACK, PIECE], F32, name=f"planes{j}", align_bytes=64) for j in range(2)]
+        dx = []
+        planes = {}
         da = {}
 
+        make_identity(nc, ident[:])
         nc.gpsimd.memset(s2_t[:].rearrange("p e i -> p (e i)").bitcast(I32), 0)
         nc.gpsimd.memset(s1_t[:].rearrange("p e i -> p (e i)").bitcast(I32), 0)
 
@@ -73,8 +79,10 @@ def tile_moe_bdx_mlp_relu_kernel(
         def as_words(view):
             return view.rearrange("p t s -> p (t s)").bitcast(BF16).rearrange("p (s t) -> p s t", t=PACK)
 
-        def load_gate(q):
-            nc.sync.dma_start(gates[q][:], gate[0:P, q * PIECE : (q + 1) * PIECE])
+        gate_pairs = gate[0:1, :].rearrange("o (e p c) -> p (o e) c", p=P, c=2)
+
+        def load_gate_rows(e):
+            nc.sync.dma_start(gate_rows[e][:], gate[0:P, e * C : (e + 1) * C])
 
         def load_pre(e):
             nc.sync.dma_start(pre[e][:], a_rows[:, :, e * C : (e + 1) * C])
@@ -86,44 +94,51 @@ def tile_moe_bdx_mlp_relu_kernel(
         load_w2(0)
         nc.sync.dma_start(s2_raw[:].bitcast(I32), w2_scales.rearrange("e g f i -> f (e g) i").bitcast(I32))
         nc.sync.dma_start(offs_t[:], offs)
-        for t in range(PACK):
+        nc.sync.dma_start(dy[0][:], dyT_rows[:, 0, :])
+        nc.sync.dma_start(gates[:], gate[0:P, PIECE : 2 * PIECE])
+        nc.sync.dma_start(gate_cols[0][:], gate_pairs[:, 0:2, :])
+        for t in range(1, PACK):
             nc.sync.dma_start(dy[t][:], dyT_rows[:, t, :])
-            if t == 0:
-                load_gate(1)
-        load_gate(0)
+        nc.sync.dma_start(gate_cols[1][:], gate_pairs[:, 5:8:2, :])
         load_w2(1)
         load_w2(2)
         load_pre(0)
-        load_pre(1)
         load_w2(4)
+        load_pre(1)
         load_pre(2)
+        load_gate_rows(4)
         load_pre(3)
-        load_gate(2)
+        load_pre(4)
+        load_gate_rows(6)
+        load_w2(6)
+        for e in range(5, E):
+            load_pre(e)
         nc.sync.dma_start(as_i32(w1_t[:]), w1_words.rearrange("e g p b -> p (e g) b").bitcast(I32))
         for r in range(4):
             nc.sync.dma_start(
                 as_i32(s1_t[r:P:32]), w1_scales[:, :, r:16:4, :].rearrange("e g f k -> f (e g) k").bitcast(I32)
             )
-        load_pre(4)
-        load_gate(3)
-        load_pre(5)
-        load_w2(6)
-        load_pre(6)
-        load_pre(7)
         nc.sync.dma_start(pos1_t[:], pos1)
         nc.sync.dma_start(pos2_t[:], pos2)
 
-        g_codes, da_codes, grouped, pairs = {}, {}, {}, {}
+        g_codes, da_codes, grouped, pairs, spread = {}, {}, {}, {}, {}
 
-        def window(q, t):
-            return dy[t][:].indirect(offs_t[:, q * PIECE // 16 : (q + 1) * PIECE // 16])
+        def window(first, width, t):
+            return dy[t][:].indirect(offs_t[:, first // 16 : (first + width) // 16])
 
-        def plain_gathers(q):
+        def plain_gathers(e, count, place):
+            rows = keep.tile([P, PACK, count * C], F32, name=place, align_bytes=64)
+            for j in range(count):
+                planes[e + j] = rows[:, :, j * C : (j + 1) * C]
             for t in range(PACK):
-                nc.scalar.activation(planes[q][:, t, :], window(q, t), COPY)
+                nc.scalar.activation(rows[:, t, :], window(e * C, count * C, t), COPY)
 
-        def gated_gather(q, t):
-            nc.vector.tensor_tensor(planes[q][:, t, :], window(q, t), gates[q][:], MULT)
+        def gated_gathers(e):
+            rows = keep.tile([P, PACK, PIECE], F32, name="gated", align_bytes=64)
+            for j in range(2):
+                planes[e + j] = rows[:, :, j * C : (j + 1) * C]
+            for t in range(PACK):
+                nc.vector.tensor_tensor(rows[:, t, :], window(e * C, PIECE, t), gates[:], MULT)
 
         def turn_scales():
             nc.vector.tensor_copy(
@@ -155,37 +170,31 @@ def tile_moe_bdx_mlp_relu_kernel(
                 )
 
         def round_g(e):
-            q, first = e // 2, e % 2 * C
-            nc.scalar.copy(
-                grouped[q][:, first : first + C, :].rearrange("p (c i) (u e) -> p c u i e", i=4, u=2),
-                planes[q][:, :, first : first + C].rearrange("p (u e) (c i) -> p c u i e", i=4, u=2),
-            )
+            nc.gpsimd.tensor_copy(grouped[e], planes[e].rearrange("p t s -> p s t"))
 
-        def gate_g(e):
-            q, first = e // 2, e % 2 * C
-            nc.vector.tensor_tensor(
-                grouped[q][:, first : first + C, :].rearrange("p (c i) t -> p c t i", i=4),
-                planes[q][:, :, first : first + C].rearrange("p t (c i) -> p c t i", i=4),
-                gates[q][:, first : first + C].rearrange("p (c i) -> p c i", i=4).unsqueeze(2).to_broadcast([P, C // 4, PACK, 4]),
+        def spread_gates(experts, columns, bank):
+            both = psum.tile([P, 2, 2, P], F32, name=f"bank{bank}")
+            for j, e in enumerate(experts):
+                spread[e] = both[:, j].rearrange("p i c -> p c i")
+                for i in range(2):
+                    nc.tensor.transpose(both[:, j, i, :], columns[:, j, i : i + 1].to_broadcast([P, P]), ident[:])
+
+        def gate_g(engine, e, gate_view):
+            n = gate_view.shape[2]
+            engine.tensor_tensor(
+                grouped[e].rearrange("p (c i) t -> p c t i", i=n),
+                planes[e].rearrange("p t (c i) -> p c t i", i=n),
+                gate_view.unsqueeze(2).to_broadcast([P, C // n, PACK, n]),
                 MULT,
             )
 
-        def quantise(source, codes, label, q, first, width, place):
-            words = keep.tile([P, width], U32, name=place or f"{label}_words{q}_{first}", align_bytes=64)
-            scales = keep.tile([P, width], U8, name=f"{label}_scales{q}_{first}", align_bytes=64)
+        def quantise(source, codes, e, name):
+            width = source.shape[1]
+            words = keep.tile([P, width], U32, name=name, align_bytes=64)
+            scales = keep.tile([P, width], U8, name=f"scales_in_{name}_{e}", align_bytes=64)
             for start in range(0, width, C):
-                codes[2 * q + (first + start) // C] = (words[:, start : start + C], scales[:, start : start + C])
-            nc.vector.quantize_mx(
-                out=words[:].bitcast(FP8X4),
-                scales=scales[:],
-                in_=source[q][:, first : first + width, :].rearrange("p s t -> p (s t)"),
-            )
-
-        def quantise_g(q, first=0, width=PIECE):
-            quantise(grouped, g_codes, "g", q, first, width, None)
-
-        def quantise_da(q, first=0, width=PIECE, place=None):
-            quantise(da, da_codes, "da", q, first, width, place)
+                codes[e + start // C] = (words[:, start : start + C], scales[:, start : start + C])
+            nc.vector.quantize_mx(out=words[:].bitcast(FP8X4), scales=scales[:], in_=source.rearrange("p s t -> p (s t)"))
 
         def make_da(e, half):
             bank = psum.tile([P, PACK, CHUNK], F32, name=f"bank{(2 * e + half) % 4}")
@@ -224,7 +233,7 @@ def tile_moe_bdx_mlp_relu_kernel(
                     stop=True,
                 )
             if e // 2 not in pairs:
-                pairs[e // 2] = keep.tile([P, 2, 2, C, 2], BF16, name=f"pairs{e // 2}")
+                pairs[e // 2] = keep.tile([P, 2, 2, C, 2], BF16, name=f"pairs{e // 2}", align_bytes=64)
             nc.vector.scalar_tensor_tensor(
                 pairs[e // 2][:, e % 2, u],
                 pre[e][:, 2 * u : 2 * u + 2, :].rearrange("p j s -> p s j"),
@@ -256,67 +265,75 @@ def tile_moe_bdx_mlp_relu_kernel(
 
         def second_products(q):
             for k in range(2):
-                second_product(k, q, 0, PIECE, 4 + 2 * (q % 2) + k, nc.scalar.copy)
+                second_product(k, q, 0, PIECE, ((4, 7), (5, 6))[q % 2][k], nc.scalar.copy)
 
-        for q in range(2):
-            grouped[q] = keep.tile([P, PIECE, PACK], BF16, name=f"grouped{q}", align_bytes=64)[:]
-        grouped[2] = as_words(pre[2][:])
-        grouped[3] = as_words(pre[4][:])
+        def words_tile(name, width):
+            return keep.tile([P, width, PACK], BF16, name=name, align_bytes=64)
+
+        rounded = words_tile("rounded", PIECE)
+        grouped.update({0: words_tile("grouped0", C)[:], 1: words_tile("grouped1", C)[:], 2: rounded[:, 0:C, :], 3: rounded[:, C:PIECE, :]})
+        for q in (0, 2, 3):
+            da[q] = words_tile(f"da{q}", PIECE)
 
         turn_words(0)
         turn_scales()
-        plain_gathers(0)
-        for t in range(PACK):
-            gated_gather(1, t)
+        spread_gates((0, 1), gate_cols[0], 4)
+        plain_gathers(0, 2, "plain")
+        gated_gathers(2)
         turn_words(1)
-        gate_g(0)
-        gate_g(1)
         round_g(2)
         round_g(3)
-        quantise_g(0, 0, C)
-        quantise_g(0, C, C)
+        gate_g(nc.vector, 0, spread[0])
+        gate_g(nc.vector, 1, spread[1])
+        quantise(grouped[0], g_codes, 0, "g_words0")
+        quantise(grouped[1], g_codes, 1, "g_words1")
         turn_words(2)
-        planes.append(planes[0])
-        plain_gathers(2)
-        quantise_g(1)
-        turn_bytes(4, "grouped1")
+        spread_gates((5, 7), gate_cols[1], 5)
+        plain_gathers(4, 2, "w2_raw2")
+        quantise(rounded[:], g_codes, 2, "g_words2")
+        turn_bytes(4, "rounded")
         for e in range(4):
             make_pairs(e, 0)
             make_pairs(e, 1)
-        planes.append(keep.tile([P, PACK, PIECE], F32, name="planes1", align_bytes=64))
-        plain_gathers(3)
-        gate_g(4)
-        gate_g(5)
-        quantise_g(2, 0, C)
-        quantise_g(2, C, C)
-        for q, place in enumerate(("dy2", "dy3", "da2", "da3")):
-            da[q] = keep.tile([P, PIECE, PACK], BF16, name=place, align_bytes=64)
+        grouped[4] = words_tile("grouped4", C)[:]
+        gate_g(nc.gpsimd, 4, gate_rows[4][:].rearrange("p (c i) -> p c i", i=WALK))
+        plain_gathers(6, 1, "gated")
         weave(0)
+        turn_words(6)
+        plain_gathers(7, 1, "w2_raw6")
+        grouped[5] = as_words(pre[3][:])[:, 0:C, :]
+        gate_g(nc.vector, 5, spread[5])
+        quantise(grouped[4], g_codes, 4, "pre2")
+        quantise(grouped[5], g_codes, 5, "g_words5")
+        quantise(da[0][:], da_codes, 0, "grouped4")
+        grouped[6] = words_tile("da0", C)[:]
+        gate_g(nc.gpsimd, 6, gate_rows[6][:].rearrange("p (c i) -> p c i", i=WALK))
+        da[1] = words_tile("dy3", PIECE)
         weave(1)
-        turn_bytes(6, "pre2")
         for e in (4, 5):
             make_pairs(e, 0)
             make_pairs(e, 1)
         weave(2)
-        gate_g(6)
-        gate_g(7)
-        quantise_g(3, 0, C)
-        quantise_da(0, place="planes1")
-        quantise_g(3, C, C)
-        quantise_da(1, place="gates3")
+        dx.append(keep.tile([P, S], F32, name="pairs2", align_bytes=64))
+        dx.append(keep.tile([P, S], F32, name="dx1"))
         second_products(0)
-        make_pairs(6, 0)
-        quantise_da(2, place="pre4")
-        make_pairs(6, 1)
-        weave(3, 1)
+        grouped[7] = as_words(pre[5][:])[:, 0:C, :]
+        gate_g(nc.vector, 7, spread[7])
+        quantise(grouped[6], g_codes, 6, "g_words6")
+        quantise(da[1][:], da_codes, 2, "w2_raw6")
+        quantise(grouped[7], g_codes, 7, "g_words7")
+        quantise(da[2][:], da_codes, 4, "pre5")
         second_products(1)
-        make_da(7, 0)
-        quantise_da(3, 0, C)
-        make_da(7, 1)
+        make_pairs(6, 0)
+        make_pairs(6, 1)
         second_products(2)
-        quantise_da(3, C, C)
-        second_product(0, 3, 0, C, 6, nc.scalar.copy)
-        second_product(1, 3, 0, C, 7, nc.scalar.copy)
+        weave(3, 1)
+        make_da(7, 0)
+        quantise(da[3][:, 0:C, :], da_codes, 6, "da_words6")
+        make_da(7, 1)
+        quantise(da[3][:, C:PIECE, :], da_codes, 7, "da_words7")
+        second_product(0, 3, 0, C, 5, nc.vector.tensor_copy)
+        second_product(1, 3, 0, C, 6, nc.scalar.copy)
         second_product(0, 3, C, C, 0, nc.vector.tensor_copy)
         second_product(1, 3, C, C, 1, nc.scalar.copy)
 

@@ -20,6 +20,7 @@ MULT = mybir.AluOpType.mult
 ADD = mybir.AluOpType.add
 IS_GT = mybir.AluOpType.is_gt
 COPY = mybir.ActivationFunctionType.Copy
+SIGN = mybir.ActivationFunctionType.Sign
 
 FLOPS = 2 * S * (N * H + H * K)
 BYTES = 4 * N * T + 4 * H * S + E * (N * H + H * K) * 17 // 32 + 4 * S + 2 * S + 2 * 2 * T + 4 * K * T
@@ -28,11 +29,8 @@ PIECE = 512
 PIECES = S // PIECE
 CHUNK = 128
 GROUPS = ((0, 1), (1, 1), (2, 2), (4, 2), (6, 2))
-WALK = 4
-SHARES = (
-    ((0, 192), (192, 256), (448, 320), (768, 256)),
-    ((0, 320), (320, 320), (640, 256), (896, 128)),
-)
+WALK = 1
+SHARES = (((0, 128), (128, 448), (576, 448)), ((0, 448), (448, 448), (896, 128)))
 
 
 def tile_moe_bdx_mlp_relu_kernel(
@@ -50,7 +48,8 @@ def tile_moe_bdx_mlp_relu_kernel(
 
         dy = [keep.tile([P, T], F32, name=f"dy{t}", align_bytes=64) for t in range(PACK)]
         gates = keep.tile([P, PIECE], F32, name="gates", align_bytes=64)
-        gate_cols = [keep.tile([P, 2, 2], F32, name=f"gate_cols{j}") for j in range(2)]
+        gate_quads = keep.tile([P, 1, PACK], F32, name="gate_quads")
+        gate_cols = keep.tile([P, 2, 2], F32, name="gate_cols")
         gate_rows = {e: keep.tile([P, C], F32, name=f"gate_rows{e}") for e in (4, 6)}
         ident = keep.tile([P, P], F32, name="ident")
         pre = [keep.tile([P, PACK, C], F32, name=f"pre{e}", align_bytes=64) for e in range(E)]
@@ -95,11 +94,11 @@ def tile_moe_bdx_mlp_relu_kernel(
         nc.sync.dma_start(s2_raw[:].bitcast(I32), w2_scales.rearrange("e g f i -> f (e g) i").bitcast(I32))
         nc.sync.dma_start(offs_t[:], offs)
         nc.sync.dma_start(dy[0][:], dyT_rows[:, 0, :])
-        nc.sync.dma_start(gates[:], gate[0:P, PIECE : 2 * PIECE])
-        nc.sync.dma_start(gate_cols[0][:], gate_pairs[:, 0:2, :])
+        nc.sync.dma_start(gates[:], gate[0:P, 0:PIECE])
+        nc.sync.dma_start(gate_quads[:], gate[0:1, PIECE : 2 * PIECE].rearrange("o (p c) -> p o c", p=P))
         for t in range(1, PACK):
             nc.sync.dma_start(dy[t][:], dyT_rows[:, t, :])
-        nc.sync.dma_start(gate_cols[1][:], gate_pairs[:, 5:8:2, :])
+        nc.sync.dma_start(gate_cols[:], gate_pairs[:, 5:8:2, :])
         load_w2(1)
         load_w2(2)
         load_pre(0)
@@ -130,6 +129,7 @@ def tile_moe_bdx_mlp_relu_kernel(
             rows = keep.tile([P, PACK, count * C], F32, name=place, align_bytes=64)
             for j in range(count):
                 planes[e + j] = rows[:, :, j * C : (j + 1) * C]
+            planes[e, count] = rows[:]
             for t in range(PACK):
                 nc.scalar.activation(rows[:, t, :], window(e * C, count * C, t), COPY)
 
@@ -172,19 +172,19 @@ def tile_moe_bdx_mlp_relu_kernel(
         def round_g(e):
             nc.gpsimd.tensor_copy(grouped[e], planes[e].rearrange("p t s -> p s t"))
 
-        def spread_gates(experts, columns, bank):
-            both = psum.tile([P, 2, 2, P], F32, name=f"bank{bank}")
-            for j, e in enumerate(experts):
-                spread[e] = both[:, j].rearrange("p i c -> p c i")
-                for i in range(2):
-                    nc.tensor.transpose(both[:, j, i, :], columns[:, j, i : i + 1].to_broadcast([P, P]), ident[:])
+        def spread_gates(columns, bank):
+            n = columns.shape[1]
+            spread = psum.tile([P, n, P], F32, name=f"bank{bank}")
+            for i in range(n):
+                nc.tensor.transpose(spread[:, i, :], columns[:, i : i + 1].to_broadcast([P, P]), ident[:])
+            return spread[:].rearrange("p i c -> p c i")
 
-        def gate_g(engine, e, gate_view):
-            n = gate_view.shape[2]
+        def gate_g(engine, into, rows, gate_view):
+            steps, n = gate_view.shape[1], gate_view.shape[2]
             engine.tensor_tensor(
-                grouped[e].rearrange("p (c i) t -> p c t i", i=n),
-                planes[e].rearrange("p t (c i) -> p c t i", i=n),
-                gate_view.unsqueeze(2).to_broadcast([P, C // n, PACK, n]),
+                into.rearrange("p (c i) t -> p c t i", i=n),
+                rows.rearrange("p t (c i) -> p c t i", i=n),
+                gate_view.unsqueeze(2).to_broadcast([P, steps, PACK, n]),
                 MULT,
             )
 
@@ -196,7 +196,7 @@ def tile_moe_bdx_mlp_relu_kernel(
                 codes[e + start // C] = (words[:, start : start + C], scales[:, start : start + C])
             nc.vector.quantize_mx(out=words[:].bitcast(FP8X4), scales=scales[:], in_=source.rearrange("p s t -> p (s t)"))
 
-        def make_da(e, half):
+        def make_da(e, half, signs):
             bank = psum.tile([P, PACK, CHUNK], F32, name=f"bank{(2 * e + half) % 4}")
             cols = slice(half * CHUNK, (half + 1) * CHUNK)
             for t in range(PACK):
@@ -212,7 +212,7 @@ def tile_moe_bdx_mlp_relu_kernel(
             first = e % 2 * C + half * CHUNK
             nc.vector.scalar_tensor_tensor(
                 da[e // 2][:, first : first + CHUNK, :],
-                pre[e][:, :, cols].rearrange("p t s -> p s t"),
+                signs[:, cols, :],
                 0.0,
                 bank[:].rearrange("p t s -> p s t"),
                 IS_GT,
@@ -243,14 +243,14 @@ def tile_moe_bdx_mlp_relu_kernel(
                 MULT,
             )
 
-        def weave(q, count=2):
+        def weave(q, count=2, copy=nc.scalar.copy):
             words = da[q][:].rearrange("p s t -> p (s t)").bitcast(U32).rearrange("p (e s u) -> p e s u", e=2, u=2)
             halves = pairs[q][:].rearrange("p e u s j -> p (e u s j)").bitcast(U32).rearrange("p (e u s) -> p e s u", e=2, u=2)
-            nc.scalar.copy(words[:, 0:count], halves[:, 0:count])
+            copy(words[:, 0:count], halves[:, 0:count])
 
-        def second_product(k, q, first, width, bank, copy):
+        def second_product(k, q, first, width, bank, copy, step=1):
             acc = psum.tile([P, PIECE], F32, name=f"bank{bank}")
-            for start in range(first, first + width, C):
+            for start in range(first, first + width, C)[::step]:
                 e = 2 * q + start // C
                 nc.tensor.matmul_mx(
                     out=acc[:, start : start + C],
@@ -265,60 +265,64 @@ def tile_moe_bdx_mlp_relu_kernel(
 
         def second_products(q):
             for k in range(2):
-                second_product(k, q, 0, PIECE, ((4, 7), (5, 6))[q % 2][k], nc.scalar.copy)
+                second_product(k, q, 0, PIECE, ((4, 7), (5, 6), (0, 1))[q][k], nc.scalar.copy)
 
         def words_tile(name, width):
             return keep.tile([P, width, PACK], BF16, name=name, align_bytes=64)
 
         rounded = words_tile("rounded", PIECE)
-        grouped.update({0: words_tile("grouped0", C)[:], 1: words_tile("grouped1", C)[:], 2: rounded[:, 0:C, :], 3: rounded[:, C:PIECE, :]})
+        grouped.update({0: rounded[:, 0:C, :], 1: rounded[:, C:PIECE, :]})
         for q in (0, 2, 3):
             da[q] = words_tile(f"da{q}", PIECE)
 
         turn_words(0)
         turn_scales()
-        spread_gates((0, 1), gate_cols[0], 4)
-        plain_gathers(0, 2, "plain")
-        gated_gathers(2)
+        spread[2] = spread_gates(gate_quads[:, 0, :], 4)
+        plain_gathers(2, 2, "plain")
+        gated_gathers(0)
         turn_words(1)
-        round_g(2)
-        round_g(3)
-        gate_g(nc.vector, 0, spread[0])
-        gate_g(nc.vector, 1, spread[1])
-        quantise(grouped[0], g_codes, 0, "g_words0")
-        quantise(grouped[1], g_codes, 1, "g_words1")
+        round_g(0)
+        round_g(1)
+        product = words_tile("product", PIECE)
+        gate_g(nc.vector, product[:], planes[2, 2], spread[2])
+        quantise(rounded[:], g_codes, 0, "g_words0")
+        quantise(product[:], g_codes, 2, "g_words2")
         turn_words(2)
-        spread_gates((5, 7), gate_cols[1], 5)
+        spread[5] = spread_gates(gate_cols[:, 0, :], 5)
+        spread[7] = spread_gates(gate_cols[:, 1, :], 6)
         plain_gathers(4, 2, "w2_raw2")
-        quantise(rounded[:], g_codes, 2, "g_words2")
-        turn_bytes(4, "rounded")
+        turn_bytes(4, "product")
         for e in range(4):
             make_pairs(e, 0)
             make_pairs(e, 1)
         grouped[4] = words_tile("grouped4", C)[:]
-        gate_g(nc.gpsimd, 4, gate_rows[4][:].rearrange("p (c i) -> p c i", i=WALK))
+        gate_g(nc.gpsimd, grouped[4], planes[4], gate_rows[4][:].rearrange("p (c i) -> p c i", i=WALK))
         plain_gathers(6, 1, "gated")
         weave(0)
         turn_words(6)
         plain_gathers(7, 1, "w2_raw6")
         grouped[5] = as_words(pre[3][:])[:, 0:C, :]
-        gate_g(nc.vector, 5, spread[5])
+        gate_g(nc.vector, grouped[5], planes[5], spread[5])
         quantise(grouped[4], g_codes, 4, "pre2")
         quantise(grouped[5], g_codes, 5, "g_words5")
         quantise(da[0][:], da_codes, 0, "grouped4")
         grouped[6] = words_tile("da0", C)[:]
-        gate_g(nc.gpsimd, 6, gate_rows[6][:].rearrange("p (c i) -> p c i", i=WALK))
+        gate_g(nc.gpsimd, grouped[6], planes[6], gate_rows[6][:].rearrange("p (c i) -> p c i", i=WALK))
         da[1] = words_tile("dy3", PIECE)
         weave(1)
         for e in (4, 5):
             make_pairs(e, 0)
             make_pairs(e, 1)
         weave(2)
-        dx.append(keep.tile([P, S], F32, name="pairs2", align_bytes=64))
+        signs = words_tile("pairs2", C)
+        nc.scalar.activation(
+            signs[:].rearrange("p (c i) t -> p c t i", i=4), pre[7][:].rearrange("p t (c i) -> p c t i", i=4), SIGN
+        )
+        dx.append(keep.tile([P, S], F32, name="pre7", align_bytes=64))
         dx.append(keep.tile([P, S], F32, name="dx1"))
         second_products(0)
         grouped[7] = as_words(pre[5][:])[:, 0:C, :]
-        gate_g(nc.vector, 7, spread[7])
+        gate_g(nc.vector, grouped[7], planes[7], spread[7])
         quantise(grouped[6], g_codes, 6, "g_words6")
         quantise(da[1][:], da_codes, 2, "w2_raw6")
         quantise(grouped[7], g_codes, 7, "g_words7")
@@ -327,15 +331,14 @@ def tile_moe_bdx_mlp_relu_kernel(
         make_pairs(6, 0)
         make_pairs(6, 1)
         second_products(2)
-        weave(3, 1)
-        make_da(7, 0)
-        quantise(da[3][:, 0:C, :], da_codes, 6, "da_words6")
-        make_da(7, 1)
+        weave(3, 1, nc.gpsimd.tensor_copy)
+        make_da(7, 0, signs)
+        make_da(7, 1, signs)
+        quantise(da[3][:, 0:C, :], da_codes, 6, "pairs2")
         quantise(da[3][:, C:PIECE, :], da_codes, 7, "da_words7")
-        second_product(0, 3, 0, C, 5, nc.vector.tensor_copy)
-        second_product(1, 3, 0, C, 6, nc.scalar.copy)
-        second_product(0, 3, C, C, 0, nc.vector.tensor_copy)
-        second_product(1, 3, C, C, 1, nc.scalar.copy)
+        second_product(0, 3, 0, C, 3, nc.vector.tensor_copy)
+        second_product(0, 3, C, C, 2, nc.vector.tensor_copy)
+        second_product(1, 3, 0, PIECE, 6, nc.vector.tensor_copy, step=-1)
 
         for k in range(2):
             for first, width in SHARES[k]:

@@ -48,7 +48,7 @@ def tile_moe_bdx_mlp_relu_kernel(
 
         dy = [keep.tile([P, T], F32, name=f"dy{t}", align_bytes=64) for t in range(PACK)]
         gates = keep.tile([P, PIECE], F32, name="gates", align_bytes=64)
-        gate_quads = keep.tile([P, 1, PACK], F32, name="gate_quads")
+        gate_quads = keep.tile([P, 2, PACK], F32, name="gate_quads")
         gate_cols = keep.tile([P, 2, 2], F32, name="gate_cols")
         gate_rows = {e: keep.tile([P, C], F32, name=f"gate_rows{e}") for e in (4, 6)}
         ident = keep.tile([P, P], F32, name="ident")
@@ -90,15 +90,15 @@ def tile_moe_bdx_mlp_relu_kernel(
             n = w2_raw[e].shape[1]
             nc.sync.dma_start(as_i32(w2_raw[e][:]), w2_words[e : e + n].bitcast(I32).rearrange("e g p b -> p (e g) b"))
 
+        nc.sync.dma_start(gate_quads[:], gate[0:1, 0 : 2 * PIECE].rearrange("o (q p c) -> p (o q) c", p=P, c=PACK))
         load_w2(0)
         nc.sync.dma_start(s2_raw[:].bitcast(I32), w2_scales.rearrange("e g f i -> f (e g) i").bitcast(I32))
         nc.sync.dma_start(offs_t[:], offs)
         nc.sync.dma_start(dy[0][:], dyT_rows[:, 0, :])
-        nc.sync.dma_start(gates[:], gate[0:P, 0:PIECE])
-        nc.sync.dma_start(gate_quads[:], gate[0:1, PIECE : 2 * PIECE].rearrange("o (p c) -> p o c", p=P))
+        nc.sync.dma_start(gate_cols[:], gate_pairs[:, 5:8:2, :])
+        nc.sync.dma_start(pos1_t[:], pos1)
         for t in range(1, PACK):
             nc.sync.dma_start(dy[t][:], dyT_rows[:, t, :])
-        nc.sync.dma_start(gate_cols[:], gate_pairs[:, 5:8:2, :])
         load_w2(1)
         load_w2(2)
         load_pre(0)
@@ -117,7 +117,6 @@ def tile_moe_bdx_mlp_relu_kernel(
             nc.sync.dma_start(
                 as_i32(s1_t[r:P:32]), w1_scales[:, :, r:16:4, :].rearrange("e g f k -> f (e g) k").bitcast(I32)
             )
-        nc.sync.dma_start(pos1_t[:], pos1)
         nc.sync.dma_start(pos2_t[:], pos2)
 
         g_codes, da_codes, grouped, pairs, spread = {}, {}, {}, {}, {}
@@ -145,7 +144,7 @@ def tile_moe_bdx_mlp_relu_kernel(
                 s2_mid[:].rearrange("p (t m) -> p t m", t=PACK), s2_raw[:].rearrange("p (m t) -> p t m", t=PACK)
             )
             for quad in range(4):
-                (nc.scalar, nc.gpsimd)[quad % 2].dma_start(as_i32(s2_t[32 * quad : 32 * quad + 4]), s2_mid[32 * quad : 32 * quad + 32].bitcast(I32))
+                (nc.gpsimd if quad else nc.scalar).dma_start(as_i32(s2_t[32 * quad : 32 * quad + 4]), s2_mid[32 * quad : 32 * quad + 32].bitcast(I32))
 
         def turned_tile(e, place):
             n = w2_raw[e].shape[1]
@@ -277,7 +276,8 @@ def tile_moe_bdx_mlp_relu_kernel(
 
         turn_words(0)
         turn_scales()
-        spread[2] = spread_gates(gate_quads[:, 0, :], 4)
+        nc.vector.tensor_copy(gates[:].rearrange("p (c i) -> p c i", i=PACK), spread_gates(gate_quads[:, 0, :], 6))
+        spread[2] = spread_gates(gate_quads[:, 1, :], 4)
         plain_gathers(2, 2, "plain")
         gated_gathers(0)
         turn_words(1)

from contextlib import ExitStack

import concourse.mybir as mybir
from concourse.masks import make_identity

K, T, E, C, H, N = 256, 1024, 8, 256, 512, 512
S = E * C
P = 128
PACK = 4

F32 = mybir.dt.float32
BF16 = mybir.dt.bfloat16
I32 = mybir.dt.int32
U32 = mybir.dt.uint32
U16 = mybir.dt.uint16
U8 = mybir.dt.uint8
FP8X4 = mybir.dt.float8_e4m3fn_x4
FP4X4 = mybir.dt.float4_e2m1fn_x4
MULT = mybir.AluOpType.mult
ADD = mybir.AluOpType.add
IS_GT = mybir.AluOpType.is_gt
COPY = mybir.ActivationFunctionType.Copy
SIGN = mybir.ActivationFunctionType.Sign

FLOPS = 2 * S * (N * H + H * K)
BYTES = 4 * N * T + 4 * H * S + E * (N * H + H * K) * 17 // 32 + 4 * S + 2 * S + 2 * 2 * T + 4 * K * T

PIECE = 512
PIECES = S // PIECE
CHUNK = 128
GROUPS = ((0, 1), (1, 1), (2, 2), (4, 2), (6, 2))
WALK = 1
SHARES = (((0, 128), (128, 448), (576, 448)), ((0, 448), (448, 448), (896, 128)))


def tile_moe_bdx_mlp_relu_kernel(
    tc, dyT, a, w2_words, w2_scales, w1_words, w1_scales, gate, offs, pos1, pos2, out
):
    nc = tc.nc
    with ExitStack() as ctx:
        lists = ctx.enter_context(tc.tile_pool(name="lists", bufs=1))
        keep = ctx.enter_context(tc.tile_pool(name="keep", bufs=1))
        psum = ctx.enter_context(tc.psum_pool(name="psum", bufs=1))

        offs_t = lists.tile([P, S // 16], U16, name="offs_t")
        pos1_t = lists.tile([P, T // 16], U16, name="pos1_t")
        pos2_t = lists.tile([P, T // 16], U16, name="pos2_t")

        dy = [keep.tile([P, T], F32, name=f"dy{t}", align_bytes=64) for t in range(PACK)]
        gates = keep.tile([P, PIECE], F32, name="gates", align_bytes=64)
        gate_quads = keep.tile([P, 2, PACK], F32, name="gate_quads")
        gate_cols = keep.tile([P, 2, 2], F32, name="gate_cols")
        gate_rows = {e: keep.tile([P, C], F32, name=f"gate_rows{e}") for e in (4, 6)}
        ident = keep.tile([P, P], F32, name="ident")
        pre = [keep.tile([P, PACK, C], F32, name=f"pre{e}", align_bytes=64) for e in range(E)]
        w2_raw = {e: keep.tile([P, n, 2 * H], U8, name=f"w2_raw{e}", align_bytes=64) for e, n in GROUPS}
        w2_t = {}
        s2_raw = keep.tile([P, H], U8, name="s2_raw")
        s2_mid = keep.tile([P, H], U8, name="s2_mid")
        s2_t = keep.tile([P, E, H], U8, name="s2_t", align_bytes=64)
        w1_t = keep.tile([P, E, 2 * K], U8, name="w1_t", align_bytes=64)
        s1_t = keep.tile([P, E, K], U8, name="s1_t", align_bytes=64)
        dx = []
        planes = {}
        da = {}

        make_identity(nc, ident[:])
        nc.gpsimd.memset(s2_t[:].rearrange("p e i -> p (e i)").bitcast(I32), 0)
        nc.gpsimd.memset(s1_t[:].rearrange("p e i -> p (e i)").bitcast(I32), 0)

        dyT_rows = dyT.rearrange("(p t) n -> p t n", t=PACK)
        a_rows = a.rearrange("(p t) s -> p t s", t=PACK)

        def as_i32(view):
            e = view.shape[1]
            return view.rearrange("p e i -> p (e i)").bitcast(I32).rearrange("p (e i) -> p e i", e=e)

        def as_words(view):
            return view.rearrange("p t s -> p (t s)").bitcast(BF16).rearrange("p (s t) -> p s t", t=PACK)

        gate_pairs = gate[0:1, :].rearrange("o (e p c) -> p (o e) c", p=P, c=2)

        def load_gate_rows(e):
            nc.sync.dma_start(gate_rows[e][:], gate[0:P, e * C : (e + 1) * C])

        def load_pre(e):
            nc.sync.dma_start(pre[e][:], a_rows[:, :, e * C : (e + 1) * C])

        def load_w2(e):
            n = w2_raw[e].shape[1]
            nc.sync.dma_start(as_i32(w2_raw[e][:]), w2_words[e : e + n].bitcast(I32).rearrange("e g p b -> p (e g) b"))

        nc.sync.dma_start(gate_quads[:], gate[0:1, 0 : 2 * PIECE].rearrange("o (q p c) -> p (o q) c", p=P, c=PACK))
        load_w2(0)
        nc.sync.dma_start(s2_raw[:].bitcast(I32), w2_scales.rearrange("e g f i -> f (e g) i").bitcast(I32))
        nc.sync.dma_start(offs_t[:], offs)
        nc.sync.dma_start(dy[0][:], dyT_rows[:, 0, :])
        nc.sync.dma_start(gate_cols[:], gate_pairs[:, 5:8:2, :])
        nc.sync.dma_start(pos1_t[:], pos1)
        for t in range(1, PACK):
            nc.sync.dma_start(dy[t][:], dyT_rows[:, t, :])
        load_w2(1)
        load_w2(2)
        load_pre(0)
        load_w2(4)
        load_pre(1)
        load_pre(2)
        load_gate_rows(4)
        load_pre(3)
        load_pre(4)
        load_gate_rows(6)
        load_w2(6)
        for e in range(5, E):
            load_pre(e)
        nc.sync.dma_start(as_i32(w1_t[:]), w1_words.rearrange("e g p b -> p (e g) b").bitcast(I32))
        for r in range(4):
            nc.sync.dma_start(
                as_i32(s1_t[r:P:32]), w1_scales[:, :, r:16:4, :].rearrange("e g f k -> f (e g) k").bitcast(I32)
            )
        nc.sync.dma_start(pos2_t[:], pos2)

        g_codes, da_codes, grouped, pairs, spread = {}, {}, {}, {}, {}

        def window(first, width, t):
            return dy[t][:].indirect(offs_t[:, first // 16 : (first + width) // 16])

        def plain_gathers(e, count, place):
            rows = keep.tile([P, PACK, count * C], F32, name=place, align_bytes=64)
            for j in range(count):
                planes[e + j] = rows[:, :, j * C : (j + 1) * C]
            planes[e, count] = rows[:]
            for t in range(PACK):
                nc.scalar.activation(rows[:, t, :], window(e * C, count * C, t), COPY)

        def gated_gathers(e):
            rows = keep.tile([P, PACK, PIECE], F32, name="gated", align_bytes=64)
            for j in range(2):
                planes[e + j] = rows[:, :, j * C : (j + 1) * C]
            for t in range(PACK):
                nc.vector.tensor_tensor(rows[:, t, :], window(e * C, PIECE, t), gates[:], MULT)

        def turn_scales():
            nc.vector.tensor_copy(
                s2_mid[:].rearrange("p (t m) -> p t m", t=PACK), s2_raw[:].rearrange("p (m t) -> p t m", t=PACK)
            )
            for quad in range(4):
                (nc.gpsimd if quad else nc.scalar).dma_start(as_i32(s2_t[32 * quad : 32 * quad + 4]), s2_mid[32 * quad : 32 * quad + 32].bitcast(I32))

        def turned_tile(e, place):
            n = w2_raw[e].shape[1]
            turned = keep.tile([P, n, 2 * H], U8, name=place, align_bytes=64)
            for j in range(n):
                w2_t[e + j] = turned[:, j, :]
            return turned

        def turn_words(e):
            n = w2_raw[e].shape[1]
            nc.scalar.copy(
                turned_tile(e, f"w2_t{e}")[:].rearrange("p e b -> p (e b)").bitcast(U16).rearrange("p (e t m) -> p e t m", e=n, t=PACK),
                w2_raw[e][:].rearrange("p e b -> p (e b)").bitcast(U16).rearrange("p (e m t) -> p e t m", e=n, t=PACK),
            )

        def turn_bytes(e, place):
            turned = turned_tile(e, place)
            for j in range(2):
                nc.gpsimd.tensor_copy(
                    turned[:, j, :].rearrange("p (t m b) -> p t m b", t=PACK, b=2),
                    w2_raw[e][:, j, :].rearrange("p (m t b) -> p t m b", t=PACK, b=2),
                )

        def round_g(e):
            nc.gpsimd.tensor_copy(grouped[e], planes[e].rearrange("p t s -> p s t"))

        def spread_gates(columns, bank):
            n = columns.shape[1]
            spread = psum.tile([P, n, P], F32, name=f"bank{bank}")
            for i in range(n):
                nc.tensor.transpose(spread[:, i, :], columns[:, i : i + 1].to_broadcast([P, P]), ident[:])
            return spread[:].rearrange("p i c -> p c i")

        def gate_g(engine, into, rows, gate_view):
            steps, n = gate_view.shape[1], gate_view.shape[2]
            engine.tensor_tensor(
                into.rearrange("p (c i) t -> p c t i", i=n),
                rows.rearrange("p t (c i) -> p c t i", i=n),
                gate_view.unsqueeze(2).to_broadcast([P, steps, PACK, n]),
                MULT,
            )

        def quantise(source, codes, e, name):
            width = source.shape[1]
            words = keep.tile([P, width], U32, name=name, align_bytes=64)
            scales = keep.tile([P, width], U8, name=f"scales_in_{name}_{e}", align_bytes=64)
            for start in range(0, width, C):
                codes[e + start // C] = (words[:, start : start + C], scales[:, start : start + C])
            nc.vector.quantize_mx(out=words[:].bitcast(FP8X4), scales=scales[:], in_=source.rearrange("p s t -> p (s t)"))

        def make_da(e, half, signs):
            bank = psum.tile([P, PACK, CHUNK], F32, name=f"bank{(2 * e + half) % 4}")
            cols = slice(half * CHUNK, (half + 1) * CHUNK)
            for t in range(PACK):
                nc.tensor.matmul_mx(
                    out=bank[:, t, :],
                    lhsT=w2_t[e][:, t * 2 * P : (t + 1) * 2 * P].bitcast(FP4X4),
                    lhsT_scale=s2_t[:, e, t * P : (t + 1) * P],
                    rhs=g_codes[e][0][:, cols].bitcast(FP8X4),
                    rhs_scale=g_codes[e][1][:, cols],
                    start=True,
                    stop=True,
                )
            first = e % 2 * C + half * CHUNK
            nc.vector.scalar_tensor_tensor(
                da[e // 2][:, first : first + CHUNK, :],
                signs[:, cols, :],
                0.0,
                bank[:].rearrange("p t s -> p s t"),
                IS_GT,
                MULT,
            )

        def make_pairs(e, u):
            bank = psum.tile([P, 2, C], F32, name=f"bank{(2 * e + u) % 4}")
            for j in range(2):
                t = 2 * u + j
                nc.tensor.matmul_mx(
                    out=bank[:, j, :],
                    lhsT=w2_t[e][:, t * 2 * P : (t + 1) * 2 * P].bitcast(FP4X4),
                    lhsT_scale=s2_t[:, e, t * P : (t + 1) * P],
                    rhs=g_codes[e][0].bitcast(FP8X4),
                    rhs_scale=g_codes[e][1],
                    start=True,
                    stop=True,
                )
            if e // 2 not in pairs:
                pairs[e // 2] = keep.tile([P, 2, 2, C, 2], BF16, name=f"pairs{e // 2}", align_bytes=64)
            nc.vector.scalar_tensor_tensor(
                pairs[e // 2][:, e % 2, u],
                pre[e][:, 2 * u : 2 * u + 2, :].rearrange("p j s -> p s j"),
                0.0,
                bank[:].rearrange("p j s -> p s j"),
                IS_GT,
                MULT,
            )

        def weave(q, count=2, copy=nc.scalar.copy):
            words = da[q][:].rearrange("p s t -> p (s t)").bitcast(U32).rearrange("p (e s u) -> p e s u", e=2, u=2)
            halves = pairs[q][:].rearrange("p e u s j -> p (e u s j)").bitcast(U32).rearrange("p (e u s) -> p e s u", e=2, u=2)
            copy(words[:, 0:count], halves[:, 0:count])

        def second_product(k, q, first, width, bank, copy, step=1):
            acc = psum.tile([P, PIECE], F32, name=f"bank{bank}")
            for start in range(first, first + width, C)[::step]:
                e = 2 * q + start // C
                nc.tensor.matmul_mx(
                    out=acc[:, start : start + C],
                    lhsT=w1_t[:, e, k * 2 * P : (k + 1) * 2 * P].bitcast(FP4X4),
                    lhsT_scale=s1_t[:, e, k * P : (k + 1) * P],
                    rhs=da_codes[e][0].bitcast(FP8X4),
                    rhs_scale=da_codes[e][1],
                    start=True,
                    stop=True,
                )
            copy(dx[k][:, q * PIECE + first : q * PIECE + first + width], acc[:, first : first + width])

        def second_products(q):
            for k in range(2):
                second_product(k, q, 0, PIECE, ((4, 7), (5, 6), (0, 1))[q][k], nc.scalar.copy)

        def words_tile(name, width):
            return keep.tile([P, width, PACK], BF16, name=name, align_bytes=64)

        rounded = words_tile("rounded", PIECE)
        grouped.update({0: rounded[:, 0:C, :], 1: rounded[:, C:PIECE, :]})
        for q in (0, 2, 3):
            da[q] = words_tile(f"da{q}", PIECE)

        turn_words(0)
        turn_scales()
        nc.vector.tensor_copy(gates[:].rearrange("p (c i) -> p c i", i=PACK), spread_gates(gate_quads[:, 0, :], 6))
        spread[2] = spread_gates(gate_quads[:, 1, :], 4)
        plain_gathers(2, 2, "plain")
        gated_gathers(0)
        turn_words(1)
        round_g(0)
        round_g(1)
        product = words_tile("product", PIECE)
        gate_g(nc.vector, product[:], planes[2, 2], spread[2])
        quantise(rounded[:], g_codes, 0, "g_words0")
        quantise(product[:], g_codes, 2, "g_words2")
        turn_words(2)
        spread[5] = spread_gates(gate_cols[:, 0, :], 5)
        spread[7] = spread_gates(gate_cols[:, 1, :], 6)
        plain_gathers(4, 2, "w2_raw2")
        turn_bytes(4, "product")
        for e in range(4):
            make_pairs(e, 0)
            make_pairs(e, 1)
        grouped[4] = words_tile("grouped4", C)[:]
        gate_g(nc.gpsimd, grouped[4], planes[4], gate_rows[4][:].rearrange("p (c i) -> p c i", i=WALK))
        plain_gathers(6, 1, "gated")
        weave(0)
        turn_words(6)
        plain_gathers(7, 1, "w2_raw6")
        grouped[5] = as_words(pre[3][:])[:, 0:C, :]
        gate_g(nc.vector, grouped[5], planes[5], spread[5])
        quantise(grouped[4], g_codes, 4, "pre2")
        quantise(grouped[5], g_codes, 5, "g_words5")
        quantise(da[0][:], da_codes, 0, "grouped4")
        grouped[6] = words_tile("da0", C)[:]
        gate_g(nc.gpsimd, grouped[6], planes[6], gate_rows[6][:].rearrange("p (c i) -> p c i", i=WALK))
        da[1] = words_tile("dy3", PIECE)
        weave(1)
        for e in (4, 5):
            make_pairs(e, 0)
            make_pairs(e, 1)
        weave(2)
        signs = words_tile("pairs2", C)
        nc.scalar.activation(
            signs[:].rearrange("p (c i) t -> p c t i", i=4), pre[7][:].rearrange("p t (c i) -> p c t i", i=4), SIGN
        )
        dx.append(keep.tile([P, S], F32, name="pre7", align_bytes=64))
        dx.append(keep.tile([P, S], F32, name="dx1"))
        second_products(0)
        grouped[7] = as_words(pre[5][:])[:, 0:C, :]
        gate_g(nc.vector, grouped[7], planes[7], spread[7])
        quantise(grouped[6], g_codes, 6, "g_words6")
        quantise(da[1][:], da_codes, 2, "w2_raw6")
        quantise(grouped[7], g_codes, 7, "g_words7")
        quantise(da[2][:], da_codes, 4, "pre5")
        second_products(1)
        make_pairs(6, 0)
        make_pairs(6, 1)
        second_products(2)
        weave(3, 1, nc.gpsimd.tensor_copy)
        make_da(7, 0, signs)
        make_da(7, 1, signs)
        quantise(da[3][:, 0:C, :], da_codes, 6, "pairs2")
        quantise(da[3][:, C:PIECE, :], da_codes, 7, "da_words7")
        second_product(0, 3, 0, C, 3, nc.vector.tensor_copy)
        second_product(0, 3, C, C, 2, nc.vector.tensor_copy)
        second_product(1, 3, 0, PIECE, 6, nc.vector.tensor_copy, step=-1)

        for k in range(2):
            for first, width in SHARES[k]:
                cols = slice(first // 16, (first + width) // 16)
                part = keep.tile([P, width], F32, name=f"part_{k}_{first}")
                total = keep.tile([P, width], F32, name=f"total_{k}_{first}")
                if (k, first) == (0, 0):
                    nc.vector.tensor_copy(part[:], dx[k][:].indirect(pos1_t[:, cols]))
                else:
                    nc.scalar.activation(part[:], dx[k][:].indirect(pos1_t[:, cols]), COPY)
                nc.vector.tensor_tensor(total[:], dx[k][:].indirect(pos2_t[:, cols]), part[:], ADD)
                nc.sync.dma_start(out[k * P : (k + 1) * P, first : first + width], total[:])
